import numpy as np
import ml_dtypes


def mxq(x, axis, fmt="e4m3"):
    dtype, down = {"e4m3": (ml_dtypes.float8_e4m3fn, 7), "e5m2": (ml_dtypes.float8_e5m2, 14)}[fmt]
    v = np.moveaxis(np.asarray(x, np.float32).astype(ml_dtypes.bfloat16).astype(np.float64), axis, -1)
    blocks = v.reshape(v.shape[:-1] + (-1, 32))
    amax = np.abs(blocks).max(-1, keepdims=True)
    byte = np.maximum(np.where(amax > 0, np.frexp(amax)[1] - 1 + 127, 0) - down, 1)
    scale = np.exp2(byte - 127.0)
    codes = (blocks / scale).astype(np.float32).astype(dtype).astype(np.float64)
    return np.moveaxis((codes * scale).reshape(v.shape), -1, axis)


WIDE = False


def mx_kscale(k):
    if not WIDE:
        return np.ones(k)
    levels = np.array([10, -10, 5, -5, 0])
    if k % 512:
        return np.exp2(np.random.permutation(np.resize(levels, k // 32))).repeat(32)
    a = np.empty((k // 512, 16))
    for p in range(k // 512):
        a[p, :8] = np.random.permutation(np.resize(levels, 8))
        for g in range(8):
            far = levels[np.abs(levels - a[p, g]) >= 10]
            a[p, g + 8] = far[np.random.randint(len(far))]
    return np.exp2(a.ravel()).repeat(32)


def f64(x):
    return np.asarray(x).astype(np.float64)


def striped(idx):
    return np.tile(idx.reshape(-1, 16).T, (8, 1)).astype(np.uint16)


def unstriped(offs):
    return offs[:16].T.reshape(-1).astype(np.int64)


E2M1 = np.array([0.0, 0.5, 1.0, 1.5, 2.0, 3.0, 4.0, 6.0, -0.0, -0.5, -1.0, -1.5, -2.0, -3.0, -4.0, -6.0])


def pack_weight(w, fmt):
    k, n = w.shape
    w = f64(np.asarray(w, np.float32).astype(ml_dtypes.bfloat16)).reshape(k // 32, 32, n)
    amax = np.abs(w).max(1)
    if fmt == "e4m3":
        byte = np.frexp(amax)[1] - 1 + 127 - 7
    else:
        mant, ex = np.frexp(amax / 6.0)
        byte = np.where(mant > 0.5, ex, ex - 1) + 127
    byte = np.clip(np.where(amax > 0, byte, 1), 1, 254)
    scaled = (w * np.exp2(127.0 - byte)[:, None, :]).reshape(k, n).astype(np.float32)
    by_word = np.ascontiguousarray(scaled.reshape(k // 512, 128, 4, n).transpose(0, 1, 3, 2))
    if fmt == "e4m3":
        words = by_word.astype(ml_dtypes.float8_e4m3fn).view(np.uint8)
    else:
        c = by_word.astype(ml_dtypes.float4_e2m1fn).view(np.uint8) & 0xF
        words = (c[..., 0::2] | (c[..., 1::2] << 4)).reshape(k // 512, 128, 2 * n)
    return np.ascontiguousarray(words), np.ascontiguousarray(byte.astype(np.uint8).reshape(k // 512, 16, n))


def unpack_weight(words, scales, fmt):
    g, _, n = scales.shape
    words = np.ascontiguousarray(words).reshape(g, 128, n, -1)
    if fmt == "e4m3":
        vals = words.view(ml_dtypes.float8_e4m3fn).astype(np.float64)
    else:
        nib = np.empty((g, 128, n, 4), np.uint8)
        nib[..., 0::2] = words & 0xF
        nib[..., 1::2] = words >> 4
        vals = E2M1[nib]
    vals = vals * np.repeat(np.exp2(scales.astype(np.float64) - 127.0), 8, axis=1)[..., None]
    return vals.transpose(0, 1, 3, 2).reshape(g * 512, n)


def sigmoid(v):
    return 1.0 / (1.0 + np.exp(-np.maximum(v, -700.0)))


K, T, E, C, H, N = 512, 1280, 4, 256, 1024, 128


def by_expert(wq, xq):
    return np.concatenate([wq[e].T @ xq[:, e * C:(e + 1) * C] for e in range(E)], axis=1)


def setup_inputs():
    n = np.random.standard_normal
    s = mx_kscale(K)[:, None]
    u = mx_kscale(H)
    w1 = [pack_weight(m, "e2m1") for m in n((E, K, H)) / np.sqrt(K) / s[None]]
    w3 = [pack_weight(m, "e2m1") for m in n((E, K, H)) / np.sqrt(K) / s[None] * u[None, None, :]]
    w2 = [pack_weight(m, "e2m1") for m in n((E, H, N)) / np.sqrt(H) / u[None, :, None]]
    x = pack_weight(n((K, T)) * s, "e4m3")
    return {
        "x_words": x[0],
        "x_scales": x[1],
        "w1_words": np.stack([m[0] for m in w1]),
        "w1_scales": np.stack([m[1] for m in w1]),
        "w3_words": np.stack([m[0] for m in w3]),
        "w3_scales": np.stack([m[1] for m in w3]),
        "w2_words": np.stack([m[0] for m in w2]),
        "w2_scales": np.stack([m[1] for m in w2]),
        "gate": np.tile(np.random.uniform(0.2, 1.0, E * C), (N, 1)).astype(np.float32),
        "offs": striped(np.random.permutation(T)[:E * C]),
    }


def reference(x_words, x_scales, w1_words, w1_scales, w3_words, w3_scales, w2_words, w2_scales, gate, offs):
    idx = unstriped(offs)
    w1 = np.stack([unpack_weight(w1_words[e], w1_scales[e], "e2m1") for e in range(E)])
    w3 = np.stack([unpack_weight(w3_words[e], w3_scales[e], "e2m1") for e in range(E)])
    w2 = np.stack([unpack_weight(w2_words[e], w2_scales[e], "e2m1") for e in range(E)])
    xq = unpack_weight(x_words, x_scales, "e4m3")[:, idx]
    h = sigmoid(by_expert(w1, xq))
    h = h * by_expert(w3, xq)
    y = by_expert(w2, mxq(h, 0, "e4m3"))
    out = np.zeros((N, T))
    out[:, idx] = f64(gate) * y
    return out

@@ -1,0 +1,178 @@
+from contextlib import ExitStack
+
+import concourse.mybir as mybir
+from concourse.masks import make_identity
+
+K, T, E, C, H, N = 512, 1280, 4, 256, 1024, 128
+FLOPS = 2 * E * C * (2 * K * H + H * N)
+
+F32 = mybir.dt.float32
+BF16 = mybir.dt.bfloat16
+I32 = mybir.dt.int32
+U32 = mybir.dt.uint32
+U16 = mybir.dt.uint16
+U8 = mybir.dt.uint8
+FP8X4 = mybir.dt.float8_e4m3fn_x4
+FP4X4 = mybir.dt.float4_e2m1fn_x4
+MULT = mybir.AluOpType.mult
+SIGMOID = mybir.ActivationFunctionType.Sigmoid
+
+P = 128
+PASS = 512
+PASSES = H // PASS
+TILES = E * C // P
+PER_EXPERT = C // P
+LIST_COLS = C // 16
+
+
+def tile_moe_pkd_glu_sigmoid_kernel(
+    tc, x_words, x_scales, w1_words, w1_scales, w3_words, w3_scales, w2_words, w2_scales, gate, offs, out
+):
+    nc = tc.nc
+    with ExitStack() as ctx:
+        keep = ctx.enter_context(tc.tile_pool(name="keep", bufs=1))
+        work = ctx.enter_context(tc.tile_pool(name="work", bufs=3))
+        psum = ctx.enter_context(tc.psum_pool(name="psum", bufs=1))
+
+        offsets = keep.tile([P, E * LIST_COLS], U16, name="offsets")
+        xw = keep.tile([P, T], I32, name="xw", align_bytes=64)
+        xs = keep.tile([P, T], U8, name="xs", align_bytes=64)
+        w1s = keep.tile([P, E * H], U8, name="w1s", align_bytes=64)
+        w3s = keep.tile([P, E * H], U8, name="w3s", align_bytes=64)
+        w2s = keep.tile([P, E * PASSES * N], U8, name="w2s", align_bytes=64)
+        w1w = [keep.tile([P, 2 * H], U8, name="w1w%d" % e, align_bytes=64) for e in range(E)]
+        w3w = [keep.tile([P, 2 * H], U8, name="w3w%d" % e, align_bytes=64) for e in range(E)]
+        w2w = keep.tile([P, E * PASSES, 2 * N], U8, name="w2w", align_bytes=64)
+        gates = keep.tile([P, E * C], F32, name="gates")
+        gated = keep.tile([P, E * C], F32, name="gated")
+        window = keep.tile([P, T], F32, name="window")
+        ident = keep.tile([P, P], F32, name="ident")
+        gw = [keep.tile([P, C], U32, name="gw%d" % e, align_bytes=64) for e in range(E)]
+        gs = [keep.tile([P, C], U8, name="gs%d" % e, align_bytes=64) for e in range(E)]
+
+        for plane in (xs, w1s, w3s, w2s):
+            nc.vector.memset(plane[:].bitcast(I32), 0)
+        make_identity(nc, ident[:])
+        nc.gpsimd.memset(window[:], 0.0)
+
+        def load_scales(plane, rows, groups):
+            for r in range(4):
+                dst = plane[r:P:32, :].bitcast(I32).rearrange("q (g w) -> q g w", g=groups)
+                nc.sync.dma_start(out=dst, in_=rows[r].bitcast(I32))
+
+        def load_words(e):
+            nc.sync.dma_start(out=w1w[e][:].bitcast(I32), in_=w1_words[e, 0].bitcast(I32))
+            nc.sync.dma_start(out=w3w[e][:].bitcast(I32), in_=w3_words[e, 0].bitcast(I32))
+
+        nc.sync.dma_start(out=xw[:], in_=x_words[0].rearrange("p t r -> p (t r)").bitcast(I32))
+        nc.sync.dma_start(offsets[:], offs)
+        load_scales(xs, x_scales.rearrange("o (q r) t -> r q o t", r=4), 1)
+        load_words(0)
+        load_scales(w1s, w1_scales.rearrange("e s (q r) i -> r q (e s) i", r=4), E)
+        load_scales(w3s, w3_scales.rearrange("e s (q r) i -> r q (e s) i", r=4), E)
+        load_scales(w2s, w2_scales.rearrange("e s (q r) n -> r q (e s) n", r=4), E * PASSES)
+        nc.sync.dma_start(out=w2w[:].bitcast(I32), in_=w2_words.rearrange("e s p b -> p (e s) b").bitcast(I32))
+        load_words(1)
+        nc.sync.dma_start(out=gates[:], in_=gate)
+        load_words(2)
+        load_words(3)
+
+        def listed(e):
+            return offsets[:, e * LIST_COLS : (e + 1) * LIST_COLS]
+
+        def gather(e):
+            nc.vector.tensor_copy(out=gw[e][:], in_=xw[:].bitcast(U32).indirect(listed(e)))
+            nc.vector.tensor_copy(out=gs[e][:], in_=xs[:].indirect(listed(e)))
+
+        hidden = {}
+        quantised = {}
+        sums = {}
+
+        def first_layer(j):
+            e, c = divmod(j, PER_EXPERT)
+            slots = slice(c * P, (c + 1) * P)
+            for s in range(PASSES):
+                a = psum.tile([P, PASS], F32, name="a", bufs=2)
+                b = psum.tile([P, PASS], F32, name="b", bufs=3)
+                for acc, words, plane in ((a, w1w[e], w1s), (b, w3w[e], w3s)):
+                    nc.tensor.matmul_mx(
+                        out=acc[:],
+                        lhsT=gw[e][:, slots].bitcast(FP8X4),
+                        lhsT_scale=gs[e][:, slots],
+                        rhs=words[:, 2 * PASS * s : 2 * PASS * (s + 1)].bitcast(FP4X4),
+                        rhs_scale=plane[:, e * H + PASS * s : e * H + PASS * (s + 1)],
+                        start=True,
+                        stop=True,
+                    )
+                sig = work.tile([P, 2, P, 2], F32, name="sig")
+                nc.scalar.activation(out=sig[:], in_=a[:].rearrange("c (p u v) -> c u p v", u=2, v=2), func=SIGMOID)
+                h = work.tile([P, 2, P, 2], BF16, name="h", bufs=4)
+                nc.vector.tensor_tensor(out=h[:], in0=b[:].rearrange("c (p u v) -> c u p v", u=2, v=2), in1=sig[:], op=MULT)
+                hidden[j, s] = h
+
+        def turn(j, passes):
+            n = len(passes)
+            xt = psum.tile([P, n, 2, P], F32, name="xt", bufs=2)
+            for k, s in enumerate(passes):
+                pairs = hidden[j, s][:].rearrange("c u p v -> c (u p v)").bitcast(F32)
+                for u in range(2):
+                    nc.tensor.transpose(xt[:, k, u, :], pairs[:, u * P : (u + 1) * P], ident[:])
+            grouped = work.tile([P, n * P * 4], BF16, name="grouped", align_bytes=64)
+            nc.scalar.copy(
+                out=grouped[:].bitcast(F32).rearrange("p (s c u) -> p s c u", s=n, u=2),
+                in_=xt[:].rearrange("p s u c -> p s c u"),
+            )
+            codes = work.tile([P, n * P], U32, name="codes", align_bytes=64)
+            scales = work.tile([P, n * P], U8, name="scales", align_bytes=64)
+            nc.vector.quantize_mx(out=codes[:].bitcast(FP8X4), scales=scales[:], in_=grouped[:])
+            for k, s in enumerate(passes):
+                quantised[j, s] = (codes[:, k * P : (k + 1) * P], scales[:, k * P : (k + 1) * P])
+
+        def second_layer(j):
+            e, c = divmod(j, PER_EXPERT)
+            if c == 0:
+                sums[e] = psum.tile([P, C], F32, name="y", bufs=1)
+            for s in range(PASSES):
+                codes, scales = quantised[j, s]
+                g = e * PASSES + s
+                nc.tensor.matmul_mx(
+                    out=sums[e][:, c * P : (c + 1) * P],
+                    lhsT=w2w[:, g, :].bitcast(FP4X4),
+                    lhsT_scale=w2s[:, g * N : (g + 1) * N],
+                    rhs=codes.bitcast(FP8X4),
+                    rhs_scale=scales,
+                    start=(s == 0),
+                    stop=(s == PASSES - 1),
+                )
+            if e == E - 1:
+                done = slice(c * P, (c + 1) * P)
+            elif c == PER_EXPERT - 1:
+                done = slice(0, C)
+            else:
+                return
+            cols = slice(e * C + done.start, e * C + done.stop)
+            nc.vector.tensor_tensor(out=gated[:, cols], in0=sums[e][:, done], in1=gates[:, cols], op=MULT)
+
+        def scatter(lo, hi):
+            nc.vector.tensor_copy(out=window[:].indirect(offsets[:, lo // 16 : hi // 16]), in_=gated[:, lo:hi])
+
+        gather(0)
+        for step in range(TILES):
+            first_layer(step)
+            if step % PER_EXPERT == 0 and step // PER_EXPERT + 1 < E:
+                gather(step // PER_EXPERT + 1)
+            if step >= 1:
+                turn(step - 1, (0, 1))
+            if step >= 2:
+                second_layer(step - 2)
+            if step in (4, 6):
+                scatter((step - 4) * P, (step - 2) * P)
+        last = TILES - 1
+        turn(last, (0,))
+        second_layer(last - 1)
+        turn(last, (1,))
+        scatter(512, 704)
+        second_layer(last)
+        scatter(704, 864)
+        scatter(864, 1024)
+        nc.sync.dma_start(out=out, in_=window[:])

@@ -22,7 +22,10 @@ PASS = 512
 PASSES = H // PASS
 TILES = E * C // P
 PER_EXPERT = C // P
-LIST_COLS = C // 16
+PER_COLUMN = 16
+ALIGN = 64
+W13_BYTES = 2 * 2 * H
+SCATTER_ENDS = (256, 512, 704, 864, 1024)
 
 
 def tile_moe_pkd_glu_sigmoid_kernel(
@@ -31,84 +34,90 @@ def tile_moe_pkd_glu_sigmoid_kernel(
     nc = tc.nc
     with ExitStack() as ctx:
         keep = ctx.enter_context(tc.tile_pool(name="keep", bufs=1))
+        shared = ctx.enter_context(tc.tile_pool(name="shared", bufs=1))
         work = ctx.enter_context(tc.tile_pool(name="work", bufs=3))
         psum = ctx.enter_context(tc.psum_pool(name="psum", bufs=1))
 
-        offsets = keep.tile([P, E * LIST_COLS], U16, name="offsets")
-        xw = keep.tile([P, T], I32, name="xw", align_bytes=64)
-        xs = keep.tile([P, T], U8, name="xs", align_bytes=64)
-        w1s = keep.tile([P, E * H], U8, name="w1s", align_bytes=64)
-        w3s = keep.tile([P, E * H], U8, name="w3s", align_bytes=64)
-        w2s = keep.tile([P, E * PASSES * N], U8, name="w2s", align_bytes=64)
-        w1w = [keep.tile([P, 2 * H], U8, name="w1w%d" % e, align_bytes=64) for e in range(E)]
-        w3w = [keep.tile([P, 2 * H], U8, name="w3w%d" % e, align_bytes=64) for e in range(E)]
-        w2w = keep.tile([P, E * PASSES, 2 * N], U8, name="w2w", align_bytes=64)
-        gates = keep.tile([P, E * C], F32, name="gates")
+        offsets = keep.tile([P, E * C // PER_COLUMN], U16, name="offsets")
+        xw = keep.tile([P, T], I32, name="xw", align_bytes=ALIGN)
+        w1s = keep.tile([P, E * H], U8, name="w1s", align_bytes=ALIGN)
+        w3s = keep.tile([P, E * H], U8, name="w3s", align_bytes=ALIGN)
+        w2s = keep.tile([P, E * PASSES * N], U8, name="w2s", align_bytes=ALIGN)
         gated = keep.tile([P, E * C], F32, name="gated")
-        window = keep.tile([P, T], F32, name="window")
         ident = keep.tile([P, P], F32, name="ident")
-        gw = [keep.tile([P, C], U32, name="gw%d" % e, align_bytes=64) for e in range(E)]
-        gs = [keep.tile([P, C], U8, name="gs%d" % e, align_bytes=64) for e in range(E)]
+        xs = shared.tile([P, T], U8, name="xs", align_bytes=ALIGN, offset=4 * W13_BYTES - ALIGN)
+        window = shared.tile([P, T], F32, name="window", align_bytes=ALIGN, offset=4 * W13_BYTES + T - 2 * ALIGN)
+        places = (W13_BYTES - ALIGN, 3 * W13_BYTES, 0, 3 * W13_BYTES)
+        w13 = [
+            shared.tile([P, 2, 2 * H], U8, name="w13_%d" % e, align_bytes=ALIGN, offset=places[e]) for e in range(E)
+        ]
+        w2w = shared.tile([P, E * PASSES, 2 * N], U8, name="w2w", align_bytes=ALIGN, offset=W13_BYTES)
+        gates = shared.tile([P, E * C], F32, name="gates", align_bytes=ALIGN, offset=2 * (W13_BYTES - ALIGN))
 
-        for plane in (xs, w1s, w3s, w2s):
+        def load_scales(plane, scale_rows, rows, queue):
+            by_row = scale_rows.rearrange("g (q r) w -> r q g w", r=4)
+            for r in rows:
+                dst = plane[r:P:32, :].bitcast(I32).rearrange("q (g w) -> q g w", g=scale_rows.shape[0])
+                queue.dma_start(out=dst, in_=by_row[r].bitcast(I32))
+
+        def load_w13(e, queue, matrices=(0, 1)):
+            for m in matrices:
+                queue.dma_start(out=w13[e][:, m, :].bitcast(I32), in_=(w1_words, w3_words)[m][e, 0].bitcast(I32))
+
+        nc.gpsimd.memset(xs[:].bitcast(I32), 0)
+        for plane in (w1s, w3s, w2s):
             nc.vector.memset(plane[:].bitcast(I32), 0)
-        make_identity(nc, ident[:])
-        nc.gpsimd.memset(window[:], 0.0)
-
-        def load_scales(plane, rows, groups):
-            for r in range(4):
-                dst = plane[r:P:32, :].bitcast(I32).rearrange("q (g w) -> q g w", g=groups)
-                nc.sync.dma_start(out=dst, in_=rows[r].bitcast(I32))
-
-        def load_words(e):
-            nc.sync.dma_start(out=w1w[e][:].bitcast(I32), in_=w1_words[e, 0].bitcast(I32))
-            nc.sync.dma_start(out=w3w[e][:].bitcast(I32), in_=w3_words[e, 0].bitcast(I32))
-
-        nc.sync.dma_start(out=xw[:], in_=x_words[0].rearrange("p t r -> p (t r)").bitcast(I32))
+        load_w13(0, nc.gpsimd)
         nc.sync.dma_start(offsets[:], offs)
-        load_scales(xs, x_scales.rearrange("o (q r) t -> r q o t", r=4), 1)
-        load_words(0)
-        load_scales(w1s, w1_scales.rearrange("e s (q r) i -> r q (e s) i", r=4), E)
-        load_scales(w3s, w3_scales.rearrange("e s (q r) i -> r q (e s) i", r=4), E)
-        load_scales(w2s, w2_scales.rearrange("e s (q r) n -> r q (e s) n", r=4), E * PASSES)
-        nc.sync.dma_start(out=w2w[:].bitcast(I32), in_=w2_words.rearrange("e s p b -> p (e s) b").bitcast(I32))
-        load_words(1)
-        nc.sync.dma_start(out=gates[:], in_=gate)
-        load_words(2)
-        load_words(3)
+        nc.sync.dma_start(out=xw[:], in_=x_words[0].rearrange("p t r -> p (t r)").bitcast(I32))
+        load_scales(xs, x_scales, range(4), nc.sync)
+        load_scales(w1s, w1_scales[:, 0], range(4), nc.sync)
+        load_scales(w3s, w3_scales[:, 0], range(2), nc.sync)
+        load_scales(w3s, w3_scales[:, 0], range(2, 4), nc.gpsimd)
+        make_identity(nc, ident[:])
+        load_scales(w2s, w2_scales.rearrange("e s f n -> (e s) f n"), range(4), nc.sync)
 
-        def listed(e):
-            return offsets[:, e * LIST_COLS : (e + 1) * LIST_COLS]
+        def listed(lo, hi):
+            return offsets[:, lo // PER_COLUMN : hi // PER_COLUMN]
 
-        def gather(e):
-            nc.vector.tensor_copy(out=gw[e][:], in_=xw[:].bitcast(U32).indirect(listed(e)))
-            nc.vector.tensor_copy(out=gs[e][:], in_=xs[:].indirect(listed(e)))
-
+        token_words = {}
+        token_scales = {}
         hidden = {}
+        grouped = {}
         quantised = {}
         sums = {}
 
-        def first_layer(j):
+        def gather_words(e):
+            token_words[e] = work.tile([P, C], U32, name="gw", bufs=2, align_bytes=ALIGN)
+            nc.vector.tensor_copy(out=token_words[e][:], in_=xw[:].bitcast(U32).indirect(listed(e * C, (e + 1) * C)))
+
+        def gather_scales(e):
+            token_scales[e] = work.tile([P, C], U8, name="gs", bufs=E, align_bytes=ALIGN)
+            nc.vector.tensor_copy(out=token_scales[e][:], in_=xs[:].indirect(listed(e * C, (e + 1) * C)))
+
+        def first_layer(j, s):
             e, c = divmod(j, PER_EXPERT)
+            gw, gs = token_words[e], token_scales[e]
             slots = slice(c * P, (c + 1) * P)
-            for s in range(PASSES):
-                a = psum.tile([P, PASS], F32, name="a", bufs=2)
-                b = psum.tile([P, PASS], F32, name="b", bufs=3)
-                for acc, words, plane in ((a, w1w[e], w1s), (b, w3w[e], w3s)):
-                    nc.tensor.matmul_mx(
-                        out=acc[:],
-                        lhsT=gw[e][:, slots].bitcast(FP8X4),
-                        lhsT_scale=gs[e][:, slots],
-                        rhs=words[:, 2 * PASS * s : 2 * PASS * (s + 1)].bitcast(FP4X4),
-                        rhs_scale=plane[:, e * H + PASS * s : e * H + PASS * (s + 1)],
-                        start=True,
-                        stop=True,
-                    )
-                sig = work.tile([P, 2, P, 2], F32, name="sig")
-                nc.scalar.activation(out=sig[:], in_=a[:].rearrange("c (p u v) -> c u p v", u=2, v=2), func=SIGMOID)
-                h = work.tile([P, 2, P, 2], BF16, name="h", bufs=4)
-                nc.vector.tensor_tensor(out=h[:], in0=b[:].rearrange("c (p u v) -> c u p v", u=2, v=2), in1=sig[:], op=MULT)
-                hidden[j, s] = h
+            a = psum.tile([P, PASS], F32, name="a", bufs=2)
+            b = psum.tile([P, PASS], F32, name="b", bufs=3)
+            for m, (acc, plane) in enumerate(((a, w1s), (b, w3s))):
+                nc.tensor.matmul_mx(
+                    out=acc[:],
+                    lhsT=gw[:, slots].bitcast(FP8X4),
+                    lhsT_scale=gs[:, slots],
+                    rhs=w13[e][:, m, 2 * PASS * s : 2 * PASS * (s + 1)].bitcast(FP4X4),
+                    rhs_scale=plane[:, e * H + PASS * s : e * H + PASS * (s + 1)],
+                    start=True,
+                    stop=True,
+                )
+            sig = work.tile([P, 2, P, 2], F32, name="sig", bufs=4)
+            nc.scalar.activation(out=sig[:], in_=a[:].rearrange("c (p u v) -> c u p v", u=2, v=2), func=SIGMOID)
+            h = work.tile([P, 2, P, 2], BF16, name="h", bufs=6)
+            nc.vector.tensor_tensor(
+                out=h[:], in0=b[:].rearrange("c (p u v) -> c u p v", u=2, v=2), in1=sig[:], op=MULT
+            )
+            hidden[j, s] = h
 
         def turn(j, passes):
             n = len(passes)
@@ -117,14 +126,18 @@ def tile_moe_pkd_glu_sigmoid_kernel(
                 pairs = hidden[j, s][:].rearrange("c u p v -> c (u p v)").bitcast(F32)
                 for u in range(2):
                     nc.tensor.transpose(xt[:, k, u, :], pairs[:, u * P : (u + 1) * P], ident[:])
-            grouped = work.tile([P, n * P * 4], BF16, name="grouped", align_bytes=64)
+            ht = work.tile([P, n * PASS], BF16, name="ht", align_bytes=ALIGN)
             nc.scalar.copy(
-                out=grouped[:].bitcast(F32).rearrange("p (s c u) -> p s c u", s=n, u=2),
+                out=ht[:].bitcast(F32).rearrange("p (s c u) -> p s c u", s=n, u=2),
                 in_=xt[:].rearrange("p s u c -> p s c u"),
             )
-            codes = work.tile([P, n * P], U32, name="codes", align_bytes=64)
-            scales = work.tile([P, n * P], U8, name="scales", align_bytes=64)
-            nc.vector.quantize_mx(out=codes[:].bitcast(FP8X4), scales=scales[:], in_=grouped[:])
+            grouped[j, passes] = ht
+
+        def quantise(j, passes):
+            n = len(passes)
+            codes = work.tile([P, n * P], U32, name="codes", align_bytes=ALIGN)
+            scales = work.tile([P, n * P], U8, name="scales", align_bytes=ALIGN)
+            nc.vector.quantize_mx(out=codes[:].bitcast(FP8X4), scales=scales[:], in_=grouped[j, passes][:])
             for k, s in enumerate(passes):
                 quantised[j, s] = (codes[:, k * P : (k + 1) * P], scales[:, k * P : (k + 1) * P])
 
@@ -144,35 +157,56 @@ def tile_moe_pkd_glu_sigmoid_kernel(
                     start=(s == 0),
                     stop=(s == PASSES - 1),
                 )
-            if e == E - 1:
-                done = slice(c * P, (c + 1) * P)
-            elif c == PER_EXPERT - 1:
-                done = slice(0, C)
-            else:
-                return
-            cols = slice(e * C + done.start, e * C + done.stop)
-            nc.vector.tensor_tensor(out=gated[:, cols], in0=sums[e][:, done], in1=gates[:, cols], op=MULT)
 
-        def scatter(lo, hi):
-            nc.vector.tensor_copy(out=window[:].indirect(offsets[:, lo // 16 : hi // 16]), in_=gated[:, lo:hi])
+        def apply_gate(lo, hi):
+            e = lo // C
+            y = sums[e][:, lo - e * C : hi - e * C]
+            nc.vector.tensor_tensor(out=gated[:, lo:hi], in0=y, in1=gates[:, lo:hi], op=MULT)
 
-        gather(0)
+        def scatter(piece):
+            lo = SCATTER_ENDS[piece - 1] if piece else 0
+            hi = SCATTER_ENDS[piece]
+            nc.vector.tensor_copy(out=window[:].indirect(listed(lo, hi)), in_=gated[:, lo:hi])
+
+        both = tuple(range(PASSES))
+        last = TILES - 1
+        gather_words(0)
+        gather_scales(0)
+        gather_words(1)
+        for e in range(1, E):
+            gather_scales(e)
+        load_w13(1, nc.sync)
+        nc.vector.memset(window[:], 0.0)
         for step in range(TILES):
-            first_layer(step)
-            if step % PER_EXPERT == 0 and step // PER_EXPERT + 1 < E:
-                gather(step // PER_EXPERT + 1)
+            first_layer(step, 0)
+            if step >= 2:
+                quantise(step - 2, both)
+            first_layer(step, 1)
+            if step == 1:
+                w2_rows = w2_words.rearrange("e s p b -> p (e s) b")
+                nc.sync.dma_start(out=w2w[:].bitcast(I32), in_=w2_rows.bitcast(I32))
+                nc.sync.dma_start(out=gates[:], in_=gate)
+            if step % PER_EXPERT == 1 and step // PER_EXPERT + 2 < E:
+                load_w13(step // PER_EXPERT + 2, nc.sync)
+                gather_words(step // PER_EXPERT + 2)
             if step >= 1:
-                turn(step - 1, (0, 1))
+                turn(step - 1, both)
             if step >= 2:
                 second_layer(step - 2)
+            if step >= 3 and step % PER_EXPERT == 1:
+                apply_gate((step - 3) * P, (step - 1) * P)
             if step in (4, 6):
-                scatter((step - 4) * P, (step - 2) * P)
-        last = TILES - 1
+                scatter((step - 4) // PER_EXPERT)
         turn(last, (0,))
-        second_layer(last - 1)
+        quantise(last - 1, both)
         turn(last, (1,))
-        scatter(512, 704)
+        second_layer(last - 1)
+        apply_gate((last - 1) * P, last * P)
+        quantise(last, (0,))
+        quantise(last, (1,))
+        scatter(2)
         second_layer(last)
-        scatter(704, 864)
-        scatter(864, 1024)
+        apply_gate(last * P, TILES * P)
+        scatter(3)
+        scatter(4)
         nc.sync.dma_start(out=out, in_=window[:])

@@ -161,12 +161,14 @@ def tile_moe_pkd_glu_sigmoid_kernel(
         def apply_gate(lo, hi):
             e = lo // C
             y = sums[e][:, lo - e * C : hi - e * C]
-            nc.vector.tensor_tensor(out=gated[:, lo:hi], in0=y, in1=gates[:, lo:hi], op=MULT)
+            nc.scalar.copy(out=gated[:, lo:hi], in_=y)
 
         def scatter(piece):
             lo = SCATTER_ENDS[piece - 1] if piece else 0
             hi = SCATTER_ENDS[piece]
-            nc.vector.tensor_copy(out=window[:].indirect(listed(lo, hi)), in_=gated[:, lo:hi])
+            nc.vector.tensor_tensor(
+                out=window[:].indirect(listed(lo, hi)), in0=gated[:, lo:hi], in1=gates[:, lo:hi], op=MULT
+            )
 
         both = tuple(range(PASSES))
         last = TILES - 1

@@ -40,19 +40,19 @@ def tile_moe_pkd_glu_sigmoid_kernel(
 
         offsets = keep.tile([P, E * C // PER_COLUMN], U16, name="offsets")
         xw = keep.tile([P, T], I32, name="xw", align_bytes=ALIGN)
-        w1s = keep.tile([P, E * H], U8, name="w1s", align_bytes=ALIGN)
-        w3s = keep.tile([P, E * H], U8, name="w3s", align_bytes=ALIGN)
+        first_planes = [keep.tile([P, H], U8, name="first_plane_%d" % m, align_bytes=ALIGN) for m in range(2)]
+        later_planes = [keep.tile([P, (E - 1) * H], U8, name="later_plane_%d" % m, align_bytes=ALIGN) for m in range(2)]
         w2s = keep.tile([P, E * PASSES * N], U8, name="w2s", align_bytes=ALIGN)
         gated = keep.tile([P, E * C], F32, name="gated")
         ident = keep.tile([P, P], F32, name="ident")
-        xs = shared.tile([P, T], U8, name="xs", align_bytes=ALIGN, offset=4 * W13_BYTES - ALIGN)
-        window = shared.tile([P, T], F32, name="window", align_bytes=ALIGN, offset=4 * W13_BYTES + T - 2 * ALIGN)
-        places = (W13_BYTES - ALIGN, 3 * W13_BYTES, 0, 3 * W13_BYTES)
+        window = keep.tile([P, T], F32, name="window", align_bytes=ALIGN)
         w13 = [
-            shared.tile([P, 2, 2 * H], U8, name="w13_%d" % e, align_bytes=ALIGN, offset=places[e]) for e in range(E)
+            shared.tile([P, 2, 2 * H], U8, name="w13_%d" % e, align_bytes=ALIGN, offset=(e % 2) * W13_BYTES)
+            for e in range(E)
         ]
-        w2w = shared.tile([P, E * PASSES, 2 * N], U8, name="w2w", align_bytes=ALIGN, offset=W13_BYTES)
-        gates = shared.tile([P, E * C], F32, name="gates", align_bytes=ALIGN, offset=2 * (W13_BYTES - ALIGN))
+        w2w = shared.tile([P, E * PASSES, 2 * N], U8, name="w2w", align_bytes=ALIGN, offset=2 * W13_BYTES)
+        xs = shared.tile([P, T], U8, name="xs", align_bytes=ALIGN, offset=2 * W13_BYTES - T // 2)
+        gates = shared.tile([P, E * C], F32, name="gates", align_bytes=ALIGN, offset=3 * W13_BYTES)
 
         def load_scales(plane, scale_rows, rows, queue):
             by_row = scale_rows.rearrange("g (q r) w -> r q g w", r=4)
@@ -60,21 +60,24 @@ def tile_moe_pkd_glu_sigmoid_kernel(
                 dst = plane[r:P:32, :].bitcast(I32).rearrange("q (g w) -> q g w", g=scale_rows.shape[0])
                 queue.dma_start(out=dst, in_=by_row[r].bitcast(I32))
 
-        def load_w13(e, queue, matrices=(0, 1)):
-            for m in matrices:
+        def load_w13(e, queue):
+            for m in range(2):
                 queue.dma_start(out=w13[e][:, m, :].bitcast(I32), in_=(w1_words, w3_words)[m][e, 0].bitcast(I32))
 
-        nc.gpsimd.memset(xs[:].bitcast(I32), 0)
-        for plane in (w1s, w3s, w2s):
+        for plane in [xs] + first_planes:
+            nc.vector.memset(plane[:].bitcast(I32), 0)
+        for plane in later_planes + [w2s]:
             nc.vector.memset(plane[:].bitcast(I32), 0)
         load_w13(0, nc.gpsimd)
         nc.sync.dma_start(offsets[:], offs)
         nc.sync.dma_start(out=xw[:], in_=x_words[0].rearrange("p t r -> p (t r)").bitcast(I32))
-        load_scales(xs, x_scales, range(4), nc.sync)
-        load_scales(w1s, w1_scales[:, 0], range(4), nc.sync)
-        load_scales(w3s, w3_scales[:, 0], range(2), nc.sync)
-        load_scales(w3s, w3_scales[:, 0], range(2, 4), nc.gpsimd)
+        load_scales(xs, x_scales, range(4), nc.scalar)
+        load_scales(first_planes[0], w1_scales[0:1, 0], range(4), nc.sync)
+        load_scales(first_planes[1], w3_scales[0:1, 0], range(4), nc.sync)
         make_identity(nc, ident[:])
+        nc.gpsimd.memset(window[:], 0.0)
+        load_scales(later_planes[0], w1_scales[1:E, 0], range(4), nc.sync)
+        load_scales(later_planes[1], w3_scales[1:E, 0], range(4), nc.sync)
         load_scales(w2s, w2_scales.rearrange("e s f n -> (e s) f n"), range(4), nc.sync)
 
         def listed(lo, hi):
@@ -82,40 +85,51 @@ def tile_moe_pkd_glu_sigmoid_kernel(
 
         token_words = {}
         token_scales = {}
+        sigmoids = {}
         hidden = {}
         grouped = {}
         quantised = {}
         sums = {}
 
         def gather_words(e):
-            token_words[e] = work.tile([P, C], U32, name="gw", bufs=2, align_bytes=ALIGN)
+            token_words[e] = work.tile([P, C], U32, name="gw", bufs=3, align_bytes=ALIGN)
             nc.vector.tensor_copy(out=token_words[e][:], in_=xw[:].bitcast(U32).indirect(listed(e * C, (e + 1) * C)))
 
         def gather_scales(e):
-            token_scales[e] = work.tile([P, C], U8, name="gs", bufs=E, align_bytes=ALIGN)
+            token_scales[e] = work.tile([P, C], U8, name="gs", bufs=4, align_bytes=ALIGN)
             nc.vector.tensor_copy(out=token_scales[e][:], in_=xs[:].indirect(listed(e * C, (e + 1) * C)))
 
-        def first_layer(j, s):
+        def first_product(j, s, m, acc):
             e, c = divmod(j, PER_EXPERT)
-            gw, gs = token_words[e], token_scales[e]
             slots = slice(c * P, (c + 1) * P)
+            plane = later_planes[m][:, (e - 1) * H : e * H] if e else first_planes[m][:]
+            nc.tensor.matmul_mx(
+                out=acc[:],
+                lhsT=token_words[e][:, slots].bitcast(FP8X4),
+                lhsT_scale=token_scales[e][:, slots],
+                rhs=w13[e][:, m, 2 * PASS * s : 2 * PASS * (s + 1)].bitcast(FP4X4),
+                rhs_scale=plane[:, PASS * s : PASS * (s + 1)],
+                start=True,
+                stop=True,
+            )
+
+        def gate_half(j, s):
             a = psum.tile([P, PASS], F32, name="a", bufs=2)
-            b = psum.tile([P, PASS], F32, name="b", bufs=3)
-            for m, (acc, plane) in enumerate(((a, w1s), (b, w3s))):
-                nc.tensor.matmul_mx(
-                    out=acc[:],
-                    lhsT=gw[:, slots].bitcast(FP8X4),
-                    lhsT_scale=gs[:, slots],
-                    rhs=w13[e][:, m, 2 * PASS * s : 2 * PASS * (s + 1)].bitcast(FP4X4),
-                    rhs_scale=plane[:, e * H + PASS * s : e * H + PASS * (s + 1)],
-                    start=True,
-                    stop=True,
-                )
-            sig = work.tile([P, 2, P, 2], F32, name="sig", bufs=4)
+            first_product(j, s, 0, a)
+            if j == 0:
+                place = 3 * W13_BYTES + s * 4 * PASS
+                sig = shared.tile([P, 2, P, 2], F32, name="first_sig_%d" % s, align_bytes=ALIGN, offset=place)
+            else:
+                sig = work.tile([P, 2, P, 2], F32, name="sig", bufs=4)
             nc.scalar.activation(out=sig[:], in_=a[:].rearrange("c (p u v) -> c u p v", u=2, v=2), func=SIGMOID)
+            sigmoids[j, s] = sig
+
+        def value_half(j, s):
+            b = psum.tile([P, PASS], F32, name="b", bufs=3)
+            first_product(j, s, 1, b)
             h = work.tile([P, 2, P, 2], BF16, name="h", bufs=6)
             nc.vector.tensor_tensor(
-                out=h[:], in0=b[:].rearrange("c (p u v) -> c u p v", u=2, v=2), in1=sig[:], op=MULT
+                out=h[:], in0=b[:].rearrange("c (p u v) -> c u p v", u=2, v=2), in1=sigmoids[j, s][:], op=MULT
             )
             hidden[j, s] = h
 
@@ -158,10 +172,9 @@ def tile_moe_pkd_glu_sigmoid_kernel(
                     stop=(s == PASSES - 1),
                 )
 
-        def apply_gate(lo, hi):
+        def empty_sums(lo, hi):
             e = lo // C
-            y = sums[e][:, lo - e * C : hi - e * C]
-            nc.scalar.copy(out=gated[:, lo:hi], in_=y)
+            nc.scalar.copy(out=gated[:, lo:hi], in_=sums[e][:, lo - e * C : hi - e * C])
 
         def scatter(piece):
             lo = SCATTER_ENDS[piece - 1] if piece else 0
@@ -172,43 +185,45 @@ def tile_moe_pkd_glu_sigmoid_kernel(
 
         both = tuple(range(PASSES))
         last = TILES - 1
-        gather_words(0)
-        gather_scales(0)
-        gather_words(1)
-        for e in range(1, E):
+        for e in range(E):
             gather_scales(e)
+        for e in range(E - 1):
+            gather_words(e)
         load_w13(1, nc.sync)
-        nc.vector.memset(window[:], 0.0)
+        w2_rows = w2_words.rearrange("e s p b -> p (e s) b")
+        nc.sync.dma_start(out=w2w[:].bitcast(I32), in_=w2_rows.bitcast(I32))
+        gate_half(0, 0)
         for step in range(TILES):
-            first_layer(step, 0)
+            value_half(step, 0)
             if step >= 2:
                 quantise(step - 2, both)
-            first_layer(step, 1)
+            gate_half(step, 1)
+            value_half(step, 1)
             if step == 1:
-                w2_rows = w2_words.rearrange("e s p b -> p (e s) b")
-                nc.sync.dma_start(out=w2w[:].bitcast(I32), in_=w2_rows.bitcast(I32))
+                gather_words(E - 1)
                 nc.sync.dma_start(out=gates[:], in_=gate)
             if step % PER_EXPERT == 1 and step // PER_EXPERT + 2 < E:
                 load_w13(step // PER_EXPERT + 2, nc.sync)
-                gather_words(step // PER_EXPERT + 2)
+            if step < last:
+                gate_half(step + 1, 0)
             if step >= 1:
                 turn(step - 1, both)
             if step >= 2:
                 second_layer(step - 2)
             if step >= 3 and step % PER_EXPERT == 1:
-                apply_gate((step - 3) * P, (step - 1) * P)
+                empty_sums((step - 3) * P, (step - 1) * P)
             if step in (4, 6):
                 scatter((step - 4) // PER_EXPERT)
         turn(last, (0,))
         quantise(last - 1, both)
         turn(last, (1,))
         second_layer(last - 1)
-        apply_gate((last - 1) * P, last * P)
+        empty_sums((last - 1) * P, last * P)
         quantise(last, (0,))
         quantise(last, (1,))
         scatter(2)
         second_layer(last)
-        apply_gate(last * P, TILES * P)
+        empty_sums(last * P, TILES * P)
         scatter(3)
         scatter(4)
         nc.sync.dma_start(out=out, in_=window[:])

@@ -25,6 +25,9 @@ PER_EXPERT = C // P
 PER_COLUMN = 16
 ALIGN = 64
 W13_BYTES = 2 * 2 * H
+W13_AT = 4 * T
+W2_AT = W13_AT + 2 * W13_BYTES
+GATES_AT = W2_AT + E * PASSES * 2 * N
 SCATTER_ENDS = (256, 512, 704, 864, 1024)
 
 
@@ -39,20 +42,20 @@ def tile_moe_pkd_glu_sigmoid_kernel(
         psum = ctx.enter_context(tc.psum_pool(name="psum", bufs=1))
 
         offsets = keep.tile([P, E * C // PER_COLUMN], U16, name="offsets")
-        xw = keep.tile([P, T], I32, name="xw", align_bytes=ALIGN)
         first_planes = [keep.tile([P, H], U8, name="first_plane_%d" % m, align_bytes=ALIGN) for m in range(2)]
         later_planes = [keep.tile([P, (E - 1) * H], U8, name="later_plane_%d" % m, align_bytes=ALIGN) for m in range(2)]
         w2s = keep.tile([P, E * PASSES * N], U8, name="w2s", align_bytes=ALIGN)
         gated = keep.tile([P, E * C], F32, name="gated")
         ident = keep.tile([P, P], F32, name="ident")
         window = keep.tile([P, T], F32, name="window", align_bytes=ALIGN)
+        xw = shared.tile([P, T], I32, name="xw", align_bytes=ALIGN, offset=0)
         w13 = [
-            shared.tile([P, 2, 2 * H], U8, name="w13_%d" % e, align_bytes=ALIGN, offset=(e % 2) * W13_BYTES)
+            shared.tile([P, W13_BYTES], U8, name="w13_%d" % e, align_bytes=ALIGN, offset=W13_AT + (e % 2) * W13_BYTES)
             for e in range(E)
         ]
-        w2w = shared.tile([P, E * PASSES, 2 * N], U8, name="w2w", align_bytes=ALIGN, offset=2 * W13_BYTES)
-        xs = shared.tile([P, T], U8, name="xs", align_bytes=ALIGN, offset=2 * W13_BYTES - T // 2)
-        gates = shared.tile([P, E * C], F32, name="gates", align_bytes=ALIGN, offset=3 * W13_BYTES)
+        w2w = shared.tile([P, E * PASSES, 2 * N], U8, name="w2w", align_bytes=ALIGN, offset=W2_AT)
+        xs = shared.tile([P, T], U8, name="xs", align_bytes=ALIGN, offset=W2_AT - T // 2)
+        gates = shared.tile([P, E * C], F32, name="gates", align_bytes=ALIGN, offset=GATES_AT)
 
         def load_scales(plane, scale_rows, rows, queue):
             by_row = scale_rows.rearrange("g (q r) w -> r q g w", r=4)
@@ -62,20 +65,19 @@ def tile_moe_pkd_glu_sigmoid_kernel(
 
         def load_w13(e, queue):
             for m in range(2):
-                queue.dma_start(out=w13[e][:, m, :].bitcast(I32), in_=(w1_words, w3_words)[m][e, 0].bitcast(I32))
+                queue.dma_start(out=w13[e][:, 2 * H * m : 2 * H * (m + 1)].bitcast(I32), in_=(w1_words, w3_words)[m][e, 0].bitcast(I32))
 
-        for plane in [xs] + first_planes:
+        nc.vector.memset(xs[:].bitcast(I32), 0)
+        for plane in first_planes + later_planes + [w2s]:
             nc.vector.memset(plane[:].bitcast(I32), 0)
-        for plane in later_planes + [w2s]:
-            nc.vector.memset(plane[:].bitcast(I32), 0)
-        load_w13(0, nc.gpsimd)
         nc.sync.dma_start(offsets[:], offs)
+        load_scales(xs, x_scales, range(4), nc.sync)
         nc.sync.dma_start(out=xw[:], in_=x_words[0].rearrange("p t r -> p (t r)").bitcast(I32))
-        load_scales(xs, x_scales, range(4), nc.scalar)
-        load_scales(first_planes[0], w1_scales[0:1, 0], range(4), nc.sync)
-        load_scales(first_planes[1], w3_scales[0:1, 0], range(4), nc.sync)
+        load_w13(0, nc.gpsimd)
         make_identity(nc, ident[:])
         nc.gpsimd.memset(window[:], 0.0)
+        load_scales(first_planes[0], w1_scales[0:1, 0], range(4), nc.sync)
+        load_scales(first_planes[1], w3_scales[0:1, 0], range(4), nc.sync)
         load_scales(later_planes[0], w1_scales[1:E, 0], range(4), nc.sync)
         load_scales(later_planes[1], w3_scales[1:E, 0], range(4), nc.sync)
         load_scales(w2s, w2_scales.rearrange("e s f n -> (e s) f n"), range(4), nc.sync)
@@ -92,7 +94,7 @@ def tile_moe_pkd_glu_sigmoid_kernel(
         sums = {}
 
         def gather_words(e):
-            token_words[e] = work.tile([P, C], U32, name="gw", bufs=3, align_bytes=ALIGN)
+            token_words[e] = work.tile([P, C], U32, name="gw", bufs=E, align_bytes=ALIGN)
             nc.vector.tensor_copy(out=token_words[e][:], in_=xw[:].bitcast(U32).indirect(listed(e * C, (e + 1) * C)))
 
         def gather_scales(e):
@@ -107,7 +109,7 @@ def tile_moe_pkd_glu_sigmoid_kernel(
                 out=acc[:],
                 lhsT=token_words[e][:, slots].bitcast(FP8X4),
                 lhsT_scale=token_scales[e][:, slots],
-                rhs=w13[e][:, m, 2 * PASS * s : 2 * PASS * (s + 1)].bitcast(FP4X4),
+                rhs=w13[e][:, 2 * (H * m + PASS * s) : 2 * (H * m + PASS * (s + 1))].bitcast(FP4X4),
                 rhs_scale=plane[:, PASS * s : PASS * (s + 1)],
                 start=True,
                 stop=True,
@@ -117,7 +119,7 @@ def tile_moe_pkd_glu_sigmoid_kernel(
             a = psum.tile([P, PASS], F32, name="a", bufs=2)
             first_product(j, s, 0, a)
             if j == 0:
-                place = 3 * W13_BYTES + s * 4 * PASS
+                place = GATES_AT + s * 4 * PASS
                 sig = shared.tile([P, 2, P, 2], F32, name="first_sig_%d" % s, align_bytes=ALIGN, offset=place)
             else:
                 sig = work.tile([P, 2, P, 2], F32, name="sig", bufs=4)
@@ -187,7 +189,7 @@ def tile_moe_pkd_glu_sigmoid_kernel(
         last = TILES - 1
         for e in range(E):
             gather_scales(e)
-        for e in range(E - 1):
+        for e in range(E):
             gather_words(e)
         load_w13(1, nc.sync)
         w2_rows = w2_words.rearrange("e s p b -> p (e s) b")
@@ -200,7 +202,6 @@ def tile_moe_pkd_glu_sigmoid_kernel(
             gate_half(step, 1)
             value_half(step, 1)
             if step == 1:
-                gather_words(E - 1)
                 nc.sync.dma_start(out=gates[:], in_=gate)
             if step % PER_EXPERT == 1 and step // PER_EXPERT + 2 < E:
                 load_w13(step // PER_EXPERT + 2, nc.sync)

@@ -24,10 +24,8 @@ TILES = E * C // P
 PER_EXPERT = C // P
 PER_COLUMN = 16
 ALIGN = 64
+BANK_BYTES = 4 * PASS
 W13_BYTES = 2 * 2 * H
-W13_AT = 4 * T
-W2_AT = W13_AT + 2 * W13_BYTES
-GATES_AT = W2_AT + E * PASSES * 2 * N
 SCATTER_ENDS = (256, 512, 704, 864, 1024)
 
 
@@ -37,7 +35,6 @@ def tile_moe_pkd_glu_sigmoid_kernel(
     nc = tc.nc
     with ExitStack() as ctx:
         keep = ctx.enter_context(tc.tile_pool(name="keep", bufs=1))
-        shared = ctx.enter_context(tc.tile_pool(name="shared", bufs=1))
         work = ctx.enter_context(tc.tile_pool(name="work", bufs=3))
         psum = ctx.enter_context(tc.psum_pool(name="psum", bufs=1))
 
@@ -47,15 +44,13 @@ def tile_moe_pkd_glu_sigmoid_kernel(
         w2s = keep.tile([P, E * PASSES * N], U8, name="w2s", align_bytes=ALIGN)
         gated = keep.tile([P, E * C], F32, name="gated")
         ident = keep.tile([P, P], F32, name="ident")
+        far_left = keep.tile([P, 8], F32, name="far_left")
         window = keep.tile([P, T], F32, name="window", align_bytes=ALIGN)
-        xw = shared.tile([P, T], I32, name="xw", align_bytes=ALIGN, offset=0)
-        w13 = [
-            shared.tile([P, W13_BYTES], U8, name="w13_%d" % e, align_bytes=ALIGN, offset=W13_AT + (e % 2) * W13_BYTES)
-            for e in range(E)
-        ]
-        w2w = shared.tile([P, E * PASSES, 2 * N], U8, name="w2w", align_bytes=ALIGN, offset=W2_AT)
-        xs = shared.tile([P, T], U8, name="xs", align_bytes=ALIGN, offset=W2_AT - T // 2)
-        gates = shared.tile([P, E * C], F32, name="gates", align_bytes=ALIGN, offset=GATES_AT)
+        xw = keep.tile([P, T], I32, name="xw", align_bytes=ALIGN)
+        w13 = [keep.tile([P, W13_BYTES], U8, name="w13_%d" % e, align_bytes=ALIGN) for e in range(E)]
+        w2w = keep.tile([P, E * PASSES, 2 * N], U8, name="w2w", align_bytes=ALIGN)
+        xs = keep.tile([P, T], U8, name="xs", align_bytes=ALIGN)
+        gates = keep.tile([P, E * C], F32, name="gates", align_bytes=ALIGN)
 
         def load_scales(plane, scale_rows, rows, queue):
             by_row = scale_rows.rearrange("g (q r) w -> r q g w", r=4)
@@ -68,6 +63,7 @@ def tile_moe_pkd_glu_sigmoid_kernel(
                 queue.dma_start(out=w13[e][:, 2 * H * m : 2 * H * (m + 1)].bitcast(I32), in_=(w1_words, w3_words)[m][e, 0].bitcast(I32))
 
         nc.vector.memset(xs[:].bitcast(I32), 0)
+        nc.vector.memset(far_left[:], -200.0)
         for plane in first_planes + later_planes + [w2s]:
             nc.vector.memset(plane[:].bitcast(I32), 0)
         nc.sync.dma_start(offsets[:], offs)
@@ -75,12 +71,19 @@ def tile_moe_pkd_glu_sigmoid_kernel(
         nc.sync.dma_start(out=xw[:], in_=x_words[0].rearrange("p t r -> p (t r)").bitcast(I32))
         load_w13(0, nc.gpsimd)
         make_identity(nc, ident[:])
-        nc.gpsimd.memset(window[:], 0.0)
-        load_scales(first_planes[0], w1_scales[0:1, 0], range(4), nc.sync)
-        load_scales(first_planes[1], w3_scales[0:1, 0], range(4), nc.sync)
+        nc.scalar.activation(out=window[:], in_=far_left[:, 0:1].to_broadcast([P, T]), func=SIGMOID)
+        for rows in (range(3), range(3, 4)):
+            load_scales(first_planes[0], w1_scales[0:1, 0], rows, nc.sync)
+            load_scales(first_planes[1], w3_scales[0:1, 0], rows, nc.sync)
         load_scales(later_planes[0], w1_scales[1:E, 0], range(4), nc.sync)
         load_scales(later_planes[1], w3_scales[1:E, 0], range(4), nc.sync)
+        load_w13(1, nc.sync)
+        w2_rows = w2_words.rearrange("e s p b -> p (e s) b")
+        nc.sync.dma_start(out=w2w[:].bitcast(I32), in_=w2_rows.bitcast(I32))
         load_scales(w2s, w2_scales.rearrange("e s f n -> (e s) f n"), range(4), nc.sync)
+        load_w13(2, nc.sync)
+        nc.sync.dma_start(out=gates[:], in_=gate)
+        load_w13(3, nc.sync)
 
         def listed(lo, hi):
             return offsets[:, lo // PER_COLUMN : hi // PER_COLUMN]
@@ -92,14 +95,23 @@ def tile_moe_pkd_glu_sigmoid_kernel(
         grouped = {}
         quantised = {}
         sums = {}
+        ring = []
 
         def gather_words(e):
-            token_words[e] = work.tile([P, C], U32, name="gw", bufs=E, align_bytes=ALIGN)
+            token_words[e] = work.tile([P, C], U32, name="gw", bufs=E - 1, align_bytes=ALIGN)
             nc.vector.tensor_copy(out=token_words[e][:], in_=xw[:].bitcast(U32).indirect(listed(e * C, (e + 1) * C)))
 
         def gather_scales(e):
-            token_scales[e] = work.tile([P, C], U8, name="gs", bufs=4, align_bytes=ALIGN)
+            token_scales[e] = work.tile([P, C], U8, name="gs", bufs=E - 1, align_bytes=ALIGN)
             nc.vector.tensor_copy(out=token_scales[e][:], in_=xs[:].indirect(listed(e * C, (e + 1) * C)))
+
+        def bank(number, shape, name):
+            return psum.tile(shape, F32, name=name, offset=number * BANK_BYTES)
+
+        def ring_bank(shape, name):
+            n = len(ring)
+            ring.append(name)
+            return bank(n % 2 if n < 4 else (n - 2) % 4, shape, name)
 
         def first_product(j, s, m, acc):
             e, c = divmod(j, PER_EXPERT)
@@ -116,18 +128,14 @@ def tile_moe_pkd_glu_sigmoid_kernel(
             )
 
         def gate_half(j, s):
-            a = psum.tile([P, PASS], F32, name="a", bufs=2)
+            a = ring_bank([P, PASS], "a_%d_%d" % (j, s))
             first_product(j, s, 0, a)
-            if j == 0:
-                place = GATES_AT + s * 4 * PASS
-                sig = shared.tile([P, 2, P, 2], F32, name="first_sig_%d" % s, align_bytes=ALIGN, offset=place)
-            else:
-                sig = work.tile([P, 2, P, 2], F32, name="sig", bufs=4)
+            sig = work.tile([P, 2, P, 2], F32, name="sig", bufs=4)
             nc.scalar.activation(out=sig[:], in_=a[:].rearrange("c (p u v) -> c u p v", u=2, v=2), func=SIGMOID)
             sigmoids[j, s] = sig
 
         def value_half(j, s):
-            b = psum.tile([P, PASS], F32, name="b", bufs=3)
+            b = bank(4 + (2 * j + s) % 3, [P, PASS], "b_%d_%d" % (j, s))
             first_product(j, s, 1, b)
             h = work.tile([P, 2, P, 2], BF16, name="h", bufs=6)
             nc.vector.tensor_tensor(
@@ -137,7 +145,7 @@ def tile_moe_pkd_glu_sigmoid_kernel(
 
         def turn(j, passes):
             n = len(passes)
-            xt = psum.tile([P, n, 2, P], F32, name="xt", bufs=2)
+            xt = ring_bank([P, n, 2, P], "xt_%d_%d" % (j, passes[0]))
             for k, s in enumerate(passes):
                 pairs = hidden[j, s][:].rearrange("c u p v -> c (u p v)").bitcast(F32)
                 for u in range(2):
@@ -160,7 +168,7 @@ def tile_moe_pkd_glu_sigmoid_kernel(
         def second_layer(j):
             e, c = divmod(j, PER_EXPERT)
             if c == 0:
-                sums[e] = psum.tile([P, C], F32, name="y", bufs=1)
+                sums[e] = bank(7, [P, C], "y_%d" % e)
             for s in range(PASSES):
                 codes, scales = quantised[j, s]
                 g = e * PASSES + s
@@ -187,42 +195,41 @@ def tile_moe_pkd_glu_sigmoid_kernel(
 
         both = tuple(range(PASSES))
         last = TILES - 1
-        for e in range(E):
+        for e in range(E - 1):
             gather_scales(e)
-        for e in range(E):
+        for e in range(E - 1):
             gather_words(e)
-        load_w13(1, nc.sync)
-        w2_rows = w2_words.rearrange("e s p b -> p (e s) b")
-        nc.sync.dma_start(out=w2w[:].bitcast(I32), in_=w2_rows.bitcast(I32))
         gate_half(0, 0)
         for step in range(TILES):
+            if step >= 2:
+                turn(step - 2, both)
             value_half(step, 0)
             if step >= 2:
                 quantise(step - 2, both)
+            if step >= 3:
+                second_layer(step - 3)
             gate_half(step, 1)
+            if step >= 4 and step % PER_EXPERT == 0:
+                empty_sums((step - 4) * P, (step - 2) * P)
             value_half(step, 1)
             if step == 1:
-                nc.sync.dma_start(out=gates[:], in_=gate)
-            if step % PER_EXPERT == 1 and step // PER_EXPERT + 2 < E:
-                load_w13(step // PER_EXPERT + 2, nc.sync)
+                gather_scales(E - 1)
+                gather_words(E - 1)
             if step < last:
                 gate_half(step + 1, 0)
-            if step >= 1:
-                turn(step - 1, both)
-            if step >= 2:
-                second_layer(step - 2)
-            if step >= 3 and step % PER_EXPERT == 1:
-                empty_sums((step - 3) * P, (step - 1) * P)
             if step in (4, 6):
                 scatter((step - 4) // PER_EXPERT)
+        turn(last - 1, both)
+        second_layer(last - 2)
+        empty_sums((last - 3) * P, (last - 1) * P)
         turn(last, (0,))
         quantise(last - 1, both)
         turn(last, (1,))
         second_layer(last - 1)
         empty_sums((last - 1) * P, last * P)
+        scatter(2)
         quantise(last, (0,))
         quantise(last, (1,))
-        scatter(2)
         second_layer(last)
         empty_sums(last * P, TILES * P)
         scatter(3)

@@ -35,6 +35,7 @@ def tile_moe_pkd_glu_sigmoid_kernel(
     nc = tc.nc
     with ExitStack() as ctx:
         keep = ctx.enter_context(tc.tile_pool(name="keep", bufs=1))
+        shared = ctx.enter_context(tc.tile_pool(name="shared", bufs=1))
         work = ctx.enter_context(tc.tile_pool(name="work", bufs=3))
         psum = ctx.enter_context(tc.psum_pool(name="psum", bufs=1))
 
@@ -62,26 +63,36 @@ def tile_moe_pkd_glu_sigmoid_kernel(
             for m in range(2):
                 queue.dma_start(out=w13[e][:, 2 * H * m : 2 * H * (m + 1)].bitcast(I32), in_=(w1_words, w3_words)[m][e, 0].bitcast(I32))
 
-        nc.vector.memset(xs[:].bitcast(I32), 0)
-        nc.vector.memset(far_left[:], -200.0)
-        for plane in first_planes + later_planes + [w2s]:
-            nc.vector.memset(plane[:].bitcast(I32), 0)
+        def clear_in_odd_runs(plane):
+            words = plane[:].bitcast(I32)
+            cut = words.shape[1] // 2 + 1
+            nc.vector.memset(words[:, :cut], 0)
+            nc.vector.memset(words[:, cut:], 0)
+
+        clear_in_odd_runs(xs)
+        nc.vector.memset(far_left[:, 0:1], -200.0)
+        for plane in first_planes + later_planes[:1]:
+            clear_in_odd_runs(plane)
+        nc.vector.memset(later_planes[1][:].bitcast(I32), 0)
         nc.sync.dma_start(offsets[:], offs)
         load_scales(xs, x_scales, range(4), nc.sync)
+        load_scales(first_planes[0], w1_scales[0:1, 0], range(1), nc.sync)
         nc.sync.dma_start(out=xw[:], in_=x_words[0].rearrange("p t r -> p (t r)").bitcast(I32))
         load_w13(0, nc.gpsimd)
+        nc.gpsimd.memset(w2s[:].bitcast(I32), 0)
         make_identity(nc, ident[:])
         nc.scalar.activation(out=window[:], in_=far_left[:, 0:1].to_broadcast([P, T]), func=SIGMOID)
-        for rows in (range(3), range(3, 4)):
-            load_scales(first_planes[0], w1_scales[0:1, 0], rows, nc.sync)
-            load_scales(first_planes[1], w3_scales[0:1, 0], rows, nc.sync)
+        load_scales(first_planes[0], w1_scales[0:1, 0], range(1, 3), nc.sync)
+        load_scales(first_planes[1], w3_scales[0:1, 0], range(3), nc.sync)
+        load_scales(first_planes[0], w1_scales[0:1, 0], range(3, 4), nc.sync)
+        load_scales(first_planes[1], w3_scales[0:1, 0], range(3, 4), nc.sync)
         load_scales(later_planes[0], w1_scales[1:E, 0], range(4), nc.sync)
         load_scales(later_planes[1], w3_scales[1:E, 0], range(4), nc.sync)
         load_w13(1, nc.sync)
         w2_rows = w2_words.rearrange("e s p b -> p (e s) b")
+        load_w13(2, nc.sync)
         nc.sync.dma_start(out=w2w[:].bitcast(I32), in_=w2_rows.bitcast(I32))
         load_scales(w2s, w2_scales.rearrange("e s f n -> (e s) f n"), range(4), nc.sync)
-        load_w13(2, nc.sync)
         nc.sync.dma_start(out=gates[:], in_=gate)
         load_w13(3, nc.sync)
 
@@ -92,18 +103,24 @@ def tile_moe_pkd_glu_sigmoid_kernel(
         token_scales = {}
         sigmoids = {}
         hidden = {}
-        grouped = {}
         quantised = {}
         sums = {}
         ring = []
 
-        def gather_words(e):
-            token_words[e] = work.tile([P, C], U32, name="gw", bufs=E - 1, align_bytes=ALIGN)
-            nc.vector.tensor_copy(out=token_words[e][:], in_=xw[:].bitcast(U32).indirect(listed(e * C, (e + 1) * C)))
+        def gather(window_of_tokens, dtype, found, experts, pool, place):
+            n = len(experts) * C
+            name = "gathered_%d_%d" % (len(found), dtype == U8)
+            tile = pool.tile([P, n], dtype, name=name, align_bytes=ALIGN, offset=place)
+            lo = experts[0] * C
+            nc.vector.tensor_copy(out=tile[:], in_=window_of_tokens.indirect(listed(lo, lo + n)))
+            for k, e in enumerate(experts):
+                found[e] = tile[:, k * C : (k + 1) * C]
 
-        def gather_scales(e):
-            token_scales[e] = work.tile([P, C], U8, name="gs", bufs=E - 1, align_bytes=ALIGN)
-            nc.vector.tensor_copy(out=token_scales[e][:], in_=xs[:].indirect(listed(e * C, (e + 1) * C)))
+        def gather_words(experts, pool=keep, place=None):
+            gather(xw[:].bitcast(U32), U32, token_words, experts, pool, place)
+
+        def gather_scales(experts, pool=keep, place=None):
+            gather(xs[:], U8, token_scales, experts, pool, place)
 
         def bank(number, shape, name):
             return psum.tile(shape, F32, name=name, offset=number * BANK_BYTES)
@@ -130,7 +147,10 @@ def tile_moe_pkd_glu_sigmoid_kernel(
         def gate_half(j, s):
             a = ring_bank([P, PASS], "a_%d_%d" % (j, s))
             first_product(j, s, 0, a)
-            sig = work.tile([P, 2, P, 2], F32, name="sig", bufs=4)
+            if (j, s) == (0, 0):
+                sig = shared.tile([P, 2, P, 2], F32, name="first_sig", align_bytes=ALIGN, offset=0)
+            else:
+                sig = work.tile([P, 2, P, 2], F32, name="sig", bufs=4)
             nc.scalar.activation(out=sig[:], in_=a[:].rearrange("c (p u v) -> c u p v", u=2, v=2), func=SIGMOID)
             sigmoids[j, s] = sig
 
@@ -143,27 +163,28 @@ def tile_moe_pkd_glu_sigmoid_kernel(
             )
             hidden[j, s] = h
 
-        def turn(j, passes):
+        def turn(j, passes, ht, at):
             n = len(passes)
             xt = ring_bank([P, n, 2, P], "xt_%d_%d" % (j, passes[0]))
             for k, s in enumerate(passes):
                 pairs = hidden[j, s][:].rearrange("c u p v -> c (u p v)").bitcast(F32)
                 for u in range(2):
                     nc.tensor.transpose(xt[:, k, u, :], pairs[:, u * P : (u + 1) * P], ident[:])
-            ht = work.tile([P, n * PASS], BF16, name="ht", align_bytes=ALIGN)
             nc.scalar.copy(
-                out=ht[:].bitcast(F32).rearrange("p (s c u) -> p s c u", s=n, u=2),
+                out=ht[:, at * PASS : (at + n) * PASS].bitcast(F32).rearrange("p (s c u) -> p s c u", s=n, u=2),
                 in_=xt[:].rearrange("p s u c -> p s c u"),
             )
-            grouped[j, passes] = ht
 
-        def quantise(j, passes):
-            n = len(passes)
+        def turned_tile(halves):
+            return work.tile([P, halves * PASS], BF16, name="ht", align_bytes=ALIGN)
+
+        def quantise(ht, halves):
+            n = len(halves)
             codes = work.tile([P, n * P], U32, name="codes", align_bytes=ALIGN)
             scales = work.tile([P, n * P], U8, name="scales", align_bytes=ALIGN)
-            nc.vector.quantize_mx(out=codes[:].bitcast(FP8X4), scales=scales[:], in_=grouped[j, passes][:])
-            for k, s in enumerate(passes):
-                quantised[j, s] = (codes[:, k * P : (k + 1) * P], scales[:, k * P : (k + 1) * P])
+            nc.vector.quantize_mx(out=codes[:].bitcast(FP8X4), scales=scales[:], in_=ht[:])
+            for k, half in enumerate(halves):
+                quantised[half] = (codes[:, k * P : (k + 1) * P], scales[:, k * P : (k + 1) * P])
 
         def second_layer(j):
             e, c = divmod(j, PER_EXPERT)
@@ -195,41 +216,43 @@ def tile_moe_pkd_glu_sigmoid_kernel(
 
         both = tuple(range(PASSES))
         last = TILES - 1
-        for e in range(E - 1):
-            gather_scales(e)
-        for e in range(E - 1):
-            gather_words(e)
+        gather_scales((0, 1, 2))
+        gather_words((0,))
+        gather_words((1, 2, 3))
         gate_half(0, 0)
         for step in range(TILES):
-            if step >= 2:
-                turn(step - 2, both)
+            j = step - 2
+            if j >= 0:
+                ht = turned_tile(PASSES)
+                turn(j, both, ht, 0)
             value_half(step, 0)
-            if step >= 2:
-                quantise(step - 2, both)
+            if step == 0:
+                gather_scales((E - 1,), shared, 0)
+            if j >= 0:
+                quantise(ht, [(j, s) for s in both])
             if step >= 3:
                 second_layer(step - 3)
             gate_half(step, 1)
             if step >= 4 and step % PER_EXPERT == 0:
                 empty_sums((step - 4) * P, (step - 2) * P)
             value_half(step, 1)
-            if step == 1:
-                gather_scales(E - 1)
-                gather_words(E - 1)
             if step < last:
                 gate_half(step + 1, 0)
             if step in (4, 6):
                 scatter((step - 4) // PER_EXPERT)
-        turn(last - 1, both)
+        ht = turned_tile(PASSES)
+        turn(last - 1, both, ht, 0)
         second_layer(last - 2)
         empty_sums((last - 3) * P, (last - 1) * P)
-        turn(last, (0,))
-        quantise(last - 1, both)
-        turn(last, (1,))
+        halves = [turned_tile(1) for s in both]
+        turn(last, (0,), halves[0], 0)
+        quantise(ht, [(last - 1, s) for s in both])
+        turn(last, (1,), halves[1], 0)
         second_layer(last - 1)
         empty_sums((last - 1) * P, last * P)
         scatter(2)
-        quantise(last, (0,))
-        quantise(last, (1,))
+        for s in both:
+            quantise(halves[s], [(last, s)])
         second_layer(last)
         empty_sums(last * P, TILES * P)
         scatter(3)

@@ -69,13 +69,16 @@ def tile_moe_pkd_glu_sigmoid_kernel(
             nc.vector.memset(words[:, :cut], 0)
             nc.vector.memset(words[:, cut:], 0)
 
-        clear_in_odd_runs(xs)
         nc.vector.memset(far_left[:, 0:1], -200.0)
         for plane in first_planes + later_planes[:1]:
             clear_in_odd_runs(plane)
         nc.vector.memset(later_planes[1][:].bitcast(I32), 0)
         nc.sync.dma_start(offsets[:], offs)
-        load_scales(xs, x_scales, range(4), nc.sync)
+        for q in range(4):
+            rows = x_scales[0, 4 * q : 4 * q + 4, :].bitcast(I32)
+            (nc.sync, nc.scalar)[q // 2].dma_start(
+                out=xs[32 * q : 32 * q + 32, :].bitcast(I32), in_=rows.unsqueeze(0).to_broadcast([8, 4, T // 4])
+            )
         load_scales(first_planes[0], w1_scales[0:1, 0], range(1), nc.sync)
         nc.sync.dma_start(out=xw[:], in_=x_words[0].rearrange("p t r -> p (t r)").bitcast(I32))
         load_w13(0, nc.gpsimd)

@@ -25,6 +25,8 @@ PER_EXPERT = C // P
 PER_COLUMN = 16
 ALIGN = 64
 BANK_BYTES = 4 * PASS
+LAST_EXPERT = (E - 1) * C
+FIRST_GATHER = T // 8
 W13_BYTES = 2 * 2 * H
 SCATTER_ENDS = (256, 512, 704, 864, 1024)
 
@@ -59,8 +61,8 @@ def tile_moe_pkd_glu_sigmoid_kernel(
                 dst = plane[r:P:32, :].bitcast(I32).rearrange("q (g w) -> q g w", g=scale_rows.shape[0])
                 queue.dma_start(out=dst, in_=by_row[r].bitcast(I32))
 
-        def load_w13(e, queue):
-            for m in range(2):
+        def load_w13(e, queue, matrices=(0, 1)):
+            for m in matrices:
                 queue.dma_start(out=w13[e][:, 2 * H * m : 2 * H * (m + 1)].bitcast(I32), in_=(w1_words, w3_words)[m][e, 0].bitcast(I32))
 
         def clear_in_odd_runs(plane):
@@ -81,11 +83,12 @@ def tile_moe_pkd_glu_sigmoid_kernel(
             )
         load_scales(first_planes[0], w1_scales[0:1, 0], range(1), nc.sync)
         nc.sync.dma_start(out=xw[:], in_=x_words[0].rearrange("p t r -> p (t r)").bitcast(I32))
-        load_w13(0, nc.gpsimd)
+        load_w13(0, nc.gpsimd, (0,))
         nc.gpsimd.memset(w2s[:].bitcast(I32), 0)
         make_identity(nc, ident[:])
         nc.scalar.activation(out=window[:], in_=far_left[:, 0:1].to_broadcast([P, T]), func=SIGMOID)
         load_scales(first_planes[0], w1_scales[0:1, 0], range(1, 3), nc.sync)
+        load_w13(0, nc.sync, (1,))
         load_scales(first_planes[1], w3_scales[0:1, 0], range(3), nc.sync)
         load_scales(first_planes[0], w1_scales[0:1, 0], range(3, 4), nc.sync)
         load_scales(first_planes[1], w3_scales[0:1, 0], range(3, 4), nc.sync)
@@ -102,28 +105,20 @@ def tile_moe_pkd_glu_sigmoid_kernel(
         def listed(lo, hi):
             return offsets[:, lo // PER_COLUMN : hi // PER_COLUMN]
 
-        token_words = {}
-        token_scales = {}
+        slot_words = keep.tile([P, E * C], U32, name="slot_words", align_bytes=ALIGN)
+        early_scales = keep.tile([P, LAST_EXPERT], U8, name="early_scales", align_bytes=ALIGN)
+        last_scales = shared.tile([P, C], U8, name="last_scales", align_bytes=ALIGN, offset=0)
         sigmoids = {}
         hidden = {}
         quantised = {}
         sums = {}
         ring = []
 
-        def gather(window_of_tokens, dtype, found, experts, pool, place):
-            n = len(experts) * C
-            name = "gathered_%d_%d" % (len(found), dtype == U8)
-            tile = pool.tile([P, n], dtype, name=name, align_bytes=ALIGN, offset=place)
-            lo = experts[0] * C
-            nc.vector.tensor_copy(out=tile[:], in_=window_of_tokens.indirect(listed(lo, lo + n)))
-            for k, e in enumerate(experts):
-                found[e] = tile[:, k * C : (k + 1) * C]
+        def gather_words(lo, hi):
+            nc.vector.tensor_copy(out=slot_words[:, lo:hi], in_=xw[:].bitcast(U32).indirect(listed(lo, hi)))
 
-        def gather_words(experts, pool=keep, place=None):
-            gather(xw[:].bitcast(U32), U32, token_words, experts, pool, place)
-
-        def gather_scales(experts, pool=keep, place=None):
-            gather(xs[:], U8, token_scales, experts, pool, place)
+        def gather_scales(tile, lo, hi):
+            nc.vector.tensor_copy(out=tile[:], in_=xs[:].indirect(listed(lo, hi)))
 
         def bank(number, shape, name):
             return psum.tile(shape, F32, name=name, offset=number * BANK_BYTES)
@@ -134,13 +129,17 @@ def tile_moe_pkd_glu_sigmoid_kernel(
             return bank(n % 2 if n < 4 else (n - 2) % 4, shape, name)
 
         def first_product(j, s, m, acc):
-            e, c = divmod(j, PER_EXPERT)
-            slots = slice(c * P, (c + 1) * P)
+            e = j // PER_EXPERT
+            lo = j * P
+            if lo < LAST_EXPERT:
+                slot_scales = early_scales[:, lo : lo + P]
+            else:
+                slot_scales = last_scales[:, lo - LAST_EXPERT : lo - LAST_EXPERT + P]
             plane = later_planes[m][:, (e - 1) * H : e * H] if e else first_planes[m][:]
             nc.tensor.matmul_mx(
                 out=acc[:],
-                lhsT=token_words[e][:, slots].bitcast(FP8X4),
-                lhsT_scale=token_scales[e][:, slots],
+                lhsT=slot_words[:, lo : lo + P].bitcast(FP8X4),
+                lhsT_scale=slot_scales,
                 rhs=w13[e][:, 2 * (H * m + PASS * s) : 2 * (H * m + PASS * (s + 1))].bitcast(FP4X4),
                 rhs_scale=plane[:, PASS * s : PASS * (s + 1)],
                 start=True,
@@ -219,9 +218,9 @@ def tile_moe_pkd_glu_sigmoid_kernel(
 
         both = tuple(range(PASSES))
         last = TILES - 1
-        gather_scales((0, 1, 2))
-        gather_words((0,))
-        gather_words((1, 2, 3))
+        gather_scales(early_scales, 0, LAST_EXPERT)
+        gather_words(0, FIRST_GATHER)
+        gather_words(FIRST_GATHER, E * C)
         gate_half(0, 0)
         for step in range(TILES):
             j = step - 2
@@ -230,7 +229,7 @@ def tile_moe_pkd_glu_sigmoid_kernel(
                 turn(j, both, ht, 0)
             value_half(step, 0)
             if step == 0:
-                gather_scales((E - 1,), shared, 0)
+                gather_scales(last_scales, LAST_EXPERT, E * C)
             if j >= 0:
                 quantise(ht, [(j, s) for s in both])
             if step >= 3:

@@ -25,6 +25,8 @@ PER_EXPERT = C // P
 PER_COLUMN = 16
 ALIGN = 64
 BANK_BYTES = 4 * PASS
+SIGMOID_RING = (1, 4, 2, 3)
+VALUE_RING = (0, 5, 6)
 LAST_EXPERT = (E - 1) * C
 FIRST_GATHER = T // 8
 W13_BYTES = 2 * 2 * H
@@ -83,14 +85,15 @@ def tile_moe_pkd_glu_sigmoid_kernel(
             )
         load_scales(first_planes[0], w1_scales[0:1, 0], range(1), nc.sync)
         nc.sync.dma_start(out=xw[:], in_=x_words[0].rearrange("p t r -> p (t r)").bitcast(I32))
-        load_w13(0, nc.gpsimd, (0,))
         nc.gpsimd.memset(w2s[:].bitcast(I32), 0)
-        make_identity(nc, ident[:])
+        nc.gpsimd.memset(ident[:], 0.0)
+        load_w13(0, nc.gpsimd, (0,))
+        make_identity(nc, ident[:], nomemset=True)
         nc.scalar.activation(out=window[:], in_=far_left[:, 0:1].to_broadcast([P, T]), func=SIGMOID)
         load_scales(first_planes[0], w1_scales[0:1, 0], range(1, 3), nc.sync)
-        load_w13(0, nc.sync, (1,))
         load_scales(first_planes[1], w3_scales[0:1, 0], range(3), nc.sync)
         load_scales(first_planes[0], w1_scales[0:1, 0], range(3, 4), nc.sync)
+        load_w13(0, nc.sync, (1,))
         load_scales(first_planes[1], w3_scales[0:1, 0], range(3, 4), nc.sync)
         load_scales(later_planes[0], w1_scales[1:E, 0], range(4), nc.sync)
         load_scales(later_planes[1], w3_scales[1:E, 0], range(4), nc.sync)
@@ -126,7 +129,7 @@ def tile_moe_pkd_glu_sigmoid_kernel(
         def ring_bank(shape, name):
             n = len(ring)
             ring.append(name)
-            return bank(n % 2 if n < 4 else (n - 2) % 4, shape, name)
+            return bank(SIGMOID_RING[(n - 2) % 4] if n >= 2 else n, shape, name)
 
         def first_product(j, s, m, acc):
             e = j // PER_EXPERT
@@ -157,7 +160,7 @@ def tile_moe_pkd_glu_sigmoid_kernel(
             sigmoids[j, s] = sig
 
         def value_half(j, s):
-            b = bank(4 + (2 * j + s) % 3, [P, PASS], "b_%d_%d" % (j, s))
+            b = bank(VALUE_RING[(2 * j + s) % 3] if (j, s) != (0, 0) else SIGMOID_RING[1], [P, PASS], "b_%d_%d" % (j, s))
             first_product(j, s, 1, b)
             h = work.tile([P, 2, P, 2], BF16, name="h", bufs=6)
             nc.vector.tensor_tensor(

@@ -73,10 +73,11 @@ def tile_moe_pkd_glu_sigmoid_kernel(
             nc.vector.memset(words[:, :cut], 0)
             nc.vector.memset(words[:, cut:], 0)
 
+        clear_in_odd_runs(first_planes[0])
         nc.vector.memset(far_left[:, 0:1], -200.0)
-        for plane in first_planes + later_planes[:1]:
-            clear_in_odd_runs(plane)
-        nc.vector.memset(later_planes[1][:].bitcast(I32), 0)
+        clear_in_odd_runs(first_planes[1])
+        for plane in later_planes + [w2s]:
+            nc.vector.memset(plane[:].bitcast(I32), 0)
         nc.sync.dma_start(offsets[:], offs)
         for q in range(4):
             rows = x_scales[0, 4 * q : 4 * q + 4, :].bitcast(I32)
@@ -85,10 +86,8 @@ def tile_moe_pkd_glu_sigmoid_kernel(
             )
         load_scales(first_planes[0], w1_scales[0:1, 0], range(1), nc.sync)
         nc.sync.dma_start(out=xw[:], in_=x_words[0].rearrange("p t r -> p (t r)").bitcast(I32))
-        nc.gpsimd.memset(w2s[:].bitcast(I32), 0)
-        nc.gpsimd.memset(ident[:], 0.0)
-        load_w13(0, nc.gpsimd, (0,))
-        make_identity(nc, ident[:], nomemset=True)
+        load_w13(0, nc.sync, (0,))
+        make_identity(nc, ident[:])
         nc.scalar.activation(out=window[:], in_=far_left[:, 0:1].to_broadcast([P, T]), func=SIGMOID)
         load_scales(first_planes[0], w1_scales[0:1, 0], range(1, 3), nc.sync)
         load_scales(first_planes[1], w3_scales[0:1, 0], range(3), nc.sync)

@@ -73,17 +73,15 @@ def tile_moe_pkd_glu_sigmoid_kernel(
             nc.vector.memset(words[:, :cut], 0)
             nc.vector.memset(words[:, cut:], 0)
 
+        clear_in_odd_runs(xs)
         clear_in_odd_runs(first_planes[0])
         nc.vector.memset(far_left[:, 0:1], -200.0)
         clear_in_odd_runs(first_planes[1])
         for plane in later_planes + [w2s]:
             nc.vector.memset(plane[:].bitcast(I32), 0)
         nc.sync.dma_start(offsets[:], offs)
-        for q in range(4):
-            rows = x_scales[0, 4 * q : 4 * q + 4, :].bitcast(I32)
-            (nc.sync, nc.scalar)[q // 2].dma_start(
-                out=xs[32 * q : 32 * q + 32, :].bitcast(I32), in_=rows.unsqueeze(0).to_broadcast([8, 4, T // 4])
-            )
+        load_scales(xs, x_scales, range(2), nc.sync)
+        load_scales(xs, x_scales, range(2, 4), nc.scalar)
         load_scales(first_planes[0], w1_scales[0:1, 0], range(1), nc.sync)
         nc.sync.dma_start(out=xw[:], in_=x_words[0].rearrange("p t r -> p (t r)").bitcast(I32))
         load_w13(0, nc.sync, (0,))

@@ -25,10 +25,11 @@ PER_EXPERT = C // P
 PER_COLUMN = 16
 ALIGN = 64
 BANK_BYTES = 4 * PASS
-SIGMOID_RING = (1, 4, 2, 3)
-VALUE_RING = (0, 5, 6)
+BANKS = (0, 1, 2, 3, 7, 0, 3, 1, 2, 3, 0, 1, 7, 0, 1, 7, 2, 3, 1, 0, 2, 3, 7, 0, 1, 2, 7, 3, 0, 1)
+VALUE_RING = (4, 5, 6)
 LAST_EXPERT = (E - 1) * C
 FIRST_GATHER = T // 8
+FIRST = 2
 W13_BYTES = 2 * 2 * H
 SCATTER_ENDS = (256, 512, 704, 864, 1024)
 
@@ -44,14 +45,14 @@ def tile_moe_pkd_glu_sigmoid_kernel(
         psum = ctx.enter_context(tc.psum_pool(name="psum", bufs=1))
 
         offsets = keep.tile([P, E * C // PER_COLUMN], U16, name="offsets")
-        first_planes = [keep.tile([P, H], U8, name="first_plane_%d" % m, align_bytes=ALIGN) for m in range(2)]
-        later_planes = [keep.tile([P, (E - 1) * H], U8, name="later_plane_%d" % m, align_bytes=ALIGN) for m in range(2)]
+        first_planes = [keep.tile([P, FIRST * H], U8, name="first_plane_%d" % m, align_bytes=ALIGN) for m in range(2)]
+        later_planes = [keep.tile([P, (E - FIRST) * H], U8, name="later_plane_%d" % m, align_bytes=ALIGN) for m in range(2)]
         w2s = keep.tile([P, E * PASSES * N], U8, name="w2s", align_bytes=ALIGN)
         gated = keep.tile([P, E * C], F32, name="gated")
         ident = keep.tile([P, P], F32, name="ident")
         far_left = keep.tile([P, 8], F32, name="far_left")
         window = keep.tile([P, T], F32, name="window", align_bytes=ALIGN)
-        xw = keep.tile([P, T], I32, name="xw", align_bytes=ALIGN)
+        xw = shared.tile([P, T], I32, name="xw", align_bytes=ALIGN, offset=0)
         w13 = [keep.tile([P, W13_BYTES], U8, name="w13_%d" % e, align_bytes=ALIGN) for e in range(E)]
         w2w = keep.tile([P, E * PASSES, 2 * N], U8, name="w2w", align_bytes=ALIGN)
         xs = keep.tile([P, T], U8, name="xs", align_bytes=ALIGN)
@@ -67,38 +68,31 @@ def tile_moe_pkd_glu_sigmoid_kernel(
             for m in matrices:
                 queue.dma_start(out=w13[e][:, 2 * H * m : 2 * H * (m + 1)].bitcast(I32), in_=(w1_words, w3_words)[m][e, 0].bitcast(I32))
 
-        def clear_in_odd_runs(plane):
-            words = plane[:].bitcast(I32)
-            cut = words.shape[1] // 2 + 1
-            nc.vector.memset(words[:, :cut], 0)
-            nc.vector.memset(words[:, cut:], 0)
-
-        clear_in_odd_runs(xs)
-        clear_in_odd_runs(first_planes[0])
+        nc.vector.memset(xs[:].bitcast(I32), 0)
+        nc.vector.memset(first_planes[0][:].bitcast(I32), 0)
         nc.vector.memset(far_left[:, 0:1], -200.0)
-        clear_in_odd_runs(first_planes[1])
-        for plane in later_planes + [w2s]:
+        for plane in first_planes[1:] + later_planes + [w2s]:
             nc.vector.memset(plane[:].bitcast(I32), 0)
+        nc.vector.memset(ident[:], 0.0)
         nc.sync.dma_start(offsets[:], offs)
         load_scales(xs, x_scales, range(2), nc.sync)
         load_scales(xs, x_scales, range(2, 4), nc.scalar)
-        load_scales(first_planes[0], w1_scales[0:1, 0], range(1), nc.sync)
+        load_scales(first_planes[0], w1_scales[0:FIRST, 0], range(1), nc.sync)
         nc.sync.dma_start(out=xw[:], in_=x_words[0].rearrange("p t r -> p (t r)").bitcast(I32))
         load_w13(0, nc.sync, (0,))
-        make_identity(nc, ident[:])
+        make_identity(nc, ident[:], nomemset=True)
         nc.scalar.activation(out=window[:], in_=far_left[:, 0:1].to_broadcast([P, T]), func=SIGMOID)
-        load_scales(first_planes[0], w1_scales[0:1, 0], range(1, 3), nc.sync)
-        load_scales(first_planes[1], w3_scales[0:1, 0], range(3), nc.sync)
-        load_scales(first_planes[0], w1_scales[0:1, 0], range(3, 4), nc.sync)
+        load_scales(first_planes[0], w1_scales[0:FIRST, 0], range(1, 4), nc.sync)
+        load_scales(first_planes[1], w3_scales[0:FIRST, 0], range(3), nc.sync)
         load_w13(0, nc.sync, (1,))
-        load_scales(first_planes[1], w3_scales[0:1, 0], range(3, 4), nc.sync)
-        load_scales(later_planes[0], w1_scales[1:E, 0], range(4), nc.sync)
-        load_scales(later_planes[1], w3_scales[1:E, 0], range(4), nc.sync)
-        load_w13(1, nc.sync)
+        load_scales(first_planes[1], w3_scales[0:FIRST, 0], range(3, 4), nc.sync)
         w2_rows = w2_words.rearrange("e s p b -> p (e s) b")
-        load_w13(2, nc.sync)
+        load_w13(1, nc.sync)
         nc.sync.dma_start(out=w2w[:].bitcast(I32), in_=w2_rows.bitcast(I32))
         load_scales(w2s, w2_scales.rearrange("e s f n -> (e s) f n"), range(4), nc.sync)
+        load_scales(later_planes[0], w1_scales[FIRST:E, 0], range(4), nc.sync)
+        load_scales(later_planes[1], w3_scales[FIRST:E, 0], range(4), nc.sync)
+        load_w13(2, nc.sync)
         nc.sync.dma_start(out=gates[:], in_=gate)
         load_w13(3, nc.sync)
 
@@ -126,7 +120,7 @@ def tile_moe_pkd_glu_sigmoid_kernel(
         def ring_bank(shape, name):
             n = len(ring)
             ring.append(name)
-            return bank(SIGMOID_RING[(n - 2) % 4] if n >= 2 else n, shape, name)
+            return bank(BANKS[n], shape, name)
 
         def first_product(j, s, m, acc):
             e = j // PER_EXPERT
@@ -135,7 +129,7 @@ def tile_moe_pkd_glu_sigmoid_kernel(
                 slot_scales = early_scales[:, lo : lo + P]
             else:
                 slot_scales = last_scales[:, lo - LAST_EXPERT : lo - LAST_EXPERT + P]
-            plane = later_planes[m][:, (e - 1) * H : e * H] if e else first_planes[m][:]
+            plane = later_planes[m][:, (e - FIRST) * H : (e - FIRST + 1) * H] if e >= FIRST else first_planes[m][:, e * H : (e + 1) * H]
             nc.tensor.matmul_mx(
                 out=acc[:],
                 lhsT=slot_words[:, lo : lo + P].bitcast(FP8X4),
@@ -149,17 +143,14 @@ def tile_moe_pkd_glu_sigmoid_kernel(
         def gate_half(j, s):
             a = ring_bank([P, PASS], "a_%d_%d" % (j, s))
             first_product(j, s, 0, a)
-            if (j, s) == (0, 0):
-                sig = shared.tile([P, 2, P, 2], F32, name="first_sig", align_bytes=ALIGN, offset=0)
-            else:
-                sig = work.tile([P, 2, P, 2], F32, name="sig", bufs=4)
+            sig = work.tile([P, 2, P, 2], F32, name="sig", bufs=6)
             nc.scalar.activation(out=sig[:], in_=a[:].rearrange("c (p u v) -> c u p v", u=2, v=2), func=SIGMOID)
             sigmoids[j, s] = sig
 
         def value_half(j, s):
-            b = bank(VALUE_RING[(2 * j + s) % 3] if (j, s) != (0, 0) else SIGMOID_RING[1], [P, PASS], "b_%d_%d" % (j, s))
+            b = bank(VALUE_RING[len(hidden) % 3] if (j, s) != (0, 0) else 7, [P, PASS], "b_%d_%d" % (j, s))
             first_product(j, s, 1, b)
-            h = work.tile([P, 2, P, 2], BF16, name="h", bufs=6)
+            h = work.tile([P, 2, P, 2], BF16, name="h", bufs=8)
             nc.vector.tensor_tensor(
                 out=h[:], in0=b[:].rearrange("c (p u v) -> c u p v", u=2, v=2), in1=sigmoids[j, s][:], op=MULT
             )
@@ -182,32 +173,31 @@ def tile_moe_pkd_glu_sigmoid_kernel(
 
         def quantise(ht, halves):
             n = len(halves)
-            codes = work.tile([P, n * P], U32, name="codes", align_bytes=ALIGN)
-            scales = work.tile([P, n * P], U8, name="scales", align_bytes=ALIGN)
+            codes = work.tile([P, n * P], U32, name="codes", bufs=4, align_bytes=ALIGN)
+            scales = work.tile([P, n * P], U8, name="scales", bufs=4, align_bytes=ALIGN)
             nc.vector.quantize_mx(out=codes[:].bitcast(FP8X4), scales=scales[:], in_=ht[:])
             for k, half in enumerate(halves):
                 quantised[half] = (codes[:, k * P : (k + 1) * P], scales[:, k * P : (k + 1) * P])
 
-        def second_layer(j):
-            e, c = divmod(j, PER_EXPERT)
-            if c == 0:
-                sums[e] = bank(7, [P, C], "y_%d" % e)
-            for s in range(PASSES):
-                codes, scales = quantised[j, s]
-                g = e * PASSES + s
-                nc.tensor.matmul_mx(
-                    out=sums[e][:, c * P : (c + 1) * P],
-                    lhsT=w2w[:, g, :].bitcast(FP4X4),
-                    lhsT_scale=w2s[:, g * N : (g + 1) * N],
-                    rhs=codes.bitcast(FP8X4),
-                    rhs_scale=scales,
-                    start=(s == 0),
-                    stop=(s == PASSES - 1),
-                )
+        def second_layer(first, count):
+            y = ring_bank([P, count * P], "y_%d" % first)
+            for c in reversed(range(count)):
+                for s in range(PASSES):
+                    codes, scales = quantised[first + c, s]
+                    g = (first + c) // PER_EXPERT * PASSES + s
+                    nc.tensor.matmul_mx(
+                        out=y[:, c * P : (c + 1) * P],
+                        lhsT=w2w[:, g, :].bitcast(FP4X4),
+                        lhsT_scale=w2s[:, g * N : (g + 1) * N],
+                        rhs=codes.bitcast(FP8X4),
+                        rhs_scale=scales,
+                        start=(s == 0),
+                        stop=(s == PASSES - 1),
+                    )
+            sums[first] = y
 
-        def empty_sums(lo, hi):
-            e = lo // C
-            nc.scalar.copy(out=gated[:, lo:hi], in_=sums[e][:, lo - e * C : hi - e * C])
+        def empty_sums(first, count):
+            nc.scalar.copy(out=gated[:, first * P : (first + count) * P], in_=sums[first][:])
 
         def scatter(piece):
             lo = SCATTER_ENDS[piece - 1] if piece else 0
@@ -217,46 +207,85 @@ def tile_moe_pkd_glu_sigmoid_kernel(
             )
 
         both = tuple(range(PASSES))
-        last = TILES - 1
-        gather_scales(early_scales, 0, LAST_EXPERT)
-        gather_words(0, FIRST_GATHER)
-        gather_words(FIRST_GATHER, E * C)
+        turned = {}
+
+        def turn_tile(j):
+            turned[j] = turned_tile(PASSES)
+            turn(j, both, turned[j], 0)
+
+        def quantise_tile(j):
+            quantise(turned[j], [(j, s) for s in both])
+
+        gather_scales(early_scales, 0, 768)
+        gather_words(0, 160)
+        gather_words(160, 384)
+        gather_words(384, 1024)
+        gather_scales(last_scales, 768, 1024)
         gate_half(0, 0)
-        for step in range(TILES):
-            j = step - 2
-            if j >= 0:
-                ht = turned_tile(PASSES)
-                turn(j, both, ht, 0)
-            value_half(step, 0)
-            if step == 0:
-                gather_scales(last_scales, LAST_EXPERT, E * C)
-            if j >= 0:
-                quantise(ht, [(j, s) for s in both])
-            if step >= 3:
-                second_layer(step - 3)
-            gate_half(step, 1)
-            if step >= 4 and step % PER_EXPERT == 0:
-                empty_sums((step - 4) * P, (step - 2) * P)
-            value_half(step, 1)
-            if step < last:
-                gate_half(step + 1, 0)
-            if step in (4, 6):
-                scatter((step - 4) // PER_EXPERT)
-        ht = turned_tile(PASSES)
-        turn(last - 1, both, ht, 0)
-        second_layer(last - 2)
-        empty_sums((last - 3) * P, (last - 1) * P)
-        halves = [turned_tile(1) for s in both]
-        turn(last, (0,), halves[0], 0)
-        quantise(ht, [(last - 1, s) for s in both])
-        turn(last, (1,), halves[1], 0)
-        second_layer(last - 1)
-        empty_sums((last - 1) * P, last * P)
+        gate_half(0, 1)
+        gate_half(1, 0)
+        value_half(0, 0)
+        value_half(0, 1)
+        gate_half(2, 0)
+        value_half(1, 0)
+        value_half(2, 0)
+        gate_half(1, 1)
+        gate_half(2, 1)
+        value_half(1, 1)
+        turn_tile(0)
+        value_half(2, 1)
+        quantise_tile(0)
+        gate_half(3, 0)
+        gate_half(3, 1)
+        value_half(3, 0)
+        turn_tile(1)
+        value_half(3, 1)
+        quantise_tile(1)
+        gate_half(4, 0)
+        gate_half(4, 1)
+        value_half(4, 0)
+        value_half(4, 1)
+        gate_half(5, 0)
+        second_layer(0, 2)
+        empty_sums(0, 2)
+        scatter(0)
+        value_half(5, 0)
+        turn_tile(2)
+        turn_tile(3)
+        gate_half(5, 1)
+        quantise_tile(2)
+        quantise_tile(3)
+        value_half(5, 1)
+        gate_half(6, 0)
+        value_half(6, 0)
+        gate_half(6, 1)
+        second_layer(2, 2)
+        value_half(6, 1)
+        empty_sums(2, 2)
+        scatter(1)
+        turn_tile(4)
+        turn_tile(5)
+        quantise_tile(4)
+        quantise_tile(5)
+        gate_half(7, 0)
+        gate_half(7, 1)
+        value_half(7, 0)
+        value_half(7, 1)
+        turn_tile(6)
+        second_layer(4, 2)
+        turned[7, 0] = turned_tile(1)
+        turn(7, (0,), turned[7, 0], 0)
+        quantise_tile(6)
+        empty_sums(4, 2)
+        turned[7, 1] = turned_tile(1)
+        turn(7, (1,), turned[7, 1], 0)
+        second_layer(6, 1)
         scatter(2)
-        for s in both:
-            quantise(halves[s], [(last, s)])
-        second_layer(last)
-        empty_sums(last * P, TILES * P)
+        quantise(turned[7, 0], [(7, 0)])
+        quantise(turned[7, 1], [(7, 1)])
+        empty_sums(6, 1)
+        second_layer(7, 1)
+        empty_sums(7, 1)
         scatter(3)
         scatter(4)
         nc.sync.dma_start(out=out, in_=window[:])

@@ -25,13 +25,12 @@ PER_EXPERT = C // P
 PER_COLUMN = 16
 ALIGN = 64
 BANK_BYTES = 4 * PASS
-BANKS = (0, 1, 2, 3, 7, 0, 3, 1, 2, 3, 0, 1, 7, 0, 1, 7, 2, 3, 1, 0, 2, 3, 7, 0, 1, 2, 7, 3, 0, 1)
-VALUE_RING = (4, 5, 6)
+BANKS = (0, 1, 2, 3, 4, 5, 6, 7, 0, 4, 1, 2, 5, 6, 3, 4, 7, 5, 0, 1, 2, 6, 4, 5, 0, 3, 1, 2, 6, 7, 0, 4, 5, 3, 7, 1, 2, 6, 4, 0, 2, 1, 2, 7)
 LAST_EXPERT = (E - 1) * C
 FIRST_GATHER = T // 8
 FIRST = 2
 W13_BYTES = 2 * 2 * H
-SCATTER_ENDS = (256, 512, 704, 864, 1024)
+SCATTER_ENDS = (256, 512, 768, 1024)
 
 
 def tile_moe_pkd_glu_sigmoid_kernel(
@@ -148,7 +147,7 @@ def tile_moe_pkd_glu_sigmoid_kernel(
             sigmoids[j, s] = sig
 
         def value_half(j, s):
-            b = bank(VALUE_RING[len(hidden) % 3] if (j, s) != (0, 0) else 7, [P, PASS], "b_%d_%d" % (j, s))
+            b = ring_bank([P, PASS], "b_%d_%d" % (j, s))
             first_product(j, s, 1, b)
             h = work.tile([P, 2, P, 2], BF16, name="h", bufs=8)
             nc.vector.tensor_tensor(
@@ -224,18 +223,18 @@ def tile_moe_pkd_glu_sigmoid_kernel(
         gate_half(0, 0)
         gate_half(0, 1)
         gate_half(1, 0)
+        gate_half(1, 1)
         value_half(0, 0)
         value_half(0, 1)
-        gate_half(2, 0)
         value_half(1, 0)
-        value_half(2, 0)
-        gate_half(1, 1)
+        gate_half(2, 0)
         gate_half(2, 1)
         value_half(1, 1)
         turn_tile(0)
+        gate_half(3, 0)
+        value_half(2, 0)
         value_half(2, 1)
         quantise_tile(0)
-        gate_half(3, 0)
         gate_half(3, 1)
         value_half(3, 0)
         turn_tile(1)
@@ -243,49 +242,42 @@ def tile_moe_pkd_glu_sigmoid_kernel(
         quantise_tile(1)
         gate_half(4, 0)
         gate_half(4, 1)
+        gate_half(5, 0)
         value_half(4, 0)
         value_half(4, 1)
-        gate_half(5, 0)
+        value_half(5, 0)
         second_layer(0, 2)
         empty_sums(0, 2)
         scatter(0)
-        value_half(5, 0)
-        turn_tile(2)
-        turn_tile(3)
         gate_half(5, 1)
-        quantise_tile(2)
-        quantise_tile(3)
+        pair = turned_tile(2 * PASSES)
+        turn(2, both, pair, 0)
+        turn(3, both, pair, PASSES)
         value_half(5, 1)
+        quantise(pair, [(j, s) for j in (2, 3) for s in both])
         gate_half(6, 0)
-        value_half(6, 0)
         gate_half(6, 1)
-        second_layer(2, 2)
+        value_half(6, 0)
         value_half(6, 1)
-        empty_sums(2, 2)
-        scatter(1)
-        turn_tile(4)
-        turn_tile(5)
-        quantise_tile(4)
-        quantise_tile(5)
+        pair = turned_tile(2 * PASSES)
+        turn(4, both, pair, 0)
+        turn(5, both, pair, PASSES)
+        quantise(pair, [(j, s) for j in (4, 5) for s in both])
         gate_half(7, 0)
         gate_half(7, 1)
         value_half(7, 0)
         value_half(7, 1)
-        turn_tile(6)
+        second_layer(2, 2)
+        empty_sums(2, 2)
+        scatter(1)
+        pair = turned_tile(2 * PASSES)
+        turn(6, both, pair, 0)
+        turn(7, both, pair, PASSES)
         second_layer(4, 2)
-        turned[7, 0] = turned_tile(1)
-        turn(7, (0,), turned[7, 0], 0)
-        quantise_tile(6)
+        quantise(pair, [(j, s) for j in (6, 7) for s in both])
         empty_sums(4, 2)
-        turned[7, 1] = turned_tile(1)
-        turn(7, (1,), turned[7, 1], 0)
-        second_layer(6, 1)
         scatter(2)
-        quantise(turned[7, 0], [(7, 0)])
-        quantise(turned[7, 1], [(7, 1)])
-        empty_sums(6, 1)
-        second_layer(7, 1)
-        empty_sums(7, 1)
+        second_layer(6, 2)
+        empty_sums(6, 2)
         scatter(3)
-        scatter(4)
         nc.sync.dma_start(out=out, in_=window[:])

@@ -25,8 +25,8 @@ PER_EXPERT = C // P
 PER_COLUMN = 16
 ALIGN = 64
 BANK_BYTES = 4 * PASS
-BANKS = (0, 1, 2, 3, 4, 5, 6, 7, 0, 4, 1, 2, 5, 6, 3, 4, 7, 5, 0, 1, 2, 6, 4, 5, 0, 3, 1, 2, 6, 7, 0, 4, 5, 3, 7, 1, 2, 6, 4, 0, 2, 1, 2, 7)
-LAST_EXPERT = (E - 1) * C
+BANKS = (0, 2, 1, 3, 4, 5, 6, 7, 0, 4, 1, 2, 5, 6, 3, 4, 7, 5, 0, 1, 2, 6, 4, 5, 0, 3, 1, 2, 6, 7, 0, 4, 5, 3, 7, 1, 2, 6, 4, 0, 2, 1, 2, 7)
+LAST_EXPERT = 512
 FIRST_GATHER = T // 8
 FIRST = 2
 W13_BYTES = 2 * 2 * H
@@ -51,7 +51,8 @@ def tile_moe_pkd_glu_sigmoid_kernel(
         ident = keep.tile([P, P], F32, name="ident")
         far_left = keep.tile([P, 8], F32, name="far_left")
         window = keep.tile([P, T], F32, name="window", align_bytes=ALIGN)
-        xw = shared.tile([P, T], I32, name="xw", align_bytes=ALIGN, offset=0)
+        xw = keep.tile([P, T], I32, name="xw", align_bytes=ALIGN)
+        first_pass = shared.tile([P, 2 * PASS], U8, name="first_pass", align_bytes=ALIGN, offset=0)
         w13 = [keep.tile([P, W13_BYTES], U8, name="w13_%d" % e, align_bytes=ALIGN) for e in range(E)]
         w2w = keep.tile([P, E * PASSES, 2 * N], U8, name="w2w", align_bytes=ALIGN)
         xs = keep.tile([P, T], U8, name="xs", align_bytes=ALIGN)
@@ -67,6 +68,11 @@ def tile_moe_pkd_glu_sigmoid_kernel(
             for m in matrices:
                 queue.dma_start(out=w13[e][:, 2 * H * m : 2 * H * (m + 1)].bitcast(I32), in_=(w1_words, w3_words)[m][e, 0].bitcast(I32))
 
+        def load_pass(m, s):
+            cols = slice(2 * PASS * s, 2 * PASS * (s + 1))
+            dst = w13[0][:, 2 * H * m : 2 * H * (m + 1)][:, cols] if s else first_pass[:]
+            nc.sync.dma_start(out=dst.bitcast(I32), in_=(w1_words, w3_words)[m][0, 0][:, cols].bitcast(I32))
+
         nc.vector.memset(xs[:].bitcast(I32), 0)
         nc.vector.memset(first_planes[0][:].bitcast(I32), 0)
         nc.vector.memset(far_left[:, 0:1], -200.0)
@@ -74,17 +80,16 @@ def tile_moe_pkd_glu_sigmoid_kernel(
             nc.vector.memset(plane[:].bitcast(I32), 0)
         nc.vector.memset(ident[:], 0.0)
         nc.sync.dma_start(offsets[:], offs)
+        load_pass(0, 0)
         load_scales(xs, x_scales, range(2), nc.sync)
         load_scales(xs, x_scales, range(2, 4), nc.scalar)
-        load_scales(first_planes[0], w1_scales[0:FIRST, 0], range(1), nc.sync)
         nc.sync.dma_start(out=xw[:], in_=x_words[0].rearrange("p t r -> p (t r)").bitcast(I32))
-        load_w13(0, nc.sync, (0,))
         make_identity(nc, ident[:], nomemset=True)
         nc.scalar.activation(out=window[:], in_=far_left[:, 0:1].to_broadcast([P, T]), func=SIGMOID)
-        load_scales(first_planes[0], w1_scales[0:FIRST, 0], range(1, 4), nc.sync)
-        load_scales(first_planes[1], w3_scales[0:FIRST, 0], range(3), nc.sync)
+        load_scales(first_planes[0], w1_scales[0:FIRST, 0], range(4), nc.sync)
+        load_pass(0, 1)
         load_w13(0, nc.sync, (1,))
-        load_scales(first_planes[1], w3_scales[0:FIRST, 0], range(3, 4), nc.sync)
+        load_scales(first_planes[1], w3_scales[0:FIRST, 0], range(4), nc.sync)
         w2_rows = w2_words.rearrange("e s p b -> p (e s) b")
         load_w13(1, nc.sync)
         nc.sync.dma_start(out=w2w[:].bitcast(I32), in_=w2_rows.bitcast(I32))
@@ -100,7 +105,7 @@ def tile_moe_pkd_glu_sigmoid_kernel(
 
         slot_words = keep.tile([P, E * C], U32, name="slot_words", align_bytes=ALIGN)
         early_scales = keep.tile([P, LAST_EXPERT], U8, name="early_scales", align_bytes=ALIGN)
-        last_scales = shared.tile([P, C], U8, name="last_scales", align_bytes=ALIGN, offset=0)
+        last_scales = shared.tile([P, E * C - LAST_EXPERT], U8, name="last_scales", align_bytes=ALIGN, offset=0)
         sigmoids = {}
         hidden = {}
         quantised = {}
@@ -129,11 +134,12 @@ def tile_moe_pkd_glu_sigmoid_kernel(
             else:
                 slot_scales = last_scales[:, lo - LAST_EXPERT : lo - LAST_EXPERT + P]
             plane = later_planes[m][:, (e - FIRST) * H : (e - FIRST + 1) * H] if e >= FIRST else first_planes[m][:, e * H : (e + 1) * H]
+            words = w13[e][:, 2 * (H * m + PASS * s) : 2 * (H * m + PASS * (s + 1))] if (e, m, s) != (0, 0, 0) else first_pass[:]
             nc.tensor.matmul_mx(
                 out=acc[:],
                 lhsT=slot_words[:, lo : lo + P].bitcast(FP8X4),
                 lhsT_scale=slot_scales,
-                rhs=w13[e][:, 2 * (H * m + PASS * s) : 2 * (H * m + PASS * (s + 1))].bitcast(FP4X4),
+                rhs=words.bitcast(FP4X4),
                 rhs_scale=plane[:, PASS * s : PASS * (s + 1)],
                 start=True,
                 stop=True,
@@ -215,14 +221,14 @@ def tile_moe_pkd_glu_sigmoid_kernel(
         def quantise_tile(j):
             quantise(turned[j], [(j, s) for s in both])
 
-        gather_scales(early_scales, 0, 768)
+        gather_scales(early_scales, 0, 512)
         gather_words(0, 160)
         gather_words(160, 384)
         gather_words(384, 1024)
-        gather_scales(last_scales, 768, 1024)
+        gather_scales(last_scales, 512, 1024)
         gate_half(0, 0)
-        gate_half(0, 1)
         gate_half(1, 0)
+        gate_half(0, 1)
         gate_half(1, 1)
         value_half(0, 0)
         value_half(0, 1)

@@ -20,17 +20,13 @@ SIGMOID = mybir.ActivationFunctionType.Sigmoid
 P = 128
 PASS = 512
 PASSES = H // PASS
-TILES = E * C // P
 PER_EXPERT = C // P
 PER_COLUMN = 16
 ALIGN = 64
 BANK_BYTES = 4 * PASS
-BANKS = (0, 2, 1, 3, 4, 5, 6, 7, 0, 4, 1, 2, 5, 6, 3, 4, 7, 5, 0, 1, 2, 6, 4, 5, 0, 3, 1, 2, 6, 7, 0, 4, 5, 3, 7, 1, 2, 6, 4, 0, 2, 1, 2, 7)
-LAST_EXPERT = 512
-FIRST_GATHER = T // 8
-FIRST = 2
-W13_BYTES = 2 * 2 * H
-SCATTER_ENDS = (256, 512, 768, 1024)
+EARLY_EXPERTS = 2
+EARLY_SLOTS = 512
+WORD_CUTS = (0, T // 8, 3 * P, E * C)
 
 
 def tile_moe_pkd_glu_sigmoid_kernel(
@@ -39,24 +35,29 @@ def tile_moe_pkd_glu_sigmoid_kernel(
     nc = tc.nc
     with ExitStack() as ctx:
         keep = ctx.enter_context(tc.tile_pool(name="keep", bufs=1))
-        shared = ctx.enter_context(tc.tile_pool(name="shared", bufs=1))
+        head_bytes = ctx.enter_context(tc.tile_pool(name="head_bytes", bufs=1))
+        tail_bytes = ctx.enter_context(tc.tile_pool(name="tail_bytes", bufs=1))
         work = ctx.enter_context(tc.tile_pool(name="work", bufs=3))
         psum = ctx.enter_context(tc.psum_pool(name="psum", bufs=1))
 
         offsets = keep.tile([P, E * C // PER_COLUMN], U16, name="offsets")
-        first_planes = [keep.tile([P, FIRST * H], U8, name="first_plane_%d" % m, align_bytes=ALIGN) for m in range(2)]
-        later_planes = [keep.tile([P, (E - FIRST) * H], U8, name="later_plane_%d" % m, align_bytes=ALIGN) for m in range(2)]
+        early_planes = [keep.tile([P, EARLY_EXPERTS * H], U8, name="early_plane_%d" % m, align_bytes=ALIGN) for m in range(2)]
+        late_planes = [keep.tile([P, (E - EARLY_EXPERTS) * H], U8, name="late_plane_%d" % m, align_bytes=ALIGN) for m in range(2)]
         w2s = keep.tile([P, E * PASSES * N], U8, name="w2s", align_bytes=ALIGN)
-        gated = keep.tile([P, E * C], F32, name="gated")
         ident = keep.tile([P, P], F32, name="ident")
         far_left = keep.tile([P, 8], F32, name="far_left")
         window = keep.tile([P, T], F32, name="window", align_bytes=ALIGN)
         xw = keep.tile([P, T], I32, name="xw", align_bytes=ALIGN)
-        first_pass = shared.tile([P, 2 * PASS], U8, name="first_pass", align_bytes=ALIGN, offset=0)
-        w13 = [keep.tile([P, W13_BYTES], U8, name="w13_%d" % e, align_bytes=ALIGN) for e in range(E)]
-        w2w = keep.tile([P, E * PASSES, 2 * N], U8, name="w2w", align_bytes=ALIGN)
         xs = keep.tile([P, T], U8, name="xs", align_bytes=ALIGN)
+        first_words = head_bytes.tile([P, 2 * PASS], U8, name="first_words", align_bytes=ALIGN, offset=0)
+        w13 = [keep.tile([P, 2 * 2 * H], U8, name="w13_%d" % e, align_bytes=ALIGN) for e in range(E)]
+        w2w = keep.tile([P, E * PASSES, 2 * N], U8, name="w2w", align_bytes=ALIGN)
         gates = keep.tile([P, E * C], F32, name="gates", align_bytes=ALIGN)
+
+        def weight_words(e, m, s):
+            if (e, m, s) == (0, 0, 0):
+                return first_words[:]
+            return w13[e][:, 2 * (H * m + PASS * s) : 2 * (H * m + PASS * (s + 1))]
 
         def load_scales(plane, scale_rows, rows, queue):
             by_row = scale_rows.rearrange("g (q r) w -> r q g w", r=4)
@@ -64,106 +65,102 @@ def tile_moe_pkd_glu_sigmoid_kernel(
                 dst = plane[r:P:32, :].bitcast(I32).rearrange("q (g w) -> q g w", g=scale_rows.shape[0])
                 queue.dma_start(out=dst, in_=by_row[r].bitcast(I32))
 
-        def load_w13(e, queue, matrices=(0, 1)):
-            for m in matrices:
-                queue.dma_start(out=w13[e][:, 2 * H * m : 2 * H * (m + 1)].bitcast(I32), in_=(w1_words, w3_words)[m][e, 0].bitcast(I32))
+        def load_matrix(e, m):
+            dst = w13[e][:, 2 * H * m : 2 * H * (m + 1)]
+            nc.sync.dma_start(out=dst.bitcast(I32), in_=(w1_words, w3_words)[m][e, 0].bitcast(I32))
 
-        def load_pass(m, s):
-            cols = slice(2 * PASS * s, 2 * PASS * (s + 1))
-            dst = w13[0][:, 2 * H * m : 2 * H * (m + 1)][:, cols] if s else first_pass[:]
-            nc.sync.dma_start(out=dst.bitcast(I32), in_=(w1_words, w3_words)[m][0, 0][:, cols].bitcast(I32))
+        def load_first_pass(s):
+            src = w1_words[0, 0][:, 2 * PASS * s : 2 * PASS * (s + 1)]
+            nc.sync.dma_start(out=weight_words(0, 0, s).bitcast(I32), in_=src.bitcast(I32))
 
         nc.vector.memset(xs[:].bitcast(I32), 0)
-        nc.vector.memset(first_planes[0][:].bitcast(I32), 0)
+        nc.vector.memset(early_planes[0][:].bitcast(I32), 0)
         nc.vector.memset(far_left[:, 0:1], -200.0)
-        for plane in first_planes[1:] + later_planes + [w2s]:
+        for plane in early_planes[1:] + late_planes + [w2s]:
             nc.vector.memset(plane[:].bitcast(I32), 0)
         nc.vector.memset(ident[:], 0.0)
         nc.sync.dma_start(offsets[:], offs)
-        load_pass(0, 0)
+        load_first_pass(0)
         load_scales(xs, x_scales, range(2), nc.sync)
         load_scales(xs, x_scales, range(2, 4), nc.scalar)
         nc.sync.dma_start(out=xw[:], in_=x_words[0].rearrange("p t r -> p (t r)").bitcast(I32))
         make_identity(nc, ident[:], nomemset=True)
         nc.scalar.activation(out=window[:], in_=far_left[:, 0:1].to_broadcast([P, T]), func=SIGMOID)
-        load_scales(first_planes[0], w1_scales[0:FIRST, 0], range(4), nc.sync)
-        load_pass(0, 1)
-        load_w13(0, nc.sync, (1,))
-        load_scales(first_planes[1], w3_scales[0:FIRST, 0], range(4), nc.sync)
-        w2_rows = w2_words.rearrange("e s p b -> p (e s) b")
-        load_w13(1, nc.sync)
-        nc.sync.dma_start(out=w2w[:].bitcast(I32), in_=w2_rows.bitcast(I32))
+        load_scales(early_planes[0], w1_scales[:EARLY_EXPERTS, 0], range(4), nc.sync)
+        load_first_pass(1)
+        load_matrix(0, 1)
+        load_scales(early_planes[1], w3_scales[:EARLY_EXPERTS, 0], range(4), nc.sync)
+        for m in range(2):
+            load_matrix(1, m)
+        nc.sync.dma_start(out=w2w[:].bitcast(I32), in_=w2_words.rearrange("e s p b -> p (e s) b").bitcast(I32))
         load_scales(w2s, w2_scales.rearrange("e s f n -> (e s) f n"), range(4), nc.sync)
-        load_scales(later_planes[0], w1_scales[FIRST:E, 0], range(4), nc.sync)
-        load_scales(later_planes[1], w3_scales[FIRST:E, 0], range(4), nc.sync)
-        load_w13(2, nc.sync)
+        load_scales(late_planes[0], w1_scales[EARLY_EXPERTS:, 0], range(4), nc.sync)
+        load_scales(late_planes[1], w3_scales[EARLY_EXPERTS:, 0], range(4), nc.sync)
+        for m in range(2):
+            load_matrix(2, m)
         nc.sync.dma_start(out=gates[:], in_=gate)
-        load_w13(3, nc.sync)
-
-        def listed(lo, hi):
-            return offsets[:, lo // PER_COLUMN : hi // PER_COLUMN]
+        for m in range(2):
+            load_matrix(3, m)
 
         slot_words = keep.tile([P, E * C], U32, name="slot_words", align_bytes=ALIGN)
-        early_scales = keep.tile([P, LAST_EXPERT], U8, name="early_scales", align_bytes=ALIGN)
-        last_scales = shared.tile([P, E * C - LAST_EXPERT], U8, name="last_scales", align_bytes=ALIGN, offset=0)
+        early_scales = keep.tile([P, EARLY_SLOTS], U8, name="early_scales", align_bytes=ALIGN)
+        late_scales = head_bytes.tile([P, E * C - EARLY_SLOTS], U8, name="late_scales", align_bytes=ALIGN, offset=0)
         sigmoids = {}
         hidden = {}
         quantised = {}
         sums = {}
-        ring = []
+        results = {}
 
-        def gather_words(lo, hi):
-            nc.vector.tensor_copy(out=slot_words[:, lo:hi], in_=xw[:].bitcast(U32).indirect(listed(lo, hi)))
-
-        def gather_scales(tile, lo, hi):
-            nc.vector.tensor_copy(out=tile[:], in_=xs[:].indirect(listed(lo, hi)))
+        def listed(lo, hi):
+            return offsets[:, lo // PER_COLUMN : hi // PER_COLUMN]
 
         def bank(number, shape, name):
             return psum.tile(shape, F32, name=name, offset=number * BANK_BYTES)
 
-        def ring_bank(shape, name):
-            n = len(ring)
-            ring.append(name)
-            return bank(BANKS[n], shape, name)
-
         def first_product(j, s, m, acc):
             e = j // PER_EXPERT
             lo = j * P
-            if lo < LAST_EXPERT:
+            if lo < EARLY_SLOTS:
                 slot_scales = early_scales[:, lo : lo + P]
             else:
-                slot_scales = last_scales[:, lo - LAST_EXPERT : lo - LAST_EXPERT + P]
-            plane = later_planes[m][:, (e - FIRST) * H : (e - FIRST + 1) * H] if e >= FIRST else first_planes[m][:, e * H : (e + 1) * H]
-            words = w13[e][:, 2 * (H * m + PASS * s) : 2 * (H * m + PASS * (s + 1))] if (e, m, s) != (0, 0, 0) else first_pass[:]
+                slot_scales = late_scales[:, lo - EARLY_SLOTS : lo - EARLY_SLOTS + P]
+            if e < EARLY_EXPERTS:
+                plane = early_planes[m][:, e * H : (e + 1) * H]
+            else:
+                plane = late_planes[m][:, (e - EARLY_EXPERTS) * H : (e - EARLY_EXPERTS + 1) * H]
             nc.tensor.matmul_mx(
                 out=acc[:],
                 lhsT=slot_words[:, lo : lo + P].bitcast(FP8X4),
                 lhsT_scale=slot_scales,
-                rhs=words.bitcast(FP4X4),
+                rhs=weight_words(e, m, s).bitcast(FP4X4),
                 rhs_scale=plane[:, PASS * s : PASS * (s + 1)],
                 start=True,
                 stop=True,
             )
 
-        def gate_half(j, s):
-            a = ring_bank([P, PASS], "a_%d_%d" % (j, s))
+        def gate_half(j, s, number):
+            a = bank(number, [P, PASS], "a_%d_%d" % (j, s))
             first_product(j, s, 0, a)
             sig = work.tile([P, 2, P, 2], F32, name="sig", bufs=6)
             nc.scalar.activation(out=sig[:], in_=a[:].rearrange("c (p u v) -> c u p v", u=2, v=2), func=SIGMOID)
             sigmoids[j, s] = sig
 
-        def value_half(j, s):
-            b = ring_bank([P, PASS], "b_%d_%d" % (j, s))
+        def value_half(j, s, number, h=None):
+            b = bank(number, [P, PASS], "b_%d_%d" % (j, s))
             first_product(j, s, 1, b)
-            h = work.tile([P, 2, P, 2], BF16, name="h", bufs=8)
+            if h is None:
+                h = work.tile([P, 2, P, 2], BF16, name="h", bufs=8)
             nc.vector.tensor_tensor(
                 out=h[:], in0=b[:].rearrange("c (p u v) -> c u p v", u=2, v=2), in1=sigmoids[j, s][:], op=MULT
             )
             hidden[j, s] = h
 
-        def turn(j, passes, ht, at):
+        def turned_tile(tiles):
+            return work.tile([P, tiles * H], BF16, name="ht", align_bytes=ALIGN)
+
+        def turn(j, passes, number, ht, at):
             n = len(passes)
-            xt = ring_bank([P, n, 2, P], "xt_%d_%d" % (j, passes[0]))
+            xt = bank(number, [P, n, 2, P], "xt_%d_%d" % (j, passes[0]))
             for k, s in enumerate(passes):
                 pairs = hidden[j, s][:].rearrange("c u p v -> c (u p v)").bitcast(F32)
                 for u in range(2):
@@ -173,23 +170,20 @@ def tile_moe_pkd_glu_sigmoid_kernel(
                 in_=xt[:].rearrange("p s u c -> p s c u"),
             )
 
-        def turned_tile(halves):
-            return work.tile([P, halves * PASS], BF16, name="ht", align_bytes=ALIGN)
-
-        def quantise(ht, halves):
-            n = len(halves)
-            codes = work.tile([P, n * P], U32, name="codes", bufs=4, align_bytes=ALIGN)
-            scales = work.tile([P, n * P], U8, name="scales", bufs=4, align_bytes=ALIGN)
+        def quantise(ht, tiles):
+            halves = [(j, s) for j in tiles for s in range(PASSES)]
+            codes = work.tile([P, len(halves) * P], U32, name="codes", bufs=4, align_bytes=ALIGN)
+            scales = work.tile([P, len(halves) * P], U8, name="scales", bufs=4, align_bytes=ALIGN)
             nc.vector.quantize_mx(out=codes[:].bitcast(FP8X4), scales=scales[:], in_=ht[:])
             for k, half in enumerate(halves):
                 quantised[half] = (codes[:, k * P : (k + 1) * P], scales[:, k * P : (k + 1) * P])
 
-        def second_layer(first, count):
-            y = ring_bank([P, count * P], "y_%d" % first)
-            for c in reversed(range(count)):
+        def second_layer(e, number):
+            y = bank(number, [P, C], "y_%d" % e)
+            for c in reversed(range(PER_EXPERT)):
                 for s in range(PASSES):
-                    codes, scales = quantised[first + c, s]
-                    g = (first + c) // PER_EXPERT * PASSES + s
+                    codes, scales = quantised[e * PER_EXPERT + c, s]
+                    g = e * PASSES + s
                     nc.tensor.matmul_mx(
                         out=y[:, c * P : (c + 1) * P],
                         lhsT=w2w[:, g, :].bitcast(FP4X4),
@@ -199,91 +193,87 @@ def tile_moe_pkd_glu_sigmoid_kernel(
                         start=(s == 0),
                         stop=(s == PASSES - 1),
                     )
-            sums[first] = y
+            sums[e] = y
 
-        def empty_sums(first, count):
-            nc.scalar.copy(out=gated[:, first * P : (first + count) * P], in_=sums[first][:])
+        def empty_sums(e, result=None):
+            if result is None:
+                result = work.tile([P, C], F32, name="result")
+            nc.scalar.copy(out=result[:], in_=sums[e][:])
+            results[e] = result
 
-        def scatter(piece):
-            lo = SCATTER_ENDS[piece - 1] if piece else 0
-            hi = SCATTER_ENDS[piece]
+        def scatter(e):
+            lo, hi = e * C, (e + 1) * C
             nc.vector.tensor_tensor(
-                out=window[:].indirect(listed(lo, hi)), in0=gated[:, lo:hi], in1=gates[:, lo:hi], op=MULT
+                out=window[:].indirect(listed(lo, hi)), in0=results[e][:], in1=gates[:, lo:hi], op=MULT
             )
 
         both = tuple(range(PASSES))
-        turned = {}
+        nc.vector.tensor_copy(out=early_scales[:], in_=xs[:].indirect(listed(0, EARLY_SLOTS)))
+        for lo, hi in zip(WORD_CUTS, WORD_CUTS[1:]):
+            nc.vector.tensor_copy(out=slot_words[:, lo:hi], in_=xw[:].bitcast(U32).indirect(listed(lo, hi)))
+        nc.vector.tensor_copy(out=late_scales[:], in_=xs[:].indirect(listed(EARLY_SLOTS, E * C)))
 
-        def turn_tile(j):
-            turned[j] = turned_tile(PASSES)
-            turn(j, both, turned[j], 0)
-
-        def quantise_tile(j):
-            quantise(turned[j], [(j, s) for s in both])
-
-        gather_scales(early_scales, 0, 512)
-        gather_words(0, 160)
-        gather_words(160, 384)
-        gather_words(384, 1024)
-        gather_scales(last_scales, 512, 1024)
-        gate_half(0, 0)
-        gate_half(1, 0)
-        gate_half(0, 1)
-        gate_half(1, 1)
-        value_half(0, 0)
-        value_half(0, 1)
-        value_half(1, 0)
-        gate_half(2, 0)
-        gate_half(2, 1)
-        value_half(1, 1)
-        turn_tile(0)
-        gate_half(3, 0)
-        value_half(2, 0)
-        value_half(2, 1)
-        quantise_tile(0)
-        gate_half(3, 1)
-        value_half(3, 0)
-        turn_tile(1)
-        value_half(3, 1)
-        quantise_tile(1)
-        gate_half(4, 0)
-        gate_half(4, 1)
-        gate_half(5, 0)
-        value_half(4, 0)
-        value_half(4, 1)
-        value_half(5, 0)
-        second_layer(0, 2)
-        empty_sums(0, 2)
+        gate_half(0, 0, 0)
+        gate_half(1, 0, 2)
+        gate_half(0, 1, 1)
+        gate_half(1, 1, 3)
+        value_half(0, 0, 4)
+        value_half(0, 1, 5)
+        value_half(1, 0, 6)
+        gate_half(2, 0, 7)
+        gate_half(2, 1, 0)
+        value_half(1, 1, 4)
+        ht = turned_tile(1)
+        turn(0, both, 1, ht, 0)
+        gate_half(3, 0, 2)
+        value_half(2, 0, 5)
+        value_half(2, 1, 6)
+        quantise(ht, (0,))
+        gate_half(3, 1, 3)
+        value_half(3, 0, 4)
+        ht = turned_tile(1)
+        turn(1, both, 7, ht, 0)
+        value_half(3, 1, 5)
+        quantise(ht, (1,))
+        gate_half(4, 0, 0)
+        gate_half(4, 1, 1)
+        gate_half(5, 0, 2)
+        value_half(4, 0, 6)
+        value_half(4, 1, 4)
+        value_half(5, 0, 5)
+        second_layer(0, 0)
+        empty_sums(0)
         scatter(0)
-        gate_half(5, 1)
-        pair = turned_tile(2 * PASSES)
-        turn(2, both, pair, 0)
-        turn(3, both, pair, PASSES)
-        value_half(5, 1)
-        quantise(pair, [(j, s) for j in (2, 3) for s in both])
-        gate_half(6, 0)
-        gate_half(6, 1)
-        value_half(6, 0)
-        value_half(6, 1)
-        pair = turned_tile(2 * PASSES)
-        turn(4, both, pair, 0)
-        turn(5, both, pair, PASSES)
-        quantise(pair, [(j, s) for j in (4, 5) for s in both])
-        gate_half(7, 0)
-        gate_half(7, 1)
-        value_half(7, 0)
-        value_half(7, 1)
-        second_layer(2, 2)
-        empty_sums(2, 2)
+        gate_half(5, 1, 3)
+        ht = turned_tile(2)
+        turn(2, both, 1, ht, 0)
+        turn(3, both, 2, ht, PASSES)
+        value_half(5, 1, 6)
+        quantise(ht, (2, 3))
+        gate_half(6, 0, 7)
+        gate_half(6, 1, 0)
+        value_half(6, 0, 4)
+        value_half(6, 1, 5)
+        ht = turned_tile(2)
+        turn(4, both, 3, ht, 0)
+        turn(5, both, 7, ht, PASSES)
+        quantise(ht, (4, 5))
+        gate_half(7, 0, 1)
+        gate_half(7, 1, 2)
+        value_half(7, 0, 6)
+        value_half(7, 1, 4, tail_bytes.tile([P, 2, P, 2], BF16, name="last_h", offset=0))
+        second_layer(1, 0)
+        empty_sums(1)
         scatter(1)
-        pair = turned_tile(2 * PASSES)
-        turn(6, both, pair, 0)
-        turn(7, both, pair, PASSES)
-        second_layer(4, 2)
-        quantise(pair, [(j, s) for j in (6, 7) for s in both])
-        empty_sums(4, 2)
+        ht = turned_tile(2)
+        turn(6, both, 1, ht, 0)
+        second_layer(2, 7)
+        turn(7, (0,), 3, ht, PASSES)
+        turn(7, (1,), 2, ht, PASSES + 1)
+        quantise(ht, (6, 7))
+        empty_sums(2, tail_bytes.tile([P, C], F32, name="third_result", offset=0))
         scatter(2)
-        second_layer(6, 2)
-        empty_sums(6, 2)
+        second_layer(3, 0)
+        empty_sums(3)
         scatter(3)
         nc.sync.dma_start(out=out, in_=window[:])

@@ -16,6 +16,7 @@ FP8X4 = mybir.dt.float8_e4m3fn_x4
 FP4X4 = mybir.dt.float4_e2m1fn_x4
 MULT = mybir.AluOpType.mult
 SIGMOID = mybir.ActivationFunctionType.Sigmoid
+COPY = mybir.ActivationFunctionType.Copy
 
 P = 128
 PASS = 512
@@ -36,7 +37,6 @@ def tile_moe_pkd_glu_sigmoid_kernel(
     with ExitStack() as ctx:
         keep = ctx.enter_context(tc.tile_pool(name="keep", bufs=1))
         head_bytes = ctx.enter_context(tc.tile_pool(name="head_bytes", bufs=1))
-        tail_bytes = ctx.enter_context(tc.tile_pool(name="tail_bytes", bufs=1))
         work = ctx.enter_context(tc.tile_pool(name="work", bufs=3))
         psum = ctx.enter_context(tc.psum_pool(name="psum", bufs=1))
 
@@ -92,13 +92,14 @@ def tile_moe_pkd_glu_sigmoid_kernel(
         load_scales(early_planes[1], w3_scales[:EARLY_EXPERTS, 0], range(4), nc.sync)
         for m in range(2):
             load_matrix(1, m)
-        nc.sync.dma_start(out=w2w[:].bitcast(I32), in_=w2_words.rearrange("e s p b -> p (e s) b").bitcast(I32))
-        load_scales(w2s, w2_scales.rearrange("e s f n -> (e s) f n"), range(4), nc.sync)
         load_scales(late_planes[0], w1_scales[EARLY_EXPERTS:, 0], range(4), nc.sync)
         load_scales(late_planes[1], w3_scales[EARLY_EXPERTS:, 0], range(4), nc.sync)
+        nc.sync.dma_start(out=w2w[:].bitcast(I32), in_=w2_words.rearrange("e s p b -> p (e s) b").bitcast(I32))
+        load_scales(w2s, w2_scales.rearrange("e s f n -> (e s) f n"), range(4), nc.sync)
+        nc.sync.dma_start(out=gates[:, :C], in_=gate[:, :C])
         for m in range(2):
             load_matrix(2, m)
-        nc.sync.dma_start(out=gates[:], in_=gate)
+        nc.sync.dma_start(out=gates[:, C:], in_=gate[:, C:])
         for m in range(2):
             load_matrix(3, m)
 
@@ -106,10 +107,12 @@ def tile_moe_pkd_glu_sigmoid_kernel(
         early_scales = keep.tile([P, EARLY_SLOTS], U8, name="early_scales", align_bytes=ALIGN)
         late_scales = head_bytes.tile([P, E * C - EARLY_SLOTS], U8, name="late_scales", align_bytes=ALIGN, offset=0)
         sigmoids = {}
+        values = {}
         hidden = {}
         quantised = {}
         sums = {}
-        results = {}
+        turned = {}
+        results = keep.tile([P, E * C], F32, name="results", align_bytes=ALIGN)
 
         def listed(lo, hi):
             return offsets[:, lo // PER_COLUMN : hi // PER_COLUMN]
@@ -145,135 +148,147 @@ def tile_moe_pkd_glu_sigmoid_kernel(
             nc.scalar.activation(out=sig[:], in_=a[:].rearrange("c (p u v) -> c u p v", u=2, v=2), func=SIGMOID)
             sigmoids[j, s] = sig
 
-        def value_half(j, s, number, h=None):
+        def value_product(j, s, number):
             b = bank(number, [P, PASS], "b_%d_%d" % (j, s))
             first_product(j, s, 1, b)
-            if h is None:
-                h = work.tile([P, 2, P, 2], BF16, name="h", bufs=8)
+            values[j, s] = b
+
+        def multiply(j, s):
+            h = work.tile([P, 2, P, 2], BF16, name="h", bufs=8)
+            b = values[j, s]
             nc.vector.tensor_tensor(
                 out=h[:], in0=b[:].rearrange("c (p u v) -> c u p v", u=2, v=2), in1=sigmoids[j, s][:], op=MULT
             )
             hidden[j, s] = h
 
-        def turned_tile(tiles):
-            return work.tile([P, tiles * H], BF16, name="ht", align_bytes=ALIGN)
+        def value_half(j, s, number):
+            value_product(j, s, number)
+            multiply(j, s)
 
-        def turn(j, passes, number, ht, at):
+        def turned_tile(tiles):
+            ht = work.tile([P, len(tiles) * H], BF16, name="ht", align_bytes=ALIGN)
+            for j in tiles:
+                turned[j] = (ht, tiles)
+
+        def turn(j, passes, number, copy):
+            ht, tiles = turned[j]
+            k = tiles.index(j)
             n = len(passes)
             xt = bank(number, [P, n, 2, P], "xt_%d_%d" % (j, passes[0]))
-            for k, s in enumerate(passes):
+            for at, s in enumerate(passes):
                 pairs = hidden[j, s][:].rearrange("c u p v -> c (u p v)").bitcast(F32)
                 for u in range(2):
-                    nc.tensor.transpose(xt[:, k, u, :], pairs[:, u * P : (u + 1) * P], ident[:])
-            nc.scalar.copy(
-                out=ht[:, at * PASS : (at + n) * PASS].bitcast(F32).rearrange("p (s c u) -> p s c u", s=n, u=2),
+                    nc.tensor.transpose(xt[:, at, u, :], pairs[:, u * P : (u + 1) * P], ident[:])
+            words = ht[:].bitcast(F32).rearrange("p (s c u) -> p s c u", s=PASSES, u=2)
+            copy(
+                out=words[:, passes[0] : passes[0] + n, k * P : (k + 1) * P, :],
                 in_=xt[:].rearrange("p s u c -> p s c u"),
             )
 
-        def quantise(ht, tiles):
-            halves = [(j, s) for j in tiles for s in range(PASSES)]
-            codes = work.tile([P, len(halves) * P], U32, name="codes", bufs=4, align_bytes=ALIGN)
-            scales = work.tile([P, len(halves) * P], U8, name="scales", bufs=4, align_bytes=ALIGN)
+        def quantise(j):
+            ht, tiles = turned[j]
+            width = PASSES * len(tiles) * P
+            codes = work.tile([P, width], U32, name="codes", bufs=4, align_bytes=ALIGN)
+            scales = work.tile([P, width], U8, name="scales", bufs=4, align_bytes=ALIGN)
             nc.vector.quantize_mx(out=codes[:].bitcast(FP8X4), scales=scales[:], in_=ht[:])
-            for k, half in enumerate(halves):
-                quantised[half] = (codes[:, k * P : (k + 1) * P], scales[:, k * P : (k + 1) * P])
+            quantised[j] = (codes, scales)
 
-        def second_layer(e, number):
-            y = bank(number, [P, C], "y_%d" % e)
-            for c in reversed(range(PER_EXPERT)):
-                for s in range(PASSES):
-                    codes, scales = quantised[e * PER_EXPERT + c, s]
-                    g = e * PASSES + s
-                    nc.tensor.matmul_mx(
-                        out=y[:, c * P : (c + 1) * P],
-                        lhsT=w2w[:, g, :].bitcast(FP4X4),
-                        lhsT_scale=w2s[:, g * N : (g + 1) * N],
-                        rhs=codes.bitcast(FP8X4),
-                        rhs_scale=scales,
-                        start=(s == 0),
-                        stop=(s == PASSES - 1),
-                    )
-            sums[e] = y
+        def second_layer(j, number):
+            slots = len(turned[j][1]) * P
+            y = bank(number, [P, slots], "y_%d" % j)
+            codes, scales = quantised[j]
+            for s in range(PASSES):
+                g = j // PER_EXPERT * PASSES + s
+                nc.tensor.matmul_mx(
+                    out=y[:],
+                    lhsT=w2w[:, g, :].bitcast(FP4X4),
+                    lhsT_scale=w2s[:, g * N : (g + 1) * N],
+                    rhs=codes[:, s * slots : (s + 1) * slots].bitcast(FP8X4),
+                    rhs_scale=scales[:, s * slots : (s + 1) * slots],
+                    start=(s == 0),
+                    stop=(s == PASSES - 1),
+                )
+            sums[j] = y
 
-        def empty_sums(e, result=None):
-            if result is None:
-                result = work.tile([P, C], F32, name="result")
-            nc.scalar.copy(out=result[:], in_=sums[e][:])
-            results[e] = result
+        def weigh(j):
+            lo, hi = j * P, (j + len(turned[j][1])) * P
+            nc.vector.tensor_tensor(out=results[:, lo:hi], in0=sums[j][:], in1=gates[:, lo:hi], op=MULT)
 
-        def scatter(e):
-            lo, hi = e * C, (e + 1) * C
-            nc.vector.tensor_tensor(
-                out=window[:].indirect(listed(lo, hi)), in0=results[e][:], in1=gates[:, lo:hi], op=MULT
-            )
+        def scatter(lo, hi):
+            nc.scalar.activation(out=window[:].indirect(listed(lo, hi)), in_=results[:, lo:hi], func=COPY)
 
         both = tuple(range(PASSES))
+        on_scalar, on_vector = nc.scalar.copy, nc.vector.tensor_copy
         nc.vector.tensor_copy(out=early_scales[:], in_=xs[:].indirect(listed(0, EARLY_SLOTS)))
         for lo, hi in zip(WORD_CUTS, WORD_CUTS[1:]):
             nc.vector.tensor_copy(out=slot_words[:, lo:hi], in_=xw[:].bitcast(U32).indirect(listed(lo, hi)))
         nc.vector.tensor_copy(out=late_scales[:], in_=xs[:].indirect(listed(EARLY_SLOTS, E * C)))
 
         gate_half(0, 0, 0)
-        gate_half(1, 0, 2)
-        gate_half(0, 1, 1)
+        gate_half(1, 0, 1)
+        gate_half(0, 1, 2)
         gate_half(1, 1, 3)
         value_half(0, 0, 4)
         value_half(0, 1, 5)
+        gate_half(2, 0, 0)
         value_half(1, 0, 6)
-        gate_half(2, 0, 7)
-        gate_half(2, 1, 0)
-        value_half(1, 1, 4)
-        ht = turned_tile(1)
-        turn(0, both, 1, ht, 0)
+        gate_half(2, 1, 1)
+        value_half(1, 1, 7)
         gate_half(3, 0, 2)
-        value_half(2, 0, 5)
-        value_half(2, 1, 6)
-        quantise(ht, (0,))
+        value_half(2, 0, 4)
         gate_half(3, 1, 3)
-        value_half(3, 0, 4)
-        ht = turned_tile(1)
-        turn(1, both, 7, ht, 0)
-        value_half(3, 1, 5)
-        quantise(ht, (1,))
+        value_half(2, 1, 5)
+        turned_tile((0, 1))
+        turn(0, both, 1, on_vector)
+        turn(1, both, 2, on_scalar)
+        value_half(3, 0, 6)
+        quantise(0)
+        value_half(3, 1, 7)
         gate_half(4, 0, 0)
-        gate_half(4, 1, 1)
-        gate_half(5, 0, 2)
-        value_half(4, 0, 6)
-        value_half(4, 1, 4)
-        value_half(5, 0, 5)
+        gate_half(4, 1, 3)
+        gate_half(5, 0, 4)
+        value_half(4, 0, 5)
+        gate_half(5, 1, 1)
         second_layer(0, 0)
-        empty_sums(0)
-        scatter(0)
-        gate_half(5, 1, 3)
-        ht = turned_tile(2)
-        turn(2, both, 1, ht, 0)
-        turn(3, both, 2, ht, PASSES)
-        value_half(5, 1, 6)
-        quantise(ht, (2, 3))
-        gate_half(6, 0, 7)
+        weigh(0)
+        value_half(4, 1, 2)
+        scatter(0, 256)
+        turned_tile((2, 3))
+        turn(2, both, 3, on_vector)
+        turn(3, both, 4, on_vector)
+        value_half(5, 0, 6)
+        value_half(5, 1, 7)
+        quantise(2)
+        gate_half(6, 0, 1)
+        value_half(6, 0, 5)
         gate_half(6, 1, 0)
-        value_half(6, 0, 4)
-        value_half(6, 1, 5)
-        ht = turned_tile(2)
-        turn(4, both, 3, ht, 0)
-        turn(5, both, 7, ht, PASSES)
-        quantise(ht, (4, 5))
-        gate_half(7, 0, 1)
-        gate_half(7, 1, 2)
-        value_half(7, 0, 6)
-        value_half(7, 1, 4, tail_bytes.tile([P, 2, P, 2], BF16, name="last_h", offset=0))
-        second_layer(1, 0)
-        empty_sums(1)
-        scatter(1)
-        ht = turned_tile(2)
-        turn(6, both, 1, ht, 0)
-        second_layer(2, 7)
-        turn(7, (0,), 3, ht, PASSES)
-        turn(7, (1,), 2, ht, PASSES + 1)
-        quantise(ht, (6, 7))
-        empty_sums(2, tail_bytes.tile([P, C], F32, name="third_result", offset=0))
-        scatter(2)
-        second_layer(3, 0)
-        empty_sums(3)
-        scatter(3)
+        turned_tile((4, 5))
+        turn(4, both, 2, on_scalar)
+        turn(5, both, 3, on_scalar)
+        value_half(6, 1, 7)
+        second_layer(2, 1)
+        gate_half(7, 0, 0)
+        quantise(4)
+        weigh(2)
+        value_half(7, 0, 2)
+        gate_half(7, 1, 3)
+        scatter(256, 512)
+        turned_tile((6,))
+        turn(6, both, 5, on_vector)
+        value_product(7, 1, 7)
+        second_layer(4, 1)
+        weigh(4)
+        multiply(7, 1)
+        scatter(512, 704)
+        turned_tile((7,))
+        quantise(6)
+        turn(7, (0,), 2, on_vector)
+        turn(7, (1,), 7, on_vector)
+        second_layer(6, 5)
+        weigh(6)
+        quantise(7)
+        scatter(704, 864)
+        second_layer(7, 2)
+        weigh(7)
+        scatter(864, 1024)
         nc.sync.dma_start(out=out, in_=window[:])

@@ -15,6 +15,7 @@ U8 = mybir.dt.uint8
 FP8X4 = mybir.dt.float8_e4m3fn_x4
 FP4X4 = mybir.dt.float4_e2m1fn_x4
 MULT = mybir.AluOpType.mult
+ADD = mybir.AluOpType.add
 SIGMOID = mybir.ActivationFunctionType.Sigmoid
 COPY = mybir.ActivationFunctionType.Copy
 
@@ -46,6 +47,7 @@ def tile_moe_pkd_glu_sigmoid_kernel(
         w2s = keep.tile([P, E * PASSES * N], U8, name="w2s", align_bytes=ALIGN)
         ident = keep.tile([P, P], F32, name="ident")
         far_left = keep.tile([P, 8], F32, name="far_left")
+        zeros = keep.tile([P, P], F32, name="zeros", align_bytes=ALIGN)
         window = keep.tile([P, T], F32, name="window", align_bytes=ALIGN)
         xw = keep.tile([P, T], I32, name="xw", align_bytes=ALIGN)
         xs = keep.tile([P, T], U8, name="xs", align_bytes=ALIGN)
@@ -79,6 +81,7 @@ def tile_moe_pkd_glu_sigmoid_kernel(
         for plane in early_planes[1:] + late_planes + [w2s]:
             nc.vector.memset(plane[:].bitcast(I32), 0)
         nc.vector.memset(ident[:], 0.0)
+        nc.vector.memset(zeros[:], 0.0)
         nc.sync.dma_start(offsets[:], offs)
         load_first_pass(0)
         load_scales(xs, x_scales, range(2), nc.sync)
@@ -112,6 +115,7 @@ def tile_moe_pkd_glu_sigmoid_kernel(
         quantised = {}
         sums = {}
         turned = {}
+        crossed = {}
         results = keep.tile([P, E * C], F32, name="results", align_bytes=ALIGN)
 
         def listed(lo, hi):
@@ -170,28 +174,33 @@ def tile_moe_pkd_glu_sigmoid_kernel(
             for j in tiles:
                 turned[j] = (ht, tiles)
 
-        def turn(j, passes, number, copy):
-            ht, tiles = turned[j]
-            k = tiles.index(j)
-            n = len(passes)
-            xt = bank(number, [P, n, 2, P], "xt_%d_%d" % (j, passes[0]))
+        def turn(j, passes, number):
+            xt = bank(number, [P, len(passes), 2, P], "xt_%d_%d" % (j, passes[0]))
             for at, s in enumerate(passes):
                 pairs = hidden[j, s][:].rearrange("c u p v -> c (u p v)").bitcast(F32)
                 for u in range(2):
                     nc.tensor.transpose(xt[:, at, u, :], pairs[:, u * P : (u + 1) * P], ident[:])
+            crossed[j, passes] = xt
+
+        def weave(j, passes, copy):
+            ht, tiles = turned[j]
+            k = tiles.index(j)
             words = ht[:].bitcast(F32).rearrange("p (s c u) -> p s c u", s=PASSES, u=2)
             copy(
-                out=words[:, passes[0] : passes[0] + n, k * P : (k + 1) * P, :],
-                in_=xt[:].rearrange("p s u c -> p s c u"),
+                out=words[:, passes[0] : passes[-1] + 1, k * P : (k + 1) * P, :],
+                in_=crossed[j, passes][:].rearrange("p s u c -> p s c u"),
             )
 
-        def quantise(j):
+        def quantise(j, passes):
             ht, tiles = turned[j]
-            width = PASSES * len(tiles) * P
-            codes = work.tile([P, width], U32, name="codes", bufs=4, align_bytes=ALIGN)
-            scales = work.tile([P, width], U8, name="scales", bufs=4, align_bytes=ALIGN)
-            nc.vector.quantize_mx(out=codes[:].bitcast(FP8X4), scales=scales[:], in_=ht[:])
-            quantised[j] = (codes, scales)
+            slots = len(tiles) * P
+            if passes[0] == 0:
+                codes = work.tile([P, PASSES * slots], U32, name="codes", bufs=4, align_bytes=ALIGN)
+                scales = work.tile([P, PASSES * slots], U8, name="scales", bufs=4, align_bytes=ALIGN)
+                quantised[j] = (codes, scales)
+            codes, scales = quantised[j]
+            lo, hi = passes[0] * slots, (passes[-1] + 1) * slots
+            nc.vector.quantize_mx(out=codes[:, lo:hi].bitcast(FP8X4), scales=scales[:, lo:hi], in_=ht[:, 4 * lo : 4 * hi])
 
         def second_layer(j, number):
             slots = len(turned[j][1]) * P
@@ -217,6 +226,11 @@ def tile_moe_pkd_glu_sigmoid_kernel(
         def scatter(lo, hi):
             nc.scalar.activation(out=window[:].indirect(listed(lo, hi)), in_=results[:, lo:hi], func=COPY)
 
+        def scatter_last(lo, hi):
+            nc.vector.tensor_tensor(
+                out=window[:].indirect(listed(lo, hi)), in0=results[:, lo:hi], in1=zeros[:, : hi - lo], op=ADD
+            )
+
         both = tuple(range(PASSES))
         on_scalar, on_vector = nc.scalar.copy, nc.vector.tensor_copy
         nc.vector.tensor_copy(out=early_scales[:], in_=xs[:].indirect(listed(0, EARLY_SLOTS)))
@@ -239,10 +253,12 @@ def tile_moe_pkd_glu_sigmoid_kernel(
         gate_half(3, 1, 3)
         value_half(2, 1, 5)
         turned_tile((0, 1))
-        turn(0, both, 1, on_vector)
-        turn(1, both, 2, on_scalar)
+        turn(0, both, 1)
+        weave(0, both, on_vector)
+        turn(1, both, 2)
+        weave(1, both, on_scalar)
         value_half(3, 0, 6)
-        quantise(0)
+        quantise(0, both)
         value_half(3, 1, 7)
         gate_half(4, 0, 0)
         gate_half(4, 1, 3)
@@ -254,41 +270,49 @@ def tile_moe_pkd_glu_sigmoid_kernel(
         value_half(4, 1, 2)
         scatter(0, 256)
         turned_tile((2, 3))
-        turn(2, both, 3, on_vector)
-        turn(3, both, 4, on_vector)
+        turn(2, both, 3)
+        weave(2, both, on_vector)
+        turn(3, both, 4)
+        weave(3, both, on_vector)
         value_half(5, 0, 6)
         value_half(5, 1, 7)
-        quantise(2)
+        quantise(2, both)
         gate_half(6, 0, 1)
         value_half(6, 0, 5)
         gate_half(6, 1, 0)
         turned_tile((4, 5))
-        turn(4, both, 2, on_scalar)
-        turn(5, both, 3, on_scalar)
+        gate_half(7, 0, 4)
+        turn(4, both, 2)
+        weave(4, both, on_scalar)
+        turn(5, both, 3)
+        weave(5, both, on_scalar)
         value_half(6, 1, 7)
         second_layer(2, 1)
-        gate_half(7, 0, 0)
-        quantise(4)
+        gate_half(7, 1, 0)
         weigh(2)
+        quantise(4, both)
         value_half(7, 0, 2)
-        gate_half(7, 1, 3)
         scatter(256, 512)
         turned_tile((6,))
-        turn(6, both, 5, on_vector)
+        turn(6, both, 5)
+        weave(6, both, on_vector)
         value_product(7, 1, 7)
         second_layer(4, 1)
+        turned_tile((7,))
+        turn(7, (0,), 2)
+        weave(7, (0,), on_scalar)
         weigh(4)
         multiply(7, 1)
-        scatter(512, 704)
-        turned_tile((7,))
-        quantise(6)
-        turn(7, (0,), 2, on_vector)
-        turn(7, (1,), 7, on_vector)
+        scatter(512, 768)
+        quantise(6, both)
+        quantise(7, (0,))
+        turn(7, (1,), 7)
+        weave(7, (1,), on_vector)
         second_layer(6, 5)
         weigh(6)
-        quantise(7)
-        scatter(704, 864)
+        quantise(7, (1,))
         second_layer(7, 2)
+        scatter_last(768, 896)
         weigh(7)
-        scatter(864, 1024)
+        scatter_last(896, 1024)
         nc.sync.dma_start(out=out, in_=window[:])

@@ -99,12 +99,12 @@ def tile_moe_pkd_glu_sigmoid_kernel(
         load_scales(late_planes[1], w3_scales[EARLY_EXPERTS:, 0], range(4), nc.sync)
         nc.sync.dma_start(out=w2w[:].bitcast(I32), in_=w2_words.rearrange("e s p b -> p (e s) b").bitcast(I32))
         load_scales(w2s, w2_scales.rearrange("e s f n -> (e s) f n"), range(4), nc.sync)
-        nc.sync.dma_start(out=gates[:, :C], in_=gate[:, :C])
         for m in range(2):
             load_matrix(2, m)
-        nc.sync.dma_start(out=gates[:, C:], in_=gate[:, C:])
+        nc.sync.dma_start(out=gates[:, :C], in_=gate[:, :C])
         for m in range(2):
             load_matrix(3, m)
+        nc.sync.dma_start(out=gates[:, C:], in_=gate[:, C:])
 
         slot_words = keep.tile([P, E * C], U32, name="slot_words", align_bytes=ALIGN)
         early_scales = keep.tile([P, EARLY_SLOTS], U8, name="early_scales", align_bytes=ALIGN)

@@ -97,13 +97,18 @@ def tile_moe_pkd_glu_sigmoid_kernel(
             load_matrix(1, m)
         load_scales(late_planes[0], w1_scales[EARLY_EXPERTS:, 0], range(4), nc.sync)
         load_scales(late_planes[1], w3_scales[EARLY_EXPERTS:, 0], range(4), nc.sync)
-        nc.sync.dma_start(out=w2w[:].bitcast(I32), in_=w2_words.rearrange("e s p b -> p (e s) b").bitcast(I32))
+        nc.sync.dma_start(
+            out=w2w[:, :PASSES, :].bitcast(I32), in_=w2_words[0].rearrange("s p b -> p s b").bitcast(I32)
+        )
         load_scales(w2s, w2_scales.rearrange("e s f n -> (e s) f n"), range(4), nc.sync)
         for m in range(2):
             load_matrix(2, m)
         nc.sync.dma_start(out=gates[:, :C], in_=gate[:, :C])
         for m in range(2):
             load_matrix(3, m)
+        nc.sync.dma_start(
+            out=w2w[:, PASSES:, :].bitcast(I32), in_=w2_words[1:].rearrange("e s p b -> p (e s) b").bitcast(I32)
+        )
         nc.sync.dma_start(out=gates[:, C:], in_=gate[:, C:])
 
         slot_words = keep.tile([P, E * C], U32, name="slot_words", align_bytes=ALIGN)

@@ -231,6 +231,19 @@ def tile_moe_pkd_glu_sigmoid_kernel(
         def scatter(lo, hi):
             nc.scalar.activation(out=window[:].indirect(listed(lo, hi)), in_=results[:, lo:hi], func=COPY)
 
+        def keep_clock(number):
+            codes, scales = quantised[2]
+            idle = bank(number, [P, PASS], "idle_%d" % number)
+            nc.tensor.matmul_mx(
+                out=idle[:],
+                lhsT=w2w[:, PASSES, :].bitcast(FP4X4),
+                lhsT_scale=w2s[:, PASSES * N : (PASSES + 1) * N],
+                rhs=codes[:].bitcast(FP8X4),
+                rhs_scale=scales[:],
+                start=True,
+                stop=True,
+            )
+
         def scatter_last(lo, hi):
             nc.vector.tensor_tensor(
                 out=window[:].indirect(listed(lo, hi)), in0=results[:, lo:hi], in1=zeros[:, : hi - lo], op=ADD
@@ -307,6 +320,8 @@ def tile_moe_pkd_glu_sigmoid_kernel(
         turn(7, (0,), 2)
         weave(7, (0,), on_scalar)
         weigh(4)
+        keep_clock(5)
+        keep_clock(1)
         multiply(7, 1)
         scatter(512, 768)
         quantise(6, both)
@@ -314,6 +329,7 @@ def tile_moe_pkd_glu_sigmoid_kernel(
         turn(7, (1,), 7)
         weave(7, (1,), on_vector)
         second_layer(6, 5)
+        keep_clock(7)
         weigh(6)
         quantise(7, (1,))
         second_layer(7, 2)

@@ -25,10 +25,14 @@ PASSES = H // PASS
 PER_EXPERT = C // P
 PER_COLUMN = 16
 ALIGN = 64
+BANKS = 8
 BANK_BYTES = 4 * PASS
 EARLY_EXPERTS = 2
-EARLY_SLOTS = 512
+EARLY_SLOTS = EARLY_EXPERTS * C
 WORD_CUTS = (0, T // 8, 3 * P, E * C)
+SIGMOID_BUFFERS = 6
+HIDDEN_BUFFERS = 8
+QUANTISED_BUFFERS = 4
 
 
 def tile_moe_pkd_glu_sigmoid_kernel(
@@ -71,7 +75,7 @@ def tile_moe_pkd_glu_sigmoid_kernel(
             dst = w13[e][:, 2 * H * m : 2 * H * (m + 1)]
             nc.sync.dma_start(out=dst.bitcast(I32), in_=(w1_words, w3_words)[m][e, 0].bitcast(I32))
 
-        def load_first_pass(s):
+        def load_first_matrix(s):
             src = w1_words[0, 0][:, 2 * PASS * s : 2 * PASS * (s + 1)]
             nc.sync.dma_start(out=weight_words(0, 0, s).bitcast(I32), in_=src.bitcast(I32))
 
@@ -83,26 +87,26 @@ def tile_moe_pkd_glu_sigmoid_kernel(
         nc.vector.memset(ident[:], 0.0)
         nc.vector.memset(zeros[:], 0.0)
         nc.sync.dma_start(offsets[:], offs)
-        load_first_pass(0)
+        load_first_matrix(0)
         load_scales(xs, x_scales, range(2), nc.sync)
         load_scales(xs, x_scales, range(2, 4), nc.scalar)
         nc.sync.dma_start(out=xw[:], in_=x_words[0].rearrange("p t r -> p (t r)").bitcast(I32))
         make_identity(nc, ident[:], nomemset=True)
         nc.scalar.activation(out=window[:], in_=far_left[:, 0:1].to_broadcast([P, T]), func=SIGMOID)
         load_scales(early_planes[0], w1_scales[:EARLY_EXPERTS, 0], range(4), nc.sync)
-        load_first_pass(1)
+        load_first_matrix(1)
         load_matrix(0, 1)
         load_scales(early_planes[1], w3_scales[:EARLY_EXPERTS, 0], range(4), nc.sync)
         for m in range(2):
             load_matrix(1, m)
-        load_scales(late_planes[0], w1_scales[EARLY_EXPERTS:, 0], range(4), nc.sync)
+        load_scales(w2s, w2_scales.rearrange("e s f n -> (e s) f n"), range(4), nc.sync)
         load_scales(late_planes[1], w3_scales[EARLY_EXPERTS:, 0], range(4), nc.sync)
+        load_matrix(2, 0)
         nc.sync.dma_start(
             out=w2w[:, :PASSES, :].bitcast(I32), in_=w2_words[0].rearrange("s p b -> p s b").bitcast(I32)
         )
-        load_scales(w2s, w2_scales.rearrange("e s f n -> (e s) f n"), range(4), nc.sync)
-        for m in range(2):
-            load_matrix(2, m)
+        load_scales(late_planes[0], w1_scales[EARLY_EXPERTS:, 0], range(4), nc.sync)
+        load_matrix(2, 1)
         nc.sync.dma_start(out=gates[:, :C], in_=gate[:, :C])
         for m in range(2):
             load_matrix(3, m)
@@ -114,31 +118,34 @@ def tile_moe_pkd_glu_sigmoid_kernel(
         slot_words = keep.tile([P, E * C], U32, name="slot_words", align_bytes=ALIGN)
         early_scales = keep.tile([P, EARLY_SLOTS], U8, name="early_scales", align_bytes=ALIGN)
         late_scales = head_bytes.tile([P, E * C - EARLY_SLOTS], U8, name="late_scales", align_bytes=ALIGN, offset=0)
+        results = keep.tile([P, E * C], F32, name="results", align_bytes=ALIGN)
         sigmoids = {}
         values = {}
         hidden = {}
+        turned = {}
         quantised = {}
         sums = {}
-        turned = {}
-        crossed = {}
-        results = keep.tile([P, E * C], F32, name="results", align_bytes=ALIGN)
+        oldest_first = list(range(BANKS))
+        bank_of = {}
+
+        def bank(name, shape, behind):
+            number = oldest_first[0] if behind is None else bank_of[behind]
+            oldest_first.remove(number)
+            oldest_first.append(number)
+            bank_of[name] = number
+            return psum.tile(shape, F32, name=name, offset=number * BANK_BYTES)
 
         def listed(lo, hi):
             return offsets[:, lo // PER_COLUMN : hi // PER_COLUMN]
 
-        def bank(number, shape, name):
-            return psum.tile(shape, F32, name=name, offset=number * BANK_BYTES)
-
         def first_product(j, s, m, acc):
             e = j // PER_EXPERT
             lo = j * P
-            if lo < EARLY_SLOTS:
-                slot_scales = early_scales[:, lo : lo + P]
-            else:
-                slot_scales = late_scales[:, lo - EARLY_SLOTS : lo - EARLY_SLOTS + P]
             if e < EARLY_EXPERTS:
+                slot_scales = early_scales[:, lo : lo + P]
                 plane = early_planes[m][:, e * H : (e + 1) * H]
             else:
+                slot_scales = late_scales[:, lo - EARLY_SLOTS : lo - EARLY_SLOTS + P]
                 plane = late_planes[m][:, (e - EARLY_EXPERTS) * H : (e - EARLY_EXPERTS + 1) * H]
             nc.tensor.matmul_mx(
                 out=acc[:],
@@ -150,28 +157,28 @@ def tile_moe_pkd_glu_sigmoid_kernel(
                 stop=True,
             )
 
-        def gate_half(j, s, number):
-            a = bank(number, [P, PASS], "a_%d_%d" % (j, s))
+        def gate_half(j, s, behind=None):
+            a = bank("a_%d_%d" % (j, s), [P, PASS], behind)
             first_product(j, s, 0, a)
-            sig = work.tile([P, 2, P, 2], F32, name="sig", bufs=6)
+            sig = work.tile([P, 2, P, 2], F32, name="sig", bufs=SIGMOID_BUFFERS)
             nc.scalar.activation(out=sig[:], in_=a[:].rearrange("c (p u v) -> c u p v", u=2, v=2), func=SIGMOID)
             sigmoids[j, s] = sig
 
-        def value_product(j, s, number):
-            b = bank(number, [P, PASS], "b_%d_%d" % (j, s))
+        def value_product(j, s, behind=None):
+            b = bank("b_%d_%d" % (j, s), [P, PASS], behind)
             first_product(j, s, 1, b)
             values[j, s] = b
 
         def multiply(j, s):
-            h = work.tile([P, 2, P, 2], BF16, name="h", bufs=8)
+            h = work.tile([P, 2, P, 2], BF16, name="h", bufs=HIDDEN_BUFFERS)
             b = values[j, s]
             nc.vector.tensor_tensor(
                 out=h[:], in0=b[:].rearrange("c (p u v) -> c u p v", u=2, v=2), in1=sigmoids[j, s][:], op=MULT
             )
             hidden[j, s] = h
 
-        def value_half(j, s, number):
-            value_product(j, s, number)
+        def value_half(j, s, behind=None):
+            value_product(j, s, behind)
             multiply(j, s)
 
         def turned_tile(tiles):
@@ -179,37 +186,34 @@ def tile_moe_pkd_glu_sigmoid_kernel(
             for j in tiles:
                 turned[j] = (ht, tiles)
 
-        def turn(j, passes, number):
-            xt = bank(number, [P, len(passes), 2, P], "xt_%d_%d" % (j, passes[0]))
+        def turn(j, passes, copy, behind=None):
+            xt = bank("xt_%d_%d" % (j, passes[0]), [P, len(passes), 2, P], behind)
             for at, s in enumerate(passes):
                 pairs = hidden[j, s][:].rearrange("c u p v -> c (u p v)").bitcast(F32)
                 for u in range(2):
                     nc.tensor.transpose(xt[:, at, u, :], pairs[:, u * P : (u + 1) * P], ident[:])
-            crossed[j, passes] = xt
-
-        def weave(j, passes, copy):
             ht, tiles = turned[j]
-            k = tiles.index(j)
+            place = tiles.index(j)
             words = ht[:].bitcast(F32).rearrange("p (s c u) -> p s c u", s=PASSES, u=2)
             copy(
-                out=words[:, passes[0] : passes[-1] + 1, k * P : (k + 1) * P, :],
-                in_=crossed[j, passes][:].rearrange("p s u c -> p s c u"),
+                out=words[:, passes[0] : passes[-1] + 1, place * P : (place + 1) * P, :],
+                in_=xt[:].rearrange("p s u c -> p s c u"),
             )
 
         def quantise(j, passes):
             ht, tiles = turned[j]
             slots = len(tiles) * P
             if passes[0] == 0:
-                codes = work.tile([P, PASSES * slots], U32, name="codes", bufs=4, align_bytes=ALIGN)
-                scales = work.tile([P, PASSES * slots], U8, name="scales", bufs=4, align_bytes=ALIGN)
+                codes = work.tile([P, PASSES * slots], U32, name="codes", bufs=QUANTISED_BUFFERS, align_bytes=ALIGN)
+                scales = work.tile([P, PASSES * slots], U8, name="scales", bufs=QUANTISED_BUFFERS, align_bytes=ALIGN)
                 quantised[j] = (codes, scales)
             codes, scales = quantised[j]
             lo, hi = passes[0] * slots, (passes[-1] + 1) * slots
             nc.vector.quantize_mx(out=codes[:, lo:hi].bitcast(FP8X4), scales=scales[:, lo:hi], in_=ht[:, 4 * lo : 4 * hi])
 
-        def second_layer(j, number):
+        def second_layer(j, behind=None):
             slots = len(turned[j][1]) * P
-            y = bank(number, [P, slots], "y_%d" % j)
+            y = bank("y_%d" % j, [P, slots], behind)
             codes, scales = quantised[j]
             for s in range(PASSES):
                 g = j // PER_EXPERT * PASSES + s
@@ -228,12 +232,17 @@ def tile_moe_pkd_glu_sigmoid_kernel(
             lo, hi = j * P, (j + len(turned[j][1])) * P
             nc.vector.tensor_tensor(out=results[:, lo:hi], in0=sums[j][:], in1=gates[:, lo:hi], op=MULT)
 
-        def scatter(lo, hi):
+        def scatter_expert(e):
+            lo, hi = e * C, (e + 1) * C
             nc.scalar.activation(out=window[:].indirect(listed(lo, hi)), in_=results[:, lo:hi], func=COPY)
 
-        def keep_clock(number):
-            codes, scales = quantised[2]
-            idle = bank(number, [P, PASS], "idle_%d" % number)
+        def scatter_tile(j):
+            lo, hi = j * P, (j + 1) * P
+            nc.vector.tensor_tensor(out=window[:].indirect(listed(lo, hi)), in0=results[:, lo:hi], in1=zeros[:], op=ADD)
+
+        def warm_up(behind):
+            codes, scales = quantised[PER_EXPERT]
+            idle = bank("idle_" + behind, [P, PASS], behind)
             nc.tensor.matmul_mx(
                 out=idle[:],
                 lhsT=w2w[:, PASSES, :].bitcast(FP4X4),
@@ -244,11 +253,6 @@ def tile_moe_pkd_glu_sigmoid_kernel(
                 stop=True,
             )
 
-        def scatter_last(lo, hi):
-            nc.vector.tensor_tensor(
-                out=window[:].indirect(listed(lo, hi)), in0=results[:, lo:hi], in1=zeros[:, : hi - lo], op=ADD
-            )
-
         both = tuple(range(PASSES))
         on_scalar, on_vector = nc.scalar.copy, nc.vector.tensor_copy
         nc.vector.tensor_copy(out=early_scales[:], in_=xs[:].indirect(listed(0, EARLY_SLOTS)))
@@ -256,84 +260,71 @@ def tile_moe_pkd_glu_sigmoid_kernel(
             nc.vector.tensor_copy(out=slot_words[:, lo:hi], in_=xw[:].bitcast(U32).indirect(listed(lo, hi)))
         nc.vector.tensor_copy(out=late_scales[:], in_=xs[:].indirect(listed(EARLY_SLOTS, E * C)))
 
-        gate_half(0, 0, 0)
-        gate_half(1, 0, 1)
-        gate_half(0, 1, 2)
-        gate_half(1, 1, 3)
-        value_half(0, 0, 4)
-        value_half(0, 1, 5)
-        gate_half(2, 0, 0)
-        value_half(1, 0, 6)
-        gate_half(2, 1, 1)
-        value_half(1, 1, 7)
-        gate_half(3, 0, 2)
-        value_half(2, 0, 4)
-        gate_half(3, 1, 3)
-        value_half(2, 1, 5)
-        turned_tile((0, 1))
-        turn(0, both, 1)
-        weave(0, both, on_vector)
-        turn(1, both, 2)
-        weave(1, both, on_scalar)
-        value_half(3, 0, 6)
-        quantise(0, both)
-        value_half(3, 1, 7)
-        gate_half(4, 0, 0)
-        gate_half(4, 1, 3)
-        gate_half(5, 0, 4)
-        value_half(4, 0, 5)
-        gate_half(5, 1, 1)
-        second_layer(0, 0)
-        weigh(0)
-        value_half(4, 1, 2)
-        scatter(0, 256)
-        turned_tile((2, 3))
-        turn(2, both, 3)
-        weave(2, both, on_vector)
-        turn(3, both, 4)
-        weave(3, both, on_vector)
-        value_half(5, 0, 6)
-        value_half(5, 1, 7)
+        for s in both:
+            for j in range(PER_EXPERT):
+                gate_half(j, s)
+        for s in both:
+            value_half(0, s)
+
+        for e, copies in ((1, (on_vector, on_scalar)), (2, (on_vector, on_vector))):
+            j = e * PER_EXPERT
+            value_half(j - 1, 0)
+            if e > 1:
+                quantise(j - 4, both)
+            gate_half(j, 0)
+            value_half(j - 1, 1)
+            gate_half(j, 1)
+            gate_half(j + 1, 0)
+            value_half(j, 0)
+            gate_half(j + 1, 1)
+            if e > 1:
+                second_layer(j - 4, behind="a_%d_0" % j)
+                weigh(j - 4)
+            value_half(j, 1)
+            turned_tile((j - 2, j - 1))
+            turn(j - 2, both, copies[0], behind="a_%d_1" % j)
+            turn(j - 1, both, copies[1], behind="a_%d_0" % (j + 1))
+            if e > 1:
+                scatter_expert(e - 2)
+
+        value_half(5, 0)
+        gate_half(6, 0)
+        value_half(5, 1)
         quantise(2, both)
-        gate_half(6, 0, 1)
-        value_half(6, 0, 5)
-        gate_half(6, 1, 0)
+        gate_half(6, 1)
+        value_half(6, 0)
+        gate_half(7, 0)
         turned_tile((4, 5))
-        gate_half(7, 0, 4)
-        turn(4, both, 2)
-        weave(4, both, on_scalar)
-        turn(5, both, 3)
-        weave(5, both, on_scalar)
-        value_half(6, 1, 7)
-        second_layer(2, 1)
-        gate_half(7, 1, 0)
+        turn(4, both, on_scalar)
+        turn(5, both, on_scalar)
+        value_half(6, 1, behind="b_5_1")
+        second_layer(2, behind="a_6_0")
+        gate_half(7, 1, behind="a_6_1")
         weigh(2)
         quantise(4, both)
-        value_half(7, 0, 2)
-        scatter(256, 512)
+        value_half(7, 0, behind="xt_4_0")
+        scatter_expert(1)
+
         turned_tile((6,))
-        turn(6, both, 5)
-        weave(6, both, on_vector)
-        value_product(7, 1, 7)
-        second_layer(4, 1)
+        turn(6, both, on_vector, behind="b_6_0")
+        value_product(7, 1, behind="b_6_1")
+        second_layer(4, behind="y_2")
         turned_tile((7,))
-        turn(7, (0,), 2)
-        weave(7, (0,), on_scalar)
+        turn(7, (0,), on_scalar, behind="b_7_0")
         weigh(4)
-        keep_clock(5)
-        keep_clock(1)
+        warm_up(behind="xt_6_0")
+        warm_up(behind="y_4")
         multiply(7, 1)
-        scatter(512, 768)
+        scatter_expert(2)
         quantise(6, both)
         quantise(7, (0,))
-        turn(7, (1,), 7)
-        weave(7, (1,), on_vector)
-        second_layer(6, 5)
-        keep_clock(7)
+        turn(7, (1,), on_vector, behind="b_7_1")
+        second_layer(6)
+        warm_up(behind="xt_7_1")
         weigh(6)
         quantise(7, (1,))
-        second_layer(7, 2)
-        scatter_last(768, 896)
+        second_layer(7)
+        scatter_tile(6)
         weigh(7)
-        scatter_last(896, 1024)
+        scatter_tile(7)
         nc.sync.dma_start(out=out, in_=window[:])

@@ -28,11 +28,13 @@ ALIGN = 64
 BANKS = 8
 BANK_BYTES = 4 * PASS
 EARLY_EXPERTS = 2
+LATE_MATRICES = 2 * (E - EARLY_EXPERTS)
+BLOCKS = 16
 EARLY_SLOTS = EARLY_EXPERTS * C
 WORD_CUTS = (0, T // 8, 3 * P, E * C)
-SIGMOID_BUFFERS = 6
+SIGMOID_BUFFERS = 8
 HIDDEN_BUFFERS = 8
-QUANTISED_BUFFERS = 4
+QUANTISED_BUFFERS = 5
 
 
 def tile_moe_pkd_glu_sigmoid_kernel(
@@ -42,12 +44,15 @@ def tile_moe_pkd_glu_sigmoid_kernel(
     with ExitStack() as ctx:
         keep = ctx.enter_context(tc.tile_pool(name="keep", bufs=1))
         head_bytes = ctx.enter_context(tc.tile_pool(name="head_bytes", bufs=1))
-        work = ctx.enter_context(tc.tile_pool(name="work", bufs=3))
+        work = ctx.enter_context(tc.tile_pool(name="work", bufs=5))
         psum = ctx.enter_context(tc.psum_pool(name="psum", bufs=1))
 
         offsets = keep.tile([P, E * C // PER_COLUMN], U16, name="offsets")
         early_planes = [keep.tile([P, EARLY_EXPERTS * H], U8, name="early_plane_%d" % m, align_bytes=ALIGN) for m in range(2)]
-        late_planes = [keep.tile([P, (E - EARLY_EXPERTS) * H], U8, name="late_plane_%d" % m, align_bytes=ALIGN) for m in range(2)]
+        late_rows = keep.tile([P, PASS], U8, name="late_rows", align_bytes=ALIGN)
+        sorted_rows = keep.tile([P, PASS], U8, name="sorted_rows", align_bytes=ALIGN)
+        late_planes = keep.tile([P, LATE_MATRICES * H], U8, name="late_planes", align_bytes=ALIGN)
+        sorted_words = [keep.tile([P, H], U16, name="sorted_words_%d" % g, align_bytes=ALIGN) for g in range(LATE_MATRICES)]
         w2s = keep.tile([P, E * PASSES * N], U8, name="w2s", align_bytes=ALIGN)
         ident = keep.tile([P, P], F32, name="ident")
         far_left = keep.tile([P, 8], F32, name="far_left")
@@ -79,10 +84,38 @@ def tile_moe_pkd_glu_sigmoid_kernel(
             src = w1_words[0, 0][:, 2 * PASS * s : 2 * PASS * (s + 1)]
             nc.sync.dma_start(out=weight_words(0, 0, s).bitcast(I32), in_=src.bitcast(I32))
 
+        def late_matrix(e, m):
+            return 2 * (e - EARLY_EXPERTS) + m
+
+        def load_late_rows(m):
+            for s in range(PASSES):
+                dst = late_rows[PASSES * m + s : P : 2 * PASSES, :]
+                src = (w1_scales, w3_scales)[m][EARLY_EXPERTS:, 0, :, PASS * s : PASS * (s + 1)].rearrange("e f w -> f e w")
+                nc.sync.dma_start(out=dst.bitcast(I32), in_=src.bitcast(I32))
+
+        def sort_rows():
+            nc.gpsimd.tensor_copy(
+                out=sorted_rows[:].rearrange("p (t c) -> p t c", t=4),
+                in_=late_rows[:].rearrange("p (c t) -> p t c", t=4),
+            )
+
+        def place_rows(q):
+            rows = 4 * LATE_MATRICES * PASSES
+            nc.sync.dma_start(
+                out=late_planes[32 * q : 32 * q + 4, :].bitcast(I32),
+                in_=sorted_rows[rows * q : rows * (q + 1), :].bitcast(I32),
+            )
+
+        def sort_words(e, m, s, copy):
+            copy(
+                out=sorted_words[late_matrix(e, m)][:, PASS * s : PASS * (s + 1)].rearrange("p (t c) -> p t c", t=4),
+                in_=weight_words(e, m, s).bitcast(U16).rearrange("p (c t) -> p t c", t=4),
+            )
+
         nc.vector.memset(xs[:].bitcast(I32), 0)
         nc.vector.memset(early_planes[0][:].bitcast(I32), 0)
         nc.vector.memset(far_left[:, 0:1], -200.0)
-        for plane in early_planes[1:] + late_planes + [w2s]:
+        for plane in early_planes[1:] + [late_planes, w2s]:
             nc.vector.memset(plane[:].bitcast(I32), 0)
         nc.vector.memset(ident[:], 0.0)
         nc.vector.memset(zeros[:], 0.0)
@@ -97,19 +130,22 @@ def tile_moe_pkd_glu_sigmoid_kernel(
         load_first_matrix(1)
         load_matrix(0, 1)
         load_scales(early_planes[1], w3_scales[:EARLY_EXPERTS, 0], range(4), nc.sync)
+        load_matrix(1, 0)
+        load_matrix(1, 1)
         for m in range(2):
-            load_matrix(1, m)
-        load_scales(w2s, w2_scales.rearrange("e s f n -> (e s) f n"), range(4), nc.sync)
-        load_scales(late_planes[1], w3_scales[EARLY_EXPERTS:, 0], range(4), nc.sync)
+            load_late_rows(m)
+        sort_rows()
         load_matrix(2, 0)
+        load_matrix(2, 1)
+        load_scales(w2s, w2_scales.rearrange("e s f n -> (e s) f n"), range(4), nc.sync)
+        for q in range(4):
+            place_rows(q)
         nc.sync.dma_start(
             out=w2w[:, :PASSES, :].bitcast(I32), in_=w2_words[0].rearrange("s p b -> p s b").bitcast(I32)
         )
-        load_scales(late_planes[0], w1_scales[EARLY_EXPERTS:, 0], range(4), nc.sync)
-        load_matrix(2, 1)
         nc.sync.dma_start(out=gates[:, :C], in_=gate[:, :C])
-        for m in range(2):
-            load_matrix(3, m)
+        load_matrix(3, 0)
+        load_matrix(3, 1)
         nc.sync.dma_start(
             out=w2w[:, PASSES:, :].bitcast(I32), in_=w2_words[1:].rearrange("e s p b -> p (e s) b").bitcast(I32)
         )
@@ -142,27 +178,60 @@ def tile_moe_pkd_glu_sigmoid_kernel(
             e = j // PER_EXPERT
             lo = j * P
             if e < EARLY_EXPERTS:
-                slot_scales = early_scales[:, lo : lo + P]
-                plane = early_planes[m][:, e * H : (e + 1) * H]
-            else:
-                slot_scales = late_scales[:, lo - EARLY_SLOTS : lo - EARLY_SLOTS + P]
-                plane = late_planes[m][:, (e - EARLY_EXPERTS) * H : (e - EARLY_EXPERTS + 1) * H]
-            nc.tensor.matmul_mx(
-                out=acc[:],
-                lhsT=slot_words[:, lo : lo + P].bitcast(FP8X4),
-                lhsT_scale=slot_scales,
-                rhs=weight_words(e, m, s).bitcast(FP4X4),
-                rhs_scale=plane[:, PASS * s : PASS * (s + 1)],
-                start=True,
-                stop=True,
-            )
+                nc.tensor.matmul_mx(
+                    out=acc[:],
+                    lhsT=slot_words[:, lo : lo + P].bitcast(FP8X4),
+                    lhsT_scale=early_scales[:, lo : lo + P],
+                    rhs=weight_words(e, m, s).bitcast(FP4X4),
+                    rhs_scale=early_planes[m][:, e * H + PASS * s : e * H + PASS * (s + 1)],
+                    start=True,
+                    stop=True,
+                )
+                return
+            g = late_matrix(e, m)
+            for t in range(4):
+                at = PASS * s + P * t
+                nc.tensor.matmul_mx(
+                    out=acc[:, P * t : P * (t + 1)],
+                    lhsT=sorted_words[g][:].bitcast(U8)[:, 2 * at : 2 * (at + P)].bitcast(FP4X4),
+                    lhsT_scale=late_planes[:, g * H + at : g * H + at + P],
+                    rhs=slot_words[:, lo : lo + P].bitcast(FP8X4),
+                    rhs_scale=late_scales[:, lo - EARLY_SLOTS : lo - EARLY_SLOTS + P],
+                    start=True,
+                    stop=True,
+                )
+
+        def bank_order(j, acc):
+            if j // PER_EXPERT < EARLY_EXPERTS:
+                return acc[:].rearrange("c (p u v) -> c u p v", u=2, v=2)
+            return acc[:].rearrange("p (t c) -> p c t", t=4)
 
         def gate_half(j, s, behind=None):
             a = bank("a_%d_%d" % (j, s), [P, PASS], behind)
             first_product(j, s, 0, a)
-            sig = work.tile([P, 2, P, 2], F32, name="sig", bufs=SIGMOID_BUFFERS)
-            nc.scalar.activation(out=sig[:], in_=a[:].rearrange("c (p u v) -> c u p v", u=2, v=2), func=SIGMOID)
+            source = bank_order(j, a)
+            sig = work.tile(list(source.shape), F32, name="sig", bufs=SIGMOID_BUFFERS)
+            nc.scalar.activation(out=sig[:], in_=source, func=SIGMOID)
             sigmoids[j, s] = sig
+
+        def gate_pair(e, s, pair, behind=None):
+            a = bank("a_%d_%d_%d" % (e, s, pair), [P, 2, C], behind)
+            g = late_matrix(e, 0)
+            lo = e * C
+            for v in range(2):
+                at = PASS * s + P * (2 * pair + v)
+                nc.tensor.matmul_mx(
+                    out=a[:, v, :],
+                    lhsT=sorted_words[g][:].bitcast(U8)[:, 2 * at : 2 * (at + P)].bitcast(FP4X4),
+                    lhsT_scale=late_planes[:, g * H + at : g * H + at + P],
+                    rhs=slot_words[:, lo : lo + C].bitcast(FP8X4),
+                    rhs_scale=late_scales[:, lo - EARLY_SLOTS : lo - EARLY_SLOTS + C],
+                    start=True,
+                    stop=True,
+                )
+            if pair == 0:
+                sigmoids[e, s, "pairs"] = work.tile([P, 2, C, 2], F32, name="sig_pairs", bufs=4)
+            nc.scalar.activation(out=sigmoids[e, s, "pairs"][:, pair], in_=a[:].rearrange("p v c -> p c v"), func=SIGMOID)
 
         def value_product(j, s, behind=None):
             b = bank("b_%d_%d" % (j, s), [P, PASS], behind)
@@ -170,12 +239,23 @@ def tile_moe_pkd_glu_sigmoid_kernel(
             values[j, s] = b
 
         def multiply(j, s):
-            h = work.tile([P, 2, P, 2], BF16, name="h", bufs=HIDDEN_BUFFERS)
-            b = values[j, s]
-            nc.vector.tensor_tensor(
-                out=h[:], in0=b[:].rearrange("c (p u v) -> c u p v", u=2, v=2), in1=sigmoids[j, s][:], op=MULT
-            )
-            hidden[j, s] = h
+            source = bank_order(j, values[j, s])
+            if j // PER_EXPERT < EARLY_EXPERTS:
+                h = work.tile([P, 2, P, 2], BF16, name="h", bufs=HIDDEN_BUFFERS)
+                hidden[j, s] = h
+                dst = h[:]
+            else:
+                ht, tiles = turned[j]
+                place = tiles.index(j)
+                dst = ht[:].rearrange("p (s c t) -> p s c t", s=PASSES, t=4)[:, s, place * P : (place + 1) * P, :]
+            if j // PER_EXPERT < EARLY_EXPERTS:
+                sig = sigmoids[j, s][:]
+            else:
+                c0 = j % PER_EXPERT * P
+                sig = sigmoids[j // PER_EXPERT, s, "pairs"][:, :, c0 : c0 + P, :].rearrange("p u c v -> p c u v")
+                source = source.rearrange("p c (u v) -> p c u v", u=2)
+                dst = dst.rearrange("p c (u v) -> p c u v", u=2)
+            nc.vector.tensor_tensor(out=dst, in0=source, in1=sig, op=MULT)
 
         def value_half(j, s, behind=None):
             value_product(j, s, behind)
@@ -240,19 +320,6 @@ def tile_moe_pkd_glu_sigmoid_kernel(
             lo, hi = j * P, (j + 1) * P
             nc.vector.tensor_tensor(out=window[:].indirect(listed(lo, hi)), in0=results[:, lo:hi], in1=zeros[:], op=ADD)
 
-        def warm_up(behind):
-            codes, scales = quantised[PER_EXPERT]
-            idle = bank("idle_" + behind, [P, PASS], behind)
-            nc.tensor.matmul_mx(
-                out=idle[:],
-                lhsT=w2w[:, PASSES, :].bitcast(FP4X4),
-                lhsT_scale=w2s[:, PASSES * N : (PASSES + 1) * N],
-                rhs=codes[:].bitcast(FP8X4),
-                rhs_scale=scales[:],
-                start=True,
-                stop=True,
-            )
-
         both = tuple(range(PASSES))
         on_scalar, on_vector = nc.scalar.copy, nc.vector.tensor_copy
         nc.vector.tensor_copy(out=early_scales[:], in_=xs[:].indirect(listed(0, EARLY_SLOTS)))
@@ -260,67 +327,86 @@ def tile_moe_pkd_glu_sigmoid_kernel(
             nc.vector.tensor_copy(out=slot_words[:, lo:hi], in_=xw[:].bitcast(U32).indirect(listed(lo, hi)))
         nc.vector.tensor_copy(out=late_scales[:], in_=xs[:].indirect(listed(EARLY_SLOTS, E * C)))
 
-        for s in both:
-            for j in range(PER_EXPERT):
-                gate_half(j, s)
-        for s in both:
-            value_half(0, s)
-
-        for e, copies in ((1, (on_vector, on_scalar)), (2, (on_vector, on_vector))):
-            j = e * PER_EXPERT
-            value_half(j - 1, 0)
-            if e > 1:
-                quantise(j - 4, both)
-            gate_half(j, 0)
-            value_half(j - 1, 1)
-            gate_half(j, 1)
-            gate_half(j + 1, 0)
-            value_half(j, 0)
-            gate_half(j + 1, 1)
-            if e > 1:
-                second_layer(j - 4, behind="a_%d_0" % j)
-                weigh(j - 4)
-            value_half(j, 1)
-            turned_tile((j - 2, j - 1))
-            turn(j - 2, both, copies[0], behind="a_%d_1" % j)
-            turn(j - 1, both, copies[1], behind="a_%d_0" % (j + 1))
-            if e > 1:
-                scatter_expert(e - 2)
-
-        value_half(5, 0)
-        gate_half(6, 0)
-        value_half(5, 1)
-        quantise(2, both)
-        gate_half(6, 1)
-        value_half(6, 0)
-        gate_half(7, 0)
+        turned_tile((0, 1))
+        turned_tile((2, 3))
         turned_tile((4, 5))
-        turn(4, both, on_scalar)
-        turn(5, both, on_scalar)
-        value_half(6, 1, behind="b_5_1")
-        second_layer(2, behind="a_6_0")
-        gate_half(7, 1, behind="a_6_1")
-        weigh(2)
-        quantise(4, both)
-        value_half(7, 0, behind="xt_4_0")
-        scatter_expert(1)
-
         turned_tile((6,))
-        turn(6, both, on_vector, behind="b_6_0")
-        value_product(7, 1, behind="b_6_1")
-        second_layer(4, behind="y_2")
         turned_tile((7,))
-        turn(7, (0,), on_scalar, behind="b_7_0")
+        sort_words(2, 0, 0, nc.gpsimd.tensor_copy)
+        sort_words(2, 0, 1, nc.gpsimd.tensor_copy)
+        sort_words(2, 1, 0, nc.gpsimd.tensor_copy)
+        sort_words(2, 1, 1, nc.gpsimd.tensor_copy)
+        sort_words(3, 0, 0, nc.gpsimd.tensor_copy)
+        sort_words(3, 0, 1, nc.gpsimd.tensor_copy)
+        sort_words(3, 1, 0, nc.gpsimd.tensor_copy)
+        sort_words(3, 1, 1, nc.gpsimd.tensor_copy)
+        gate_half(0, 0)
+        gate_half(1, 0)
+        gate_half(0, 1)
+        gate_half(1, 1)
+        value_product(0, 0)
+        multiply(0, 0)
+        value_product(0, 1)
+        multiply(0, 1)
+        gate_half(2, 0)
+        value_product(1, 0)
+        multiply(1, 0)
+        gate_half(2, 1)
+        value_product(1, 1)
+        multiply(1, 1)
+        gate_half(3, 0)
+        value_product(2, 0)
+        multiply(2, 0)
+        gate_half(3, 1)
+        value_product(2, 1)
+        turn(0, both, on_scalar, behind="a_2_1")
+        turn(1, both, on_scalar, behind="a_3_0")
+        multiply(2, 1)
+        value_product(3, 0)
+        multiply(3, 0)
+        gate_pair(2, 0, 0)
+        value_product(3, 1)
+        multiply(3, 1)
+        gate_pair(2, 0, 1)
+        quantise(0, both)
+        gate_pair(2, 1, 0)
+        value_product(4, 0)
+        multiply(4, 0)
+        gate_pair(2, 1, 1)
+        second_layer(0, behind="a_2_0_1")
+        value_product(5, 0)
+        weigh(0)
+        multiply(5, 0)
+        scatter_expert(0)
+        turn(2, both, on_vector, behind="a_2_1_0")
+        turn(3, both, on_vector, behind="a_2_1_1")
+        value_product(4, 1)
+        gate_pair(3, 0, 0)
+        multiply(4, 1)
+        value_product(5, 1)
+        gate_pair(3, 0, 1)
+        quantise(2, both)
+        multiply(5, 1)
+        gate_pair(3, 1, 0)
+        value_product(6, 0)
+        second_layer(2, behind="a_3_0_1")
+        gate_pair(3, 1, 1)
+        weigh(2)
+        value_product(7, 0)
+        multiply(6, 0)
+        quantise(4, both)
+        scatter_expert(1)
+        value_product(6, 1)
+        multiply(7, 0)
+        second_layer(4, behind="b_6_0")
+        value_product(7, 1)
         weigh(4)
-        warm_up(behind="xt_6_0")
-        warm_up(behind="y_4")
+        multiply(6, 1)
+        quantise(7, (0,))
+        quantise(6, both)
         multiply(7, 1)
         scatter_expert(2)
-        quantise(6, both)
-        quantise(7, (0,))
-        turn(7, (1,), on_vector, behind="b_7_1")
         second_layer(6)
-        warm_up(behind="xt_7_1")
         weigh(6)
         quantise(7, (1,))
         second_layer(7)

@@ -44,6 +44,7 @@ def tile_moe_pkd_glu_sigmoid_kernel(
     with ExitStack() as ctx:
         keep = ctx.enter_context(tc.tile_pool(name="keep", bufs=1))
         head_bytes = ctx.enter_context(tc.tile_pool(name="head_bytes", bufs=1))
+        first_turned = ctx.enter_context(tc.tile_pool(name="first_turned", bufs=1))
         work = ctx.enter_context(tc.tile_pool(name="work", bufs=5))
         psum = ctx.enter_context(tc.psum_pool(name="psum", bufs=1))
 
@@ -52,7 +53,7 @@ def tile_moe_pkd_glu_sigmoid_kernel(
         late_rows = keep.tile([P, PASS], U8, name="late_rows", align_bytes=ALIGN)
         sorted_rows = keep.tile([P, PASS], U8, name="sorted_rows", align_bytes=ALIGN)
         late_planes = keep.tile([P, LATE_MATRICES * H], U8, name="late_planes", align_bytes=ALIGN)
-        sorted_words = [keep.tile([P, H], U16, name="sorted_words_%d" % g, align_bytes=ALIGN) for g in range(LATE_MATRICES)]
+        sorted_words = {}
         w2s = keep.tile([P, E * PASSES * N], U8, name="w2s", align_bytes=ALIGN)
         ident = keep.tile([P, P], F32, name="ident")
         far_left = keep.tile([P, 8], F32, name="far_left")
@@ -106,9 +107,14 @@ def tile_moe_pkd_glu_sigmoid_kernel(
                 in_=sorted_rows[rows * q : rows * (q + 1), :].bitcast(I32),
             )
 
-        def sort_words(e, m, s, copy):
+        def sort_words(e, m, s, copy, behind_first_quantiser=False):
+            name = "sorted_words_%d_%d_%d" % (e, m, s)
+            if behind_first_quantiser:
+                sorted_words[e, m, s] = first_turned.tile([P, PASS], U16, name=name, align_bytes=ALIGN, offset=0)
+            else:
+                sorted_words[e, m, s] = keep.tile([P, PASS], U16, name=name, align_bytes=ALIGN)
             copy(
-                out=sorted_words[late_matrix(e, m)][:, PASS * s : PASS * (s + 1)].rearrange("p (t c) -> p t c", t=4),
+                out=sorted_words[e, m, s][:].rearrange("p (t c) -> p t c", t=4),
                 in_=weight_words(e, m, s).bitcast(U16).rearrange("p (c t) -> p t c", t=4),
             )
 
@@ -140,11 +146,11 @@ def tile_moe_pkd_glu_sigmoid_kernel(
         load_scales(w2s, w2_scales.rearrange("e s f n -> (e s) f n"), range(4), nc.sync)
         for q in range(4):
             place_rows(q)
+        load_matrix(3, 0)
         nc.sync.dma_start(
             out=w2w[:, :PASSES, :].bitcast(I32), in_=w2_words[0].rearrange("s p b -> p s b").bitcast(I32)
         )
         nc.sync.dma_start(out=gates[:, :C], in_=gate[:, :C])
-        load_matrix(3, 0)
         load_matrix(3, 1)
         nc.sync.dma_start(
             out=w2w[:, PASSES:, :].bitcast(I32), in_=w2_words[1:].rearrange("e s p b -> p (e s) b").bitcast(I32)
@@ -193,7 +199,7 @@ def tile_moe_pkd_glu_sigmoid_kernel(
                 at = PASS * s + P * t
                 nc.tensor.matmul_mx(
                     out=acc[:, P * t : P * (t + 1)],
-                    lhsT=sorted_words[g][:].bitcast(U8)[:, 2 * at : 2 * (at + P)].bitcast(FP4X4),
+                    lhsT=sorted_words[e, m, s][:].bitcast(U8)[:, 2 * P * t : 2 * P * (t + 1)].bitcast(FP4X4),
                     lhsT_scale=late_planes[:, g * H + at : g * H + at + P],
                     rhs=slot_words[:, lo : lo + P].bitcast(FP8X4),
                     rhs_scale=late_scales[:, lo - EARLY_SLOTS : lo - EARLY_SLOTS + P],
@@ -222,7 +228,7 @@ def tile_moe_pkd_glu_sigmoid_kernel(
                 at = PASS * s + P * (2 * pair + v)
                 nc.tensor.matmul_mx(
                     out=a[:, v, :],
-                    lhsT=sorted_words[g][:].bitcast(U8)[:, 2 * at : 2 * (at + P)].bitcast(FP4X4),
+                    lhsT=sorted_words[e, 0, s][:].bitcast(U8)[:, 2 * (at - PASS * s) : 2 * (at - PASS * s + P)].bitcast(FP4X4),
                     lhsT_scale=late_planes[:, g * H + at : g * H + at + P],
                     rhs=slot_words[:, lo : lo + C].bitcast(FP8X4),
                     rhs_scale=late_scales[:, lo - EARLY_SLOTS : lo - EARLY_SLOTS + C],
@@ -230,8 +236,8 @@ def tile_moe_pkd_glu_sigmoid_kernel(
                     stop=True,
                 )
             if pair == 0:
-                sigmoids[e, s, "pairs"] = work.tile([P, 2, C, 2], F32, name="sig_pairs", bufs=4)
-            nc.scalar.activation(out=sigmoids[e, s, "pairs"][:, pair], in_=a[:].rearrange("p v c -> p c v"), func=SIGMOID)
+                sigmoids[e, s, "pairs"] = work.tile([P, 2, C // 2, 2, 2], F32, name="sig_pairs", bufs=4)
+            nc.scalar.activation(out=sigmoids[e, s, "pairs"][:, pair], in_=a[:].rearrange("p v (c i) -> p c v i", i=2), func=SIGMOID)
 
         def value_product(j, s, behind=None):
             b = bank("b_%d_%d" % (j, s), [P, PASS], behind)
@@ -251,10 +257,10 @@ def tile_moe_pkd_glu_sigmoid_kernel(
             if j // PER_EXPERT < EARLY_EXPERTS:
                 sig = sigmoids[j, s][:]
             else:
-                c0 = j % PER_EXPERT * P
-                sig = sigmoids[j // PER_EXPERT, s, "pairs"][:, :, c0 : c0 + P, :].rearrange("p u c v -> p c u v")
-                source = source.rearrange("p c (u v) -> p c u v", u=2)
-                dst = dst.rearrange("p c (u v) -> p c u v", u=2)
+                c0 = j % PER_EXPERT * P // 2
+                sig = sigmoids[j // PER_EXPERT, s, "pairs"][:, :, c0 : c0 + P // 2].rearrange("p u c v i -> p c u v i")
+                source = source.rearrange("p (c i) (u v) -> p c u v i", i=2, u=2)
+                dst = dst.rearrange("p (c i) (u v) -> p c u v i", i=2, u=2)
             nc.vector.tensor_tensor(out=dst, in0=source, in1=sig, op=MULT)
 
         def value_half(j, s, behind=None):
@@ -262,7 +268,10 @@ def tile_moe_pkd_glu_sigmoid_kernel(
             multiply(j, s)
 
         def turned_tile(tiles):
-            ht = work.tile([P, len(tiles) * H], BF16, name="ht", align_bytes=ALIGN)
+            if tiles[0] == 0:
+                ht = first_turned.tile([P, len(tiles) * H], BF16, name="first_ht", align_bytes=ALIGN, offset=0)
+            else:
+                ht = work.tile([P, len(tiles) * H], BF16, name="ht", align_bytes=ALIGN)
             for j in tiles:
                 turned[j] = (ht, tiles)
 
@@ -337,9 +346,6 @@ def tile_moe_pkd_glu_sigmoid_kernel(
         sort_words(2, 1, 0, nc.gpsimd.tensor_copy)
         sort_words(2, 1, 1, nc.gpsimd.tensor_copy)
         sort_words(3, 0, 0, nc.gpsimd.tensor_copy)
-        sort_words(3, 0, 1, nc.gpsimd.tensor_copy)
-        sort_words(3, 1, 0, nc.gpsimd.tensor_copy)
-        sort_words(3, 1, 1, nc.gpsimd.tensor_copy)
         gate_half(0, 0)
         gate_half(1, 0)
         gate_half(0, 1)
@@ -363,49 +369,52 @@ def tile_moe_pkd_glu_sigmoid_kernel(
         turn(1, both, on_scalar, behind="a_3_0")
         multiply(2, 1)
         value_product(3, 0)
-        multiply(3, 0)
         gate_pair(2, 0, 0)
+        multiply(3, 0)
         value_product(3, 1)
-        multiply(3, 1)
         gate_pair(2, 0, 1)
-        quantise(0, both)
+        multiply(3, 1)
         gate_pair(2, 1, 0)
+        quantise(0, both)
+        sort_words(3, 0, 1, nc.gpsimd.tensor_copy, behind_first_quantiser=True)
+        sort_words(3, 1, 0, nc.gpsimd.tensor_copy)
+        sort_words(3, 1, 1, nc.gpsimd.tensor_copy)
         value_product(4, 0)
-        multiply(4, 0)
         gate_pair(2, 1, 1)
-        second_layer(0, behind="a_2_0_1")
+        multiply(4, 0)
         value_product(5, 0)
-        weigh(0)
-        multiply(5, 0)
-        scatter_expert(0)
-        turn(2, both, on_vector, behind="a_2_1_0")
-        turn(3, both, on_vector, behind="a_2_1_1")
-        value_product(4, 1)
         gate_pair(3, 0, 0)
-        multiply(4, 1)
-        value_product(5, 1)
+        multiply(5, 0)
+        value_product(4, 1)
         gate_pair(3, 0, 1)
-        quantise(2, both)
-        multiply(5, 1)
+        multiply(4, 1)
+        turn(2, both, on_vector, behind="a_2_1_0")
+        turn(3, both, on_scalar, behind="a_2_1_1")
+        second_layer(0, behind="a_3_0_0")
+        weigh(0)
+        scatter_expert(0)
+        value_product(5, 1)
         gate_pair(3, 1, 0)
-        value_product(6, 0)
-        second_layer(2, behind="a_3_0_1")
         gate_pair(3, 1, 1)
-        weigh(2)
+        multiply(5, 1)
+        value_product(6, 0)
+        quantise(2, both)
         value_product(7, 0)
-        multiply(6, 0)
         quantise(4, both)
-        scatter_expert(1)
+        second_layer(2)
+        multiply(6, 0)
+        second_layer(4)
+        weigh(2)
         value_product(6, 1)
-        multiply(7, 0)
-        second_layer(4, behind="b_6_0")
-        value_product(7, 1)
         weigh(4)
+        scatter_expert(1)
+        multiply(7, 0)
+        value_product(7, 1)
+        scatter_expert(2)
         multiply(6, 1)
         quantise(7, (0,))
         quantise(6, both)
         multiply(7, 1)
-        scatter_expert(2)
         second_layer(6)
         weigh(6)
         quantise(7, (1,))

@@ -43,24 +43,29 @@ def tile_moe_pkd_glu_sigmoid_kernel(
     nc = tc.nc
     with ExitStack() as ctx:
         keep = ctx.enter_context(tc.tile_pool(name="keep", bufs=1))
+        token_scales = ctx.enter_context(tc.tile_pool(name="token_scales", bufs=1))
         head_bytes = ctx.enter_context(tc.tile_pool(name="head_bytes", bufs=1))
         first_turned = ctx.enter_context(tc.tile_pool(name="first_turned", bufs=1))
         work = ctx.enter_context(tc.tile_pool(name="work", bufs=5))
         psum = ctx.enter_context(tc.psum_pool(name="psum", bufs=1))
 
         offsets = keep.tile([P, E * C // PER_COLUMN], U16, name="offsets")
-        early_planes = [keep.tile([P, EARLY_EXPERTS * H], U8, name="early_plane_%d" % m, align_bytes=ALIGN) for m in range(2)]
+        early_tiles = [keep.tile([P, EARLY_EXPERTS * H + 4], U8, name="early_plane_%d" % m, align_bytes=ALIGN) for m in range(2)]
+        early_planes = [t[:, : EARLY_EXPERTS * H] for t in early_tiles]
         late_rows = keep.tile([P, PASS], U8, name="late_rows", align_bytes=ALIGN)
-        sorted_rows = keep.tile([P, PASS], U8, name="sorted_rows", align_bytes=ALIGN)
         late_planes = keep.tile([P, LATE_MATRICES * H], U8, name="late_planes", align_bytes=ALIGN)
         sorted_words = {}
-        w2s = keep.tile([P, E * PASSES * N], U8, name="w2s", align_bytes=ALIGN)
-        ident = keep.tile([P, P], F32, name="ident")
+        w2s_tile = keep.tile([P, E * PASSES * N + 4], U8, name="w2s", align_bytes=ALIGN)
+        w2s = w2s_tile[:, : E * PASSES * N]
+        ident_tile = keep.tile([P, P + 1], F32, name="ident")
+        ident = ident_tile[:, :P]
         far_left = keep.tile([P, 8], F32, name="far_left")
-        zeros = keep.tile([P, P], F32, name="zeros", align_bytes=ALIGN)
+        zeros_tile = keep.tile([P, P + 1], F32, name="zeros", align_bytes=ALIGN)
+        zeros = zeros_tile[:, :P]
         window = keep.tile([P, T], F32, name="window", align_bytes=ALIGN)
         xw = keep.tile([P, T], I32, name="xw", align_bytes=ALIGN)
-        xs = keep.tile([P, T], U8, name="xs", align_bytes=ALIGN)
+        xs_tile = token_scales.tile([P, T + 4], U8, name="xs", align_bytes=ALIGN, offset=0)
+        xs = xs_tile[:, :T]
         first_words = head_bytes.tile([P, 2 * PASS], U8, name="first_words", align_bytes=ALIGN, offset=0)
         w13 = [keep.tile([P, 2 * 2 * H], U8, name="w13_%d" % e, align_bytes=ALIGN) for e in range(E)]
         w2w = keep.tile([P, E * PASSES, 2 * N], U8, name="w2w", align_bytes=ALIGN)
@@ -91,8 +96,8 @@ def tile_moe_pkd_glu_sigmoid_kernel(
         def load_late_rows(m):
             for s in range(PASSES):
                 dst = late_rows[PASSES * m + s : P : 2 * PASSES, :]
-                src = (w1_scales, w3_scales)[m][EARLY_EXPERTS:, 0, :, PASS * s : PASS * (s + 1)].rearrange("e f w -> f e w")
-                nc.sync.dma_start(out=dst.bitcast(I32), in_=src.bitcast(I32))
+                src = (w1_scales, w3_scales)[m][EARLY_EXPERTS:, 0, :, PASS * s : PASS * (s + 1)]
+                nc.gpsimd.dma_start(out=dst.bitcast(I32), in_=src.rearrange("e (q r) w -> r (e q) w", r=4).bitcast(I32))
 
         def sort_rows():
             nc.gpsimd.tensor_copy(
@@ -100,12 +105,14 @@ def tile_moe_pkd_glu_sigmoid_kernel(
                 in_=late_rows[:].rearrange("p (c t) -> p t c", t=4),
             )
 
-        def place_rows(q):
-            rows = 4 * LATE_MATRICES * PASSES
-            nc.sync.dma_start(
-                out=late_planes[32 * q : 32 * q + 4, :].bitcast(I32),
-                in_=sorted_rows[rows * q : rows * (q + 1), :].bitcast(I32),
-            )
+        def place_rows(e):
+            late = e - EARLY_EXPERTS
+            for r in range(4):
+                lo = 32 * r + BLOCKS * late
+                nc.sync.dma_start(
+                    out=late_planes[r:P:32, 2 * H * late : 2 * H * (late + 1)].bitcast(I32),
+                    in_=sorted_rows[lo : lo + BLOCKS, :].bitcast(I32),
+                )
 
         def sort_words(e, m, s, copy, behind_first_quantiser=False):
             name = "sorted_words_%d_%d_%d" % (e, m, s)
@@ -118,13 +125,16 @@ def tile_moe_pkd_glu_sigmoid_kernel(
                 in_=weight_words(e, m, s).bitcast(U16).rearrange("p (c t) -> p t c", t=4),
             )
 
-        nc.vector.memset(xs[:].bitcast(I32), 0)
-        nc.vector.memset(early_planes[0][:].bitcast(I32), 0)
+        for m in range(2):
+            load_late_rows(m)
+        nc.vector.memset(xs_tile[:].bitcast(I32), 0)
+        nc.vector.memset(early_tiles[0][:].bitcast(I32), 0)
         nc.vector.memset(far_left[:, 0:1], -200.0)
-        for plane in early_planes[1:] + [late_planes, w2s]:
+        for plane in early_tiles[1:] + [w2s_tile]:
             nc.vector.memset(plane[:].bitcast(I32), 0)
-        nc.vector.memset(ident[:], 0.0)
-        nc.vector.memset(zeros[:], 0.0)
+        nc.vector.memset(ident_tile[:], 0.0)
+        nc.vector.memset(zeros_tile[:], 0.0)
+        nc.vector.memset(late_planes[:].bitcast(I32), 0)
         nc.sync.dma_start(offsets[:], offs)
         load_first_matrix(0)
         load_scales(xs, x_scales, range(2), nc.sync)
@@ -138,24 +148,10 @@ def tile_moe_pkd_glu_sigmoid_kernel(
         load_scales(early_planes[1], w3_scales[:EARLY_EXPERTS, 0], range(4), nc.sync)
         load_matrix(1, 0)
         load_matrix(1, 1)
-        for m in range(2):
-            load_late_rows(m)
-        sort_rows()
         load_matrix(2, 0)
         load_matrix(2, 1)
         load_scales(w2s, w2_scales.rearrange("e s f n -> (e s) f n"), range(4), nc.sync)
-        for q in range(4):
-            place_rows(q)
         load_matrix(3, 0)
-        nc.sync.dma_start(
-            out=w2w[:, :PASSES, :].bitcast(I32), in_=w2_words[0].rearrange("s p b -> p s b").bitcast(I32)
-        )
-        nc.sync.dma_start(out=gates[:, :C], in_=gate[:, :C])
-        load_matrix(3, 1)
-        nc.sync.dma_start(
-            out=w2w[:, PASSES:, :].bitcast(I32), in_=w2_words[1:].rearrange("e s p b -> p (e s) b").bitcast(I32)
-        )
-        nc.sync.dma_start(out=gates[:, C:], in_=gate[:, C:])
 
         slot_words = keep.tile([P, E * C], U32, name="slot_words", align_bytes=ALIGN)
         early_scales = keep.tile([P, EARLY_SLOTS], U8, name="early_scales", align_bytes=ALIGN)
@@ -335,6 +331,15 @@ def tile_moe_pkd_glu_sigmoid_kernel(
         for lo, hi in zip(WORD_CUTS, WORD_CUTS[1:]):
             nc.vector.tensor_copy(out=slot_words[:, lo:hi], in_=xw[:].bitcast(U32).indirect(listed(lo, hi)))
         nc.vector.tensor_copy(out=late_scales[:], in_=xs[:].indirect(listed(EARLY_SLOTS, E * C)))
+        sorted_rows = token_scales.tile([P, PASS], U8, name="sorted_rows", align_bytes=ALIGN, offset=0)
+        sort_rows()
+        place_rows(2)
+        place_rows(3)
+        nc.sync.dma_start(out=w2w[:].bitcast(I32), in_=w2_words.rearrange("e s p b -> p (e s) b").bitcast(I32))
+        nc.sync.dma_start(out=gates[:, :C], in_=gate[:, :C])
+        load_matrix(3, 1)
+        nc.sync.dma_start(out=gates[:, C:], in_=gate[:, C:])
+
 
         turned_tile((0, 1))
         turned_tile((2, 3))
@@ -388,7 +393,7 @@ def tile_moe_pkd_glu_sigmoid_kernel(
         value_product(4, 1)
         gate_pair(3, 0, 1)
         multiply(4, 1)
-        turn(2, both, on_vector, behind="a_2_1_0")
+        turn(2, both, on_vector, behind="b_5_0")
         turn(3, both, on_scalar, behind="a_2_1_1")
         second_layer(0, behind="a_3_0_0")
         weigh(0)

@@ -331,7 +331,7 @@ def tile_moe_pkd_glu_sigmoid_kernel(
         for lo, hi in zip(WORD_CUTS, WORD_CUTS[1:]):
             nc.vector.tensor_copy(out=slot_words[:, lo:hi], in_=xw[:].bitcast(U32).indirect(listed(lo, hi)))
         nc.vector.tensor_copy(out=late_scales[:], in_=xs[:].indirect(listed(EARLY_SLOTS, E * C)))
-        sorted_rows = token_scales.tile([P, PASS], U8, name="sorted_rows", align_bytes=ALIGN, offset=0)
+        sorted_rows = keep.tile([P, PASS], U8, name="sorted_rows", align_bytes=ALIGN)
         sort_rows()
         place_rows(2)
         place_rows(3)

@@ -31,7 +31,7 @@ EARLY_EXPERTS = 2
 LATE_MATRICES = 2 * (E - EARLY_EXPERTS)
 BLOCKS = 16
 EARLY_SLOTS = EARLY_EXPERTS * C
-WORD_CUTS = (0, T // 8, 3 * P, E * C)
+WORD_CUTS = (0, P, 3 * P, E * C)
 SIGMOID_BUFFERS = 8
 HIDDEN_BUFFERS = 8
 QUANTISED_BUFFERS = 5
@@ -52,8 +52,9 @@ def tile_moe_pkd_glu_sigmoid_kernel(
         offsets = keep.tile([P, E * C // PER_COLUMN], U16, name="offsets")
         early_tiles = [keep.tile([P, EARLY_EXPERTS * H + 4], U8, name="early_plane_%d" % m, align_bytes=ALIGN) for m in range(2)]
         early_planes = [t[:, : EARLY_EXPERTS * H] for t in early_tiles]
-        late_rows = keep.tile([P, PASS], U8, name="late_rows", align_bytes=ALIGN)
-        late_planes = keep.tile([P, LATE_MATRICES * H], U8, name="late_planes", align_bytes=ALIGN)
+        late_rows = keep.tile([P, H], U8, name="late_rows", align_bytes=ALIGN)
+        late_tile = keep.tile([P, LATE_MATRICES * H + 4], U8, name="late_planes", align_bytes=ALIGN)
+        late_planes = late_tile[:, : LATE_MATRICES * H]
         sorted_words = {}
         w2s_tile = keep.tile([P, E * PASSES * N + 4], U8, name="w2s", align_bytes=ALIGN)
         w2s = w2s_tile[:, : E * PASSES * N]
@@ -94,24 +95,23 @@ def tile_moe_pkd_glu_sigmoid_kernel(
             return 2 * (e - EARLY_EXPERTS) + m
 
         def load_late_rows(m):
-            for s in range(PASSES):
-                dst = late_rows[PASSES * m + s : P : 2 * PASSES, :]
-                src = (w1_scales, w3_scales)[m][EARLY_EXPERTS:, 0, :, PASS * s : PASS * (s + 1)]
-                nc.gpsimd.dma_start(out=dst.bitcast(I32), in_=src.rearrange("e (q r) w -> r (e q) w", r=4).bitcast(I32))
+            dst = late_rows[m : LATE_MATRICES * BLOCKS : 2, :]
+            src = (w1_scales, w3_scales)[m][EARLY_EXPERTS:, 0].rearrange("e (q r) w -> r (e q) w", r=4)
+            nc.gpsimd.dma_start(out=dst.bitcast(I32), in_=src.bitcast(I32))
 
         def sort_rows():
             nc.gpsimd.tensor_copy(
-                out=sorted_rows[:].rearrange("p (t c) -> p t c", t=4),
-                in_=late_rows[:].rearrange("p (c t) -> p t c", t=4),
+                out=sorted_rows[:].rearrange("p (s t c) -> p s t c", s=PASSES, t=4),
+                in_=late_rows[:].rearrange("p (s c t) -> p s t c", s=PASSES, t=4),
             )
 
         def place_rows(e):
             late = e - EARLY_EXPERTS
             for r in range(4):
-                lo = 32 * r + BLOCKS * late
+                lo = 4 * LATE_MATRICES * r + 8 * late
                 nc.sync.dma_start(
                     out=late_planes[r:P:32, 2 * H * late : 2 * H * (late + 1)].bitcast(I32),
-                    in_=sorted_rows[lo : lo + BLOCKS, :].bitcast(I32),
+                    in_=sorted_rows[lo : lo + 8, :].bitcast(I32),
                 )
 
         def sort_words(e, m, s, copy, behind_first_quantiser=False):
@@ -125,22 +125,22 @@ def tile_moe_pkd_glu_sigmoid_kernel(
                 in_=weight_words(e, m, s).bitcast(U16).rearrange("p (c t) -> p t c", t=4),
             )
 
+        nc.gpsimd.memset(xs_tile[:].bitcast(I32), 0)
+        nc.gpsimd.dma_start(out=first_words[:].bitcast(I32), in_=w1_words[0, 0][:, : 2 * PASS].bitcast(I32))
         for m in range(2):
             load_late_rows(m)
-        nc.vector.memset(xs_tile[:].bitcast(I32), 0)
+        nc.gpsimd.memset(late_rows[LATE_MATRICES * BLOCKS :, :].bitcast(I32), 0)
         nc.vector.memset(early_tiles[0][:].bitcast(I32), 0)
         nc.vector.memset(far_left[:, 0:1], -200.0)
         for plane in early_tiles[1:] + [w2s_tile]:
             nc.vector.memset(plane[:].bitcast(I32), 0)
-        nc.vector.memset(ident_tile[:], 0.0)
-        nc.vector.memset(zeros_tile[:], 0.0)
-        nc.vector.memset(late_planes[:].bitcast(I32), 0)
+        nc.gpsimd.memset(late_tile[:].bitcast(I32), 0)
+        nc.gpsimd.memset(zeros_tile[:], 0.0)
         nc.sync.dma_start(offsets[:], offs)
-        load_first_matrix(0)
         load_scales(xs, x_scales, range(2), nc.sync)
         load_scales(xs, x_scales, range(2, 4), nc.scalar)
         nc.sync.dma_start(out=xw[:], in_=x_words[0].rearrange("p t r -> p (t r)").bitcast(I32))
-        make_identity(nc, ident[:], nomemset=True)
+        make_identity(nc, ident[:])
         nc.scalar.activation(out=window[:], in_=far_left[:, 0:1].to_broadcast([P, T]), func=SIGMOID)
         load_scales(early_planes[0], w1_scales[:EARLY_EXPERTS, 0], range(4), nc.sync)
         load_first_matrix(1)
@@ -331,7 +331,7 @@ def tile_moe_pkd_glu_sigmoid_kernel(
         for lo, hi in zip(WORD_CUTS, WORD_CUTS[1:]):
             nc.vector.tensor_copy(out=slot_words[:, lo:hi], in_=xw[:].bitcast(U32).indirect(listed(lo, hi)))
         nc.vector.tensor_copy(out=late_scales[:], in_=xs[:].indirect(listed(EARLY_SLOTS, E * C)))
-        sorted_rows = keep.tile([P, PASS], U8, name="sorted_rows", align_bytes=ALIGN)
+        sorted_rows = keep.tile([P, H], U8, name="sorted_rows", align_bytes=ALIGN)
         sort_rows()
         place_rows(2)
         place_rows(3)

@@ -22,6 +22,9 @@ COPY = mybir.ActivationFunctionType.Copy
 P = 128
 PASS = 512
 PASSES = H // PASS
+VALUES = 4
+ROWS = 4
+GROUP = 32
 PER_EXPERT = C // P
 PER_COLUMN = 16
 ALIGN = 64
@@ -29,12 +32,11 @@ BANKS = 8
 BANK_BYTES = 4 * PASS
 EARLY_EXPERTS = 2
 LATE_MATRICES = 2 * (E - EARLY_EXPERTS)
-BLOCKS = 16
 EARLY_SLOTS = EARLY_EXPERTS * C
 WORD_CUTS = (0, P, 3 * P, E * C)
-SIGMOID_BUFFERS = 8
-HIDDEN_BUFFERS = 8
-QUANTISED_BUFFERS = 5
+EARLY_HALVES = EARLY_EXPERTS * PER_EXPERT * PASSES
+LATE_HALVES = (E - EARLY_EXPERTS) * PASSES
+GROUPS = ((0, 1), (2, 3), (4, 5), (6,), (7,))
 
 
 def tile_moe_pkd_glu_sigmoid_kernel(
@@ -43,19 +45,18 @@ def tile_moe_pkd_glu_sigmoid_kernel(
     nc = tc.nc
     with ExitStack() as ctx:
         keep = ctx.enter_context(tc.tile_pool(name="keep", bufs=1))
-        token_scales = ctx.enter_context(tc.tile_pool(name="token_scales", bufs=1))
         head_bytes = ctx.enter_context(tc.tile_pool(name="head_bytes", bufs=1))
-        first_turned = ctx.enter_context(tc.tile_pool(name="first_turned", bufs=1))
-        work = ctx.enter_context(tc.tile_pool(name="work", bufs=5))
+        first_h_bytes = ctx.enter_context(tc.tile_pool(name="first_h_bytes", bufs=1))
+        work = ctx.enter_context(tc.tile_pool(name="work", bufs=len(GROUPS)))
         psum = ctx.enter_context(tc.psum_pool(name="psum", bufs=1))
 
         offsets = keep.tile([P, E * C // PER_COLUMN], U16, name="offsets")
-        early_tiles = [keep.tile([P, EARLY_EXPERTS * H + 4], U8, name="early_plane_%d" % m, align_bytes=ALIGN) for m in range(2)]
-        early_planes = [t[:, : EARLY_EXPERTS * H] for t in early_tiles]
+        early_tiles = [
+            keep.tile([P, EARLY_EXPERTS * H + 4], U8, name="early_plane_%d" % m, align_bytes=ALIGN) for m in range(2)
+        ]
+        early_planes = [tile[:, : EARLY_EXPERTS * H] for tile in early_tiles]
         late_rows = keep.tile([P, H], U8, name="late_rows", align_bytes=ALIGN)
-        late_tile = keep.tile([P, LATE_MATRICES * H + 4], U8, name="late_planes", align_bytes=ALIGN)
-        late_planes = late_tile[:, : LATE_MATRICES * H]
-        sorted_words = {}
+        late_planes = keep.tile([P, LATE_MATRICES * H], U8, name="late_planes", align_bytes=ALIGN)
         w2s_tile = keep.tile([P, E * PASSES * N + 4], U8, name="w2s", align_bytes=ALIGN)
         w2s = w2s_tile[:, : E * PASSES * N]
         ident_tile = keep.tile([P, P + 1], F32, name="ident")
@@ -65,8 +66,7 @@ def tile_moe_pkd_glu_sigmoid_kernel(
         zeros = zeros_tile[:, :P]
         window = keep.tile([P, T], F32, name="window", align_bytes=ALIGN)
         xw = keep.tile([P, T], I32, name="xw", align_bytes=ALIGN)
-        xs_tile = token_scales.tile([P, T + 4], U8, name="xs", align_bytes=ALIGN, offset=0)
-        xs = xs_tile[:, :T]
+        xs = keep.tile([P, T], U8, name="xs", align_bytes=ALIGN)
         first_words = head_bytes.tile([P, 2 * PASS], U8, name="first_words", align_bytes=ALIGN, offset=0)
         w13 = [keep.tile([P, 2 * 2 * H], U8, name="w13_%d" % e, align_bytes=ALIGN) for e in range(E)]
         w2w = keep.tile([P, E * PASSES, 2 * N], U8, name="w2w", align_bytes=ALIGN)
@@ -78,89 +78,74 @@ def tile_moe_pkd_glu_sigmoid_kernel(
             return w13[e][:, 2 * (H * m + PASS * s) : 2 * (H * m + PASS * (s + 1))]
 
         def load_scales(plane, scale_rows, rows, queue):
-            by_row = scale_rows.rearrange("g (q r) w -> r q g w", r=4)
+            by_row = scale_rows.rearrange("g (q r) w -> r q g w", r=ROWS)
             for r in rows:
-                dst = plane[r:P:32, :].bitcast(I32).rearrange("q (g w) -> q g w", g=scale_rows.shape[0])
+                dst = plane[r:P:GROUP, :].bitcast(I32).rearrange("q (g w) -> q g w", g=scale_rows.shape[0])
                 queue.dma_start(out=dst, in_=by_row[r].bitcast(I32))
 
         def load_matrix(e, m):
             dst = w13[e][:, 2 * H * m : 2 * H * (m + 1)]
             nc.sync.dma_start(out=dst.bitcast(I32), in_=(w1_words, w3_words)[m][e, 0].bitcast(I32))
 
-        def load_first_matrix(s):
+        def load_first_matrix(s, queue):
             src = w1_words[0, 0][:, 2 * PASS * s : 2 * PASS * (s + 1)]
-            nc.sync.dma_start(out=weight_words(0, 0, s).bitcast(I32), in_=src.bitcast(I32))
+            queue.dma_start(out=weight_words(0, 0, s).bitcast(I32), in_=src.bitcast(I32))
 
-        def late_matrix(e, m):
-            return 2 * (e - EARLY_EXPERTS) + m
+        late_partitions = LATE_MATRICES * ROWS * ROWS
 
         def load_late_rows(m):
-            dst = late_rows[m : LATE_MATRICES * BLOCKS : 2, :]
-            src = (w1_scales, w3_scales)[m][EARLY_EXPERTS:, 0].rearrange("e (q r) w -> r (e q) w", r=4)
-            nc.gpsimd.dma_start(out=dst.bitcast(I32), in_=src.bitcast(I32))
-
-        def sort_rows():
-            nc.gpsimd.tensor_copy(
-                out=sorted_rows[:].rearrange("p (s t c) -> p s t c", s=PASSES, t=4),
-                in_=late_rows[:].rearrange("p (s c t) -> p s t c", s=PASSES, t=4),
-            )
+            src = (w1_scales, w3_scales)[m][EARLY_EXPERTS:, 0].rearrange("e (q r) w -> r (e q) w", r=ROWS)
+            nc.gpsimd.dma_start(out=late_rows[m:late_partitions:2, :].bitcast(I32), in_=src.bitcast(I32))
 
         def place_rows(e):
             late = e - EARLY_EXPERTS
-            for r in range(4):
-                lo = 4 * LATE_MATRICES * r + 8 * late
+            for r in range(ROWS):
+                lo = ROWS * (LATE_MATRICES * r + 2 * late)
                 nc.sync.dma_start(
-                    out=late_planes[r:P:32, 2 * H * late : 2 * H * (late + 1)].bitcast(I32),
-                    in_=sorted_rows[lo : lo + 8, :].bitcast(I32),
+                    out=late_planes[r:P:GROUP, 2 * H * late : 2 * H * (late + 1)].bitcast(I32),
+                    in_=sorted_rows[lo : lo + 2 * ROWS, :].bitcast(I32),
                 )
 
-        def sort_words(e, m, s, copy, behind_first_quantiser=False):
-            name = "sorted_words_%d_%d_%d" % (e, m, s)
-            if behind_first_quantiser:
-                sorted_words[e, m, s] = first_turned.tile([P, PASS], U16, name=name, align_bytes=ALIGN, offset=0)
-            else:
-                sorted_words[e, m, s] = keep.tile([P, PASS], U16, name=name, align_bytes=ALIGN)
-            copy(
-                out=sorted_words[e, m, s][:].rearrange("p (t c) -> p t c", t=4),
-                in_=weight_words(e, m, s).bitcast(U16).rearrange("p (c t) -> p t c", t=4),
-            )
-
-        nc.gpsimd.memset(xs_tile[:].bitcast(I32), 0)
-        nc.gpsimd.dma_start(out=first_words[:].bitcast(I32), in_=w1_words[0, 0][:, : 2 * PASS].bitcast(I32))
+        nc.gpsimd.memset(xs[:].bitcast(I32), 0)
+        load_first_matrix(0, nc.gpsimd)
         for m in range(2):
             load_late_rows(m)
-        nc.gpsimd.memset(late_rows[LATE_MATRICES * BLOCKS :, :].bitcast(I32), 0)
+        nc.gpsimd.memset(late_rows[late_partitions:, :].bitcast(I32), 0)
         nc.vector.memset(early_tiles[0][:].bitcast(I32), 0)
         nc.vector.memset(far_left[:, 0:1], -200.0)
-        for plane in early_tiles[1:] + [w2s_tile]:
-            nc.vector.memset(plane[:].bitcast(I32), 0)
-        nc.gpsimd.memset(late_tile[:].bitcast(I32), 0)
-        nc.gpsimd.memset(zeros_tile[:], 0.0)
+        for tile in (early_tiles[1], w2s_tile):
+            nc.vector.memset(tile[:].bitcast(I32), 0)
+        nc.vector.memset(ident_tile[:], 0.0)
+        nc.vector.memset(zeros_tile[:], 0.0)
         nc.sync.dma_start(offsets[:], offs)
-        load_scales(xs, x_scales, range(2), nc.sync)
-        load_scales(xs, x_scales, range(2, 4), nc.scalar)
+        load_scales(xs, x_scales, range(ROWS // 2), nc.sync)
+        load_scales(xs, x_scales, range(ROWS // 2, ROWS), nc.scalar)
         nc.sync.dma_start(out=xw[:], in_=x_words[0].rearrange("p t r -> p (t r)").bitcast(I32))
-        make_identity(nc, ident[:])
+        make_identity(nc, ident[:], nomemset=True)
         nc.scalar.activation(out=window[:], in_=far_left[:, 0:1].to_broadcast([P, T]), func=SIGMOID)
-        load_scales(early_planes[0], w1_scales[:EARLY_EXPERTS, 0], range(4), nc.sync)
-        load_first_matrix(1)
+        nc.scalar.copy(
+            out=late_planes[:].bitcast(U32), in_=zeros[:, 0:1].bitcast(U32).to_broadcast([P, LATE_MATRICES * H // 4])
+        )
+        load_scales(early_planes[0], w1_scales[:EARLY_EXPERTS, 0], range(ROWS), nc.sync)
+        load_first_matrix(1, nc.sync)
         load_matrix(0, 1)
-        load_scales(early_planes[1], w3_scales[:EARLY_EXPERTS, 0], range(4), nc.sync)
-        load_matrix(1, 0)
-        load_matrix(1, 1)
-        load_matrix(2, 0)
-        load_matrix(2, 1)
-        load_scales(w2s, w2_scales.rearrange("e s f n -> (e s) f n"), range(4), nc.sync)
+        load_scales(early_planes[1], w3_scales[:EARLY_EXPERTS, 0], range(ROWS), nc.sync)
+        for e in (1, 2):
+            for m in range(2):
+                load_matrix(e, m)
+        load_scales(w2s, w2_scales.rearrange("e s f n -> (e s) f n"), range(ROWS), nc.sync)
         load_matrix(3, 0)
 
         slot_words = keep.tile([P, E * C], U32, name="slot_words", align_bytes=ALIGN)
         early_scales = keep.tile([P, EARLY_SLOTS], U8, name="early_scales", align_bytes=ALIGN)
         late_scales = head_bytes.tile([P, E * C - EARLY_SLOTS], U8, name="late_scales", align_bytes=ALIGN, offset=0)
         results = keep.tile([P, E * C], F32, name="results", align_bytes=ALIGN)
-        sigmoids = {}
+        sorted_words = {}
+        early_sigmoids = {}
+        late_sigmoids = {}
         values = {}
         hidden = {}
-        turned = {}
+        quantiser_input = {}
         quantised = {}
         sums = {}
         oldest_first = list(range(BANKS))
@@ -176,134 +161,115 @@ def tile_moe_pkd_glu_sigmoid_kernel(
         def listed(lo, hi):
             return offsets[:, lo // PER_COLUMN : hi // PER_COLUMN]
 
-        def first_product(j, s, m, acc):
-            e = j // PER_EXPERT
-            lo = j * P
-            if e < EARLY_EXPERTS:
-                nc.tensor.matmul_mx(
-                    out=acc[:],
-                    lhsT=slot_words[:, lo : lo + P].bitcast(FP8X4),
-                    lhsT_scale=early_scales[:, lo : lo + P],
-                    rhs=weight_words(e, m, s).bitcast(FP4X4),
-                    rhs_scale=early_planes[m][:, e * H + PASS * s : e * H + PASS * (s + 1)],
-                    start=True,
-                    stop=True,
-                )
-                return
-            g = late_matrix(e, m)
-            for t in range(4):
-                at = PASS * s + P * t
-                nc.tensor.matmul_mx(
-                    out=acc[:, P * t : P * (t + 1)],
-                    lhsT=sorted_words[e, m, s][:].bitcast(U8)[:, 2 * P * t : 2 * P * (t + 1)].bitcast(FP4X4),
-                    lhsT_scale=late_planes[:, g * H + at : g * H + at + P],
-                    rhs=slot_words[:, lo : lo + P].bitcast(FP8X4),
-                    rhs_scale=late_scales[:, lo - EARLY_SLOTS : lo - EARLY_SLOTS + P],
-                    start=True,
-                    stop=True,
-                )
-
-        def bank_order(j, acc):
-            if j // PER_EXPERT < EARLY_EXPERTS:
-                return acc[:].rearrange("c (p u v) -> c u p v", u=2, v=2)
-            return acc[:].rearrange("p (t c) -> p c t", t=4)
-
-        def gate_half(j, s, behind=None):
-            a = bank("a_%d_%d" % (j, s), [P, PASS], behind)
-            first_product(j, s, 0, a)
-            source = bank_order(j, a)
-            sig = work.tile(list(source.shape), F32, name="sig", bufs=SIGMOID_BUFFERS)
-            nc.scalar.activation(out=sig[:], in_=source, func=SIGMOID)
-            sigmoids[j, s] = sig
-
-        def gate_pair(e, s, pair, behind=None):
-            a = bank("a_%d_%d_%d" % (e, s, pair), [P, 2, C], behind)
-            g = late_matrix(e, 0)
-            lo = e * C
-            for v in range(2):
-                at = PASS * s + P * (2 * pair + v)
-                nc.tensor.matmul_mx(
-                    out=a[:, v, :],
-                    lhsT=sorted_words[e, 0, s][:].bitcast(U8)[:, 2 * (at - PASS * s) : 2 * (at - PASS * s + P)].bitcast(FP4X4),
-                    lhsT_scale=late_planes[:, g * H + at : g * H + at + P],
-                    rhs=slot_words[:, lo : lo + C].bitcast(FP8X4),
-                    rhs_scale=late_scales[:, lo - EARLY_SLOTS : lo - EARLY_SLOTS + C],
-                    start=True,
-                    stop=True,
-                )
-            if pair == 0:
-                sigmoids[e, s, "pairs"] = work.tile([P, 2, C // 2, 2, 2], F32, name="sig_pairs", bufs=4)
-            nc.scalar.activation(out=sigmoids[e, s, "pairs"][:, pair], in_=a[:].rearrange("p v (c i) -> p c v i", i=2), func=SIGMOID)
-
-        def value_product(j, s, behind=None):
-            b = bank("b_%d_%d" % (j, s), [P, PASS], behind)
-            first_product(j, s, 1, b)
-            values[j, s] = b
-
-        def multiply(j, s):
-            source = bank_order(j, values[j, s])
-            if j // PER_EXPERT < EARLY_EXPERTS:
-                h = work.tile([P, 2, P, 2], BF16, name="h", bufs=HIDDEN_BUFFERS)
-                hidden[j, s] = h
-                dst = h[:]
-            else:
-                ht, tiles = turned[j]
-                place = tiles.index(j)
-                dst = ht[:].rearrange("p (s c t) -> p s c t", s=PASSES, t=4)[:, s, place * P : (place + 1) * P, :]
-            if j // PER_EXPERT < EARLY_EXPERTS:
-                sig = sigmoids[j, s][:]
-            else:
-                c0 = j % PER_EXPERT * P // 2
-                sig = sigmoids[j // PER_EXPERT, s, "pairs"][:, :, c0 : c0 + P // 2].rearrange("p u c v i -> p c u v i")
-                source = source.rearrange("p (c i) (u v) -> p c u v i", i=2, u=2)
-                dst = dst.rearrange("p (c i) (u v) -> p c u v i", i=2, u=2)
-            nc.vector.tensor_tensor(out=dst, in0=source, in1=sig, op=MULT)
-
-        def value_half(j, s, behind=None):
-            value_product(j, s, behind)
-            multiply(j, s)
-
-        def turned_tile(tiles):
-            if tiles[0] == 0:
-                ht = first_turned.tile([P, len(tiles) * H], BF16, name="first_ht", align_bytes=ALIGN, offset=0)
-            else:
-                ht = work.tile([P, len(tiles) * H], BF16, name="ht", align_bytes=ALIGN)
-            for j in tiles:
-                turned[j] = (ht, tiles)
-
-        def turn(j, passes, copy, behind=None):
-            xt = bank("xt_%d_%d" % (j, passes[0]), [P, len(passes), 2, P], behind)
-            for at, s in enumerate(passes):
-                pairs = hidden[j, s][:].rearrange("c u p v -> c (u p v)").bitcast(F32)
-                for u in range(2):
-                    nc.tensor.transpose(xt[:, at, u, :], pairs[:, u * P : (u + 1) * P], ident[:])
-            ht, tiles = turned[j]
-            place = tiles.index(j)
-            words = ht[:].bitcast(F32).rearrange("p (s c u) -> p s c u", s=PASSES, u=2)
-            copy(
-                out=words[:, passes[0] : passes[-1] + 1, place * P : (place + 1) * P, :],
-                in_=xt[:].rearrange("p s u c -> p s c u"),
+        def sort_words(e, m, s, pool=keep, offset=None):
+            name = "sorted_words_%d_%d_%d" % (e, m, s)
+            sorted_words[e, m, s] = pool.tile([P, VALUES, P], U16, name=name, align_bytes=ALIGN, offset=offset)
+            nc.gpsimd.tensor_copy(
+                out=sorted_words[e, m, s][:],
+                in_=weight_words(e, m, s).bitcast(U16).rearrange("k (p t) -> k t p", t=VALUES),
             )
 
-        def quantise(j, passes):
-            ht, tiles = turned[j]
+        def early_product(j, s, m, acc):
+            e = j // PER_EXPERT
+            nc.tensor.matmul_mx(
+                out=acc,
+                lhsT=slot_words[:, j * P : (j + 1) * P].bitcast(FP8X4),
+                lhsT_scale=early_scales[:, j * P : (j + 1) * P],
+                rhs=weight_words(e, m, s).bitcast(FP4X4),
+                rhs_scale=early_planes[m][:, e * H + PASS * s : e * H + PASS * (s + 1)],
+                start=True,
+                stop=True,
+            )
+
+        def late_product(e, m, s, t, lo, hi, acc):
+            at = (2 * (e - EARLY_EXPERTS) + m) * H + PASS * s + P * t
+            nc.tensor.matmul_mx(
+                out=acc,
+                lhsT=sorted_words[e, m, s][:, t, :].bitcast(U8).bitcast(FP4X4),
+                lhsT_scale=late_planes[:, at : at + P],
+                rhs=slot_words[:, lo:hi].bitcast(FP8X4),
+                rhs_scale=late_scales[:, lo - EARLY_SLOTS : hi - EARLY_SLOTS],
+                start=True,
+                stop=True,
+            )
+
+        def early_order(acc):
+            return acc[:].rearrange("c (p u v) -> c u p v", u=2, v=2)
+
+        def early_sigmoid(j, s):
+            a = bank("a_%d_%d" % (j, s), [P, PASS], None)
+            early_product(j, s, 0, a[:])
+            early_sigmoids[j, s] = work.tile([P, 2, P, 2], F32, name="early_sigmoid", bufs=EARLY_HALVES)
+            nc.scalar.activation(out=early_sigmoids[j, s][:], in_=early_order(a), func=SIGMOID)
+
+        def late_sigmoid(e, s, u):
+            a = bank("a_%d_%d_%d" % (e, s, u), [P, 2, C], None)
+            for v in range(2):
+                late_product(e, 0, s, 2 * u + v, e * C, (e + 1) * C, a[:, v, :])
+            if u == 0:
+                late_sigmoids[e, s] = work.tile([P, 2, C // 2, 2, 2], F32, name="late_sigmoid", bufs=LATE_HALVES)
+            nc.scalar.activation(
+                out=late_sigmoids[e, s][:, u], in_=a[:].rearrange("p v (d n) -> p d v n", n=2), func=SIGMOID
+            )
+
+        def value_product(j, s):
+            e = j // PER_EXPERT
+            values[j, s] = bank("b_%d_%d" % (j, s), [P, PASS], None)
+            if e < EARLY_EXPERTS:
+                early_product(j, s, 1, values[j, s][:])
+            else:
+                for t in range(VALUES):
+                    late_product(e, 1, s, t, j * P, (j + 1) * P, values[j, s][:, P * t : P * (t + 1)])
+
+        def slots_of(j, s):
+            h, tiles = quantiser_input[j]
+            place = tiles.index(j)
+            return h[:].rearrange("p (s c t) -> p s c t", s=PASSES, t=VALUES)[:, s, place * P : (place + 1) * P, :]
+
+        def multiply(j, s):
+            e = j // PER_EXPERT
+            if e < EARLY_EXPERTS:
+                hidden[j, s] = work.tile([P, 2, P, 2], BF16, name="early_h", bufs=EARLY_HALVES)
+                dst, b, sig = hidden[j, s][:], early_order(values[j, s]), early_sigmoids[j, s][:]
+            else:
+                first_pair = j % PER_EXPERT * P // 2
+                dst = slots_of(j, s).rearrange("p (d n) (u v) -> p d u v n", n=2, u=2)
+                b = values[j, s][:].rearrange("p (u v d n) -> p d u v n", u=2, v=2, n=2)
+                sig = late_sigmoids[e, s][:, :, first_pair : first_pair + P // 2].rearrange("p u d v n -> p d u v n")
+            nc.vector.tensor_tensor(out=dst, in0=b, in1=sig, op=MULT)
+
+        def turn(j, copy, behind):
+            xt = bank("xt_%d" % j, [P, PASSES, 2, P], behind)
+            for s in range(PASSES):
+                pairs = hidden[j, s][:].rearrange("c u p v -> c (u p v)").bitcast(F32)
+                for u in range(2):
+                    nc.tensor.transpose(xt[:, s, u, :], pairs[:, u * P : (u + 1) * P], ident[:])
+            h, tiles = quantiser_input[j]
+            place = tiles.index(j)
+            words = h[:].bitcast(F32).rearrange("p (s c u) -> p s c u", s=PASSES, u=2)
+            copy(out=words[:, :, place * P : (place + 1) * P, :], in_=xt[:].rearrange("p s u c -> p s c u"))
+
+        def quantise(j, passes=range(PASSES)):
+            h, tiles = quantiser_input[j]
             slots = len(tiles) * P
             if passes[0] == 0:
-                codes = work.tile([P, PASSES * slots], U32, name="codes", bufs=QUANTISED_BUFFERS, align_bytes=ALIGN)
-                scales = work.tile([P, PASSES * slots], U8, name="scales", bufs=QUANTISED_BUFFERS, align_bytes=ALIGN)
+                codes = work.tile([P, PASSES * slots], U32, name="codes", align_bytes=ALIGN)
+                scales = work.tile([P, PASSES * slots], U8, name="scales", align_bytes=ALIGN)
                 quantised[j] = (codes, scales)
             codes, scales = quantised[j]
             lo, hi = passes[0] * slots, (passes[-1] + 1) * slots
-            nc.vector.quantize_mx(out=codes[:, lo:hi].bitcast(FP8X4), scales=scales[:, lo:hi], in_=ht[:, 4 * lo : 4 * hi])
+            nc.vector.quantize_mx(
+                out=codes[:, lo:hi].bitcast(FP8X4), scales=scales[:, lo:hi], in_=h[:, VALUES * lo : VALUES * hi]
+            )
 
         def second_layer(j, behind=None):
-            slots = len(turned[j][1]) * P
-            y = bank("y_%d" % j, [P, slots], behind)
+            slots = len(quantiser_input[j][1]) * P
+            sums[j] = bank("y_%d" % j, [P, slots], behind)
             codes, scales = quantised[j]
             for s in range(PASSES):
                 g = j // PER_EXPERT * PASSES + s
                 nc.tensor.matmul_mx(
-                    out=y[:],
+                    out=sums[j][:],
                     lhsT=w2w[:, g, :].bitcast(FP4X4),
                     lhsT_scale=w2s[:, g * N : (g + 1) * N],
                     rhs=codes[:, s * slots : (s + 1) * slots].bitcast(FP8X4),
@@ -311,10 +277,9 @@ def tile_moe_pkd_glu_sigmoid_kernel(
                     start=(s == 0),
                     stop=(s == PASSES - 1),
                 )
-            sums[j] = y
 
         def weigh(j):
-            lo, hi = j * P, (j + len(turned[j][1])) * P
+            lo, hi = j * P, (j + len(quantiser_input[j][1])) * P
             nc.vector.tensor_tensor(out=results[:, lo:hi], in0=sums[j][:], in1=gates[:, lo:hi], op=MULT)
 
         def scatter_expert(e):
@@ -325,87 +290,85 @@ def tile_moe_pkd_glu_sigmoid_kernel(
             lo, hi = j * P, (j + 1) * P
             nc.vector.tensor_tensor(out=window[:].indirect(listed(lo, hi)), in0=results[:, lo:hi], in1=zeros[:], op=ADD)
 
-        both = tuple(range(PASSES))
-        on_scalar, on_vector = nc.scalar.copy, nc.vector.tensor_copy
         nc.vector.tensor_copy(out=early_scales[:], in_=xs[:].indirect(listed(0, EARLY_SLOTS)))
         for lo, hi in zip(WORD_CUTS, WORD_CUTS[1:]):
             nc.vector.tensor_copy(out=slot_words[:, lo:hi], in_=xw[:].bitcast(U32).indirect(listed(lo, hi)))
         nc.vector.tensor_copy(out=late_scales[:], in_=xs[:].indirect(listed(EARLY_SLOTS, E * C)))
+
         sorted_rows = keep.tile([P, H], U8, name="sorted_rows", align_bytes=ALIGN)
-        sort_rows()
-        place_rows(2)
-        place_rows(3)
+        nc.gpsimd.tensor_copy(
+            out=sorted_rows[:].rearrange("row (s t p) -> row s t p", s=PASSES, t=VALUES),
+            in_=late_rows[:].rearrange("row (s p t) -> row s t p", s=PASSES, t=VALUES),
+        )
+        for e in range(EARLY_EXPERTS, E):
+            place_rows(e)
         nc.sync.dma_start(out=w2w[:].bitcast(I32), in_=w2_words.rearrange("e s p b -> p (e s) b").bitcast(I32))
         nc.sync.dma_start(out=gates[:, :C], in_=gate[:, :C])
         load_matrix(3, 1)
         nc.sync.dma_start(out=gates[:, C:], in_=gate[:, C:])
 
+        for tiles in GROUPS:
+            if tiles == GROUPS[0]:
+                h = first_h_bytes.tile([P, len(tiles) * H], BF16, name="first_h", align_bytes=ALIGN, offset=0)
+            else:
+                h = work.tile([P, len(tiles) * H], BF16, name="h", align_bytes=ALIGN)
+            for j in tiles:
+                quantiser_input[j] = (h, tiles)
 
-        turned_tile((0, 1))
-        turned_tile((2, 3))
-        turned_tile((4, 5))
-        turned_tile((6,))
-        turned_tile((7,))
-        sort_words(2, 0, 0, nc.gpsimd.tensor_copy)
-        sort_words(2, 0, 1, nc.gpsimd.tensor_copy)
-        sort_words(2, 1, 0, nc.gpsimd.tensor_copy)
-        sort_words(2, 1, 1, nc.gpsimd.tensor_copy)
-        sort_words(3, 0, 0, nc.gpsimd.tensor_copy)
-        gate_half(0, 0)
-        gate_half(1, 0)
-        gate_half(0, 1)
-        gate_half(1, 1)
-        value_product(0, 0)
-        multiply(0, 0)
-        value_product(0, 1)
-        multiply(0, 1)
-        gate_half(2, 0)
-        value_product(1, 0)
-        multiply(1, 0)
-        gate_half(2, 1)
-        value_product(1, 1)
-        multiply(1, 1)
-        gate_half(3, 0)
+        for m in range(2):
+            for s in range(PASSES):
+                sort_words(2, m, s)
+        sort_words(3, 0, 0)
+
+        for s in range(PASSES):
+            for j in GROUPS[0]:
+                early_sigmoid(j, s)
+        for s in range(PASSES):
+            value_product(0, s)
+            multiply(0, s)
+        for s in range(PASSES):
+            early_sigmoid(2, s)
+            value_product(1, s)
+            multiply(1, s)
+        early_sigmoid(3, 0)
         value_product(2, 0)
         multiply(2, 0)
-        gate_half(3, 1)
+        early_sigmoid(3, 1)
         value_product(2, 1)
-        turn(0, both, on_scalar, behind="a_2_1")
-        turn(1, both, on_scalar, behind="a_3_0")
+        turn(0, nc.scalar.copy, behind="a_2_1")
+        turn(1, nc.scalar.copy, behind="a_3_0")
         multiply(2, 1)
-        value_product(3, 0)
-        gate_pair(2, 0, 0)
-        multiply(3, 0)
-        value_product(3, 1)
-        gate_pair(2, 0, 1)
-        multiply(3, 1)
-        gate_pair(2, 1, 0)
-        quantise(0, both)
-        sort_words(3, 0, 1, nc.gpsimd.tensor_copy, behind_first_quantiser=True)
-        sort_words(3, 1, 0, nc.gpsimd.tensor_copy)
-        sort_words(3, 1, 1, nc.gpsimd.tensor_copy)
+        for s in range(PASSES):
+            value_product(3, s)
+            late_sigmoid(2, 0, s)
+            multiply(3, s)
+        late_sigmoid(2, 1, 0)
+        quantise(0)
+        sort_words(3, 0, 1, pool=first_h_bytes, offset=0)
+        for s in range(PASSES):
+            sort_words(3, 1, s)
         value_product(4, 0)
-        gate_pair(2, 1, 1)
+        late_sigmoid(2, 1, 1)
         multiply(4, 0)
         value_product(5, 0)
-        gate_pair(3, 0, 0)
+        late_sigmoid(3, 0, 0)
         multiply(5, 0)
         value_product(4, 1)
-        gate_pair(3, 0, 1)
+        late_sigmoid(3, 0, 1)
         multiply(4, 1)
-        turn(2, both, on_vector, behind="b_5_0")
-        turn(3, both, on_scalar, behind="a_2_1_1")
+        turn(2, nc.vector.tensor_copy, behind="b_5_0")
+        turn(3, nc.scalar.copy, behind="a_2_1_1")
         second_layer(0, behind="a_3_0_0")
         weigh(0)
         scatter_expert(0)
         value_product(5, 1)
-        gate_pair(3, 1, 0)
-        gate_pair(3, 1, 1)
+        for u in range(2):
+            late_sigmoid(3, 1, u)
         multiply(5, 1)
         value_product(6, 0)
-        quantise(2, both)
+        quantise(2)
         value_product(7, 0)
-        quantise(4, both)
+        quantise(4)
         second_layer(2)
         multiply(6, 0)
         second_layer(4)
@@ -417,12 +380,12 @@ def tile_moe_pkd_glu_sigmoid_kernel(
         value_product(7, 1)
         scatter_expert(2)
         multiply(6, 1)
-        quantise(7, (0,))
-        quantise(6, both)
+        quantise(7, range(1))
+        quantise(6)
         multiply(7, 1)
         second_layer(6)
         weigh(6)
-        quantise(7, (1,))
+        quantise(7, range(1, PASSES))
         second_layer(7)
         scatter_tile(6)
         weigh(7)

from contextlib import ExitStack

import concourse.mybir as mybir
from concourse.masks import make_identity

K, T, E, C, H, N = 512, 1280, 4, 256, 1024, 128
FLOPS = 2 * E * C * (2 * K * H + H * N)

F32 = mybir.dt.float32
BF16 = mybir.dt.bfloat16
I32 = mybir.dt.int32
U32 = mybir.dt.uint32
U16 = mybir.dt.uint16
U8 = mybir.dt.uint8
FP8X4 = mybir.dt.float8_e4m3fn_x4
FP4X4 = mybir.dt.float4_e2m1fn_x4
MULT = mybir.AluOpType.mult
ADD = mybir.AluOpType.add
SIGMOID = mybir.ActivationFunctionType.Sigmoid
COPY = mybir.ActivationFunctionType.Copy

P = 128
PASS = 512
PASSES = H // PASS
VALUES = 4
ROWS = 4
GROUP = 32
PER_EXPERT = C // P
PER_COLUMN = 16
ALIGN = 64
BANKS = 8
BANK_BYTES = 4 * PASS
EARLY_EXPERTS = 2
LATE_MATRICES = 2 * (E - EARLY_EXPERTS)
EARLY_SLOTS = EARLY_EXPERTS * C
WORD_CUTS = (0, P, 3 * P, E * C)
EARLY_HALVES = EARLY_EXPERTS * PER_EXPERT * PASSES
LATE_HALVES = (E - EARLY_EXPERTS) * PASSES
GROUPS = ((0, 1), (2, 3), (4, 5), (6,), (7,))


def tile_moe_pkd_glu_sigmoid_kernel(
    tc, x_words, x_scales, w1_words, w1_scales, w3_words, w3_scales, w2_words, w2_scales, gate, offs, out
):
    nc = tc.nc
    with ExitStack() as ctx:
        keep = ctx.enter_context(tc.tile_pool(name="keep", bufs=1))
        head_bytes = ctx.enter_context(tc.tile_pool(name="head_bytes", bufs=1))
        first_h_bytes = ctx.enter_context(tc.tile_pool(name="first_h_bytes", bufs=1))
        work = ctx.enter_context(tc.tile_pool(name="work", bufs=len(GROUPS)))
        psum = ctx.enter_context(tc.psum_pool(name="psum", bufs=1))

        offsets = keep.tile([P, E * C // PER_COLUMN], U16, name="offsets")
        early_tiles = [
            keep.tile([P, EARLY_EXPERTS * H + 4], U8, name="early_plane_%d" % m, align_bytes=ALIGN) for m in range(2)
        ]
        early_planes = [tile[:, : EARLY_EXPERTS * H] for tile in early_tiles]
        late_rows = keep.tile([P, H], U8, name="late_rows", align_bytes=ALIGN)
        late_planes = keep.tile([P, LATE_MATRICES * H], U8, name="late_planes", align_bytes=ALIGN)
        w2s_tile = keep.tile([P, E * PASSES * N + 4], U8, name="w2s", align_bytes=ALIGN)
        w2s = w2s_tile[:, : E * PASSES * N]
        ident_tile = keep.tile([P, P + 1], F32, name="ident")
        ident = ident_tile[:, :P]
        far_left = keep.tile([P, 8], F32, name="far_left")
        zeros_tile = keep.tile([P, P + 1], F32, name="zeros", align_bytes=ALIGN)
        zeros = zeros_tile[:, :P]
        window = keep.tile([P, T], F32, name="window", align_bytes=ALIGN)
        xw = keep.tile([P, T], I32, name="xw", align_bytes=ALIGN)
        xs = keep.tile([P, T], U8, name="xs", align_bytes=ALIGN)
        first_words = head_bytes.tile([P, 2 * PASS], U8, name="first_words", align_bytes=ALIGN, offset=0)
        w13 = [keep.tile([P, 2 * 2 * H], U8, name="w13_%d" % e, align_bytes=ALIGN) for e in range(E)]
        w2w = keep.tile([P, E * PASSES, 2 * N], U8, name="w2w", align_bytes=ALIGN)
        gates = keep.tile([P, E * C], F32, name="gates", align_bytes=ALIGN)

        def weight_words(e, m, s):
            if (e, m, s) == (0, 0, 0):
                return first_words[:]
            return w13[e][:, 2 * (H * m + PASS * s) : 2 * (H * m + PASS * (s + 1))]

        def load_scales(plane, scale_rows, rows, queue):
            by_row = scale_rows.rearrange("g (q r) w -> r q g w", r=ROWS)
            for r in rows:
                dst = plane[r:P:GROUP, :].bitcast(I32).rearrange("q (g w) -> q g w", g=scale_rows.shape[0])
                queue.dma_start(out=dst, in_=by_row[r].bitcast(I32))

        def load_matrix(e, m):
            dst = w13[e][:, 2 * H * m : 2 * H * (m + 1)]
            nc.sync.dma_start(out=dst.bitcast(I32), in_=(w1_words, w3_words)[m][e, 0].bitcast(I32))

        def load_first_matrix(s, queue):
            src = w1_words[0, 0][:, 2 * PASS * s : 2 * PASS * (s + 1)]
            queue.dma_start(out=weight_words(0, 0, s).bitcast(I32), in_=src.bitcast(I32))

        late_partitions = LATE_MATRICES * ROWS * ROWS

        def load_late_rows(m):
            src = (w1_scales, w3_scales)[m][EARLY_EXPERTS:, 0].rearrange("e (q r) w -> r (e q) w", r=ROWS)
            nc.gpsimd.dma_start(out=late_rows[m:late_partitions:2, :].bitcast(I32), in_=src.bitcast(I32))

        def place_rows(e):
            late = e - EARLY_EXPERTS
            for r in range(ROWS):
                lo = ROWS * (LATE_MATRICES * r + 2 * late)
                nc.sync.dma_start(
                    out=late_planes[r:P:GROUP, 2 * H * late : 2 * H * (late + 1)].bitcast(I32),
                    in_=sorted_rows[lo : lo + 2 * ROWS, :].bitcast(I32),
                )

        nc.gpsimd.memset(xs[:].bitcast(I32), 0)
        load_first_matrix(0, nc.gpsimd)
        for m in range(2):
            load_late_rows(m)
        nc.gpsimd.memset(late_rows[late_partitions:, :].bitcast(I32), 0)
        nc.vector.memset(early_tiles[0][:].bitcast(I32), 0)
        nc.vector.memset(far_left[:, 0:1], -200.0)
        for tile in (early_tiles[1], w2s_tile):
            nc.vector.memset(tile[:].bitcast(I32), 0)
        nc.vector.memset(ident_tile[:], 0.0)
        nc.vector.memset(zeros_tile[:], 0.0)
        nc.sync.dma_start(offsets[:], offs)
        load_scales(xs, x_scales, range(ROWS // 2), nc.sync)
        load_scales(xs, x_scales, range(ROWS // 2, ROWS), nc.scalar)
        nc.sync.dma_start(out=xw[:], in_=x_words[0].rearrange("p t r -> p (t r)").bitcast(I32))
        make_identity(nc, ident[:], nomemset=True)
        nc.scalar.activation(out=window[:], in_=far_left[:, 0:1].to_broadcast([P, T]), func=SIGMOID)
        nc.scalar.copy(
            out=late_planes[:].bitcast(U32), in_=zeros[:, 0:1].bitcast(U32).to_broadcast([P, LATE_MATRICES * H // 4])
        )
        load_scales(early_planes[0], w1_scales[:EARLY_EXPERTS, 0], range(ROWS), nc.sync)
        load_first_matrix(1, nc.sync)
        load_matrix(0, 1)
        load_scales(early_planes[1], w3_scales[:EARLY_EXPERTS, 0], range(ROWS), nc.sync)
        for e in (1, 2):
            for m in range(2):
                load_matrix(e, m)
        load_scales(w2s, w2_scales.rearrange("e s f n -> (e s) f n"), range(ROWS), nc.sync)
        load_matrix(3, 0)

        slot_words = keep.tile([P, E * C], U32, name="slot_words", align_bytes=ALIGN)
        early_scales = keep.tile([P, EARLY_SLOTS], U8, name="early_scales", align_bytes=ALIGN)
        late_scales = head_bytes.tile([P, E * C - EARLY_SLOTS], U8, name="late_scales", align_bytes=ALIGN, offset=0)
        results = keep.tile([P, E * C], F32, name="results", align_bytes=ALIGN)
        sorted_words = {}
        early_sigmoids = {}
        late_sigmoids = {}
        values = {}
        hidden = {}
        quantiser_input = {}
        quantised = {}
        sums = {}
        oldest_first = list(range(BANKS))
        bank_of = {}

        def bank(name, shape, behind):
            number = oldest_first[0] if behind is None else bank_of[behind]
            oldest_first.remove(number)
            oldest_first.append(number)
            bank_of[name] = number
            return psum.tile(shape, F32, name=name, offset=number * BANK_BYTES)

        def listed(lo, hi):
            return offsets[:, lo // PER_COLUMN : hi // PER_COLUMN]

        def sort_words(e, m, s, pool=keep, offset=None):
            name = "sorted_words_%d_%d_%d" % (e, m, s)
            sorted_words[e, m, s] = pool.tile([P, VALUES, P], U16, name=name, align_bytes=ALIGN, offset=offset)
            nc.gpsimd.tensor_copy(
                out=sorted_words[e, m, s][:],
                in_=weight_words(e, m, s).bitcast(U16).rearrange("k (p t) -> k t p", t=VALUES),
            )

        def early_product(j, s, m, acc):
            e = j // PER_EXPERT
            nc.tensor.matmul_mx(
                out=acc,
                lhsT=slot_words[:, j * P : (j + 1) * P].bitcast(FP8X4),
                lhsT_scale=early_scales[:, j * P : (j + 1) * P],
                rhs=weight_words(e, m, s).bitcast(FP4X4),
                rhs_scale=early_planes[m][:, e * H + PASS * s : e * H + PASS * (s + 1)],
                start=True,
                stop=True,
            )

        def late_product(e, m, s, t, lo, hi, acc):
            at = (2 * (e - EARLY_EXPERTS) + m) * H + PASS * s + P * t
            nc.tensor.matmul_mx(
                out=acc,
                lhsT=sorted_words[e, m, s][:, t, :].bitcast(U8).bitcast(FP4X4),
                lhsT_scale=late_planes[:, at : at + P],
                rhs=slot_words[:, lo:hi].bitcast(FP8X4),
                rhs_scale=late_scales[:, lo - EARLY_SLOTS : hi - EARLY_SLOTS],
                start=True,
                stop=True,
            )

        def early_order(acc):
            return acc[:].rearrange("c (p u v) -> c u p v", u=2, v=2)

        def early_sigmoid(j, s):
            a = bank("a_%d_%d" % (j, s), [P, PASS], None)
            early_product(j, s, 0, a[:])
            early_sigmoids[j, s] = work.tile([P, 2, P, 2], F32, name="early_sigmoid", bufs=EARLY_HALVES)
            nc.scalar.activation(out=early_sigmoids[j, s][:], in_=early_order(a), func=SIGMOID)

        def late_sigmoid(e, s, u):
            a = bank("a_%d_%d_%d" % (e, s, u), [P, 2, C], None)
            for v in range(2):
                late_product(e, 0, s, 2 * u + v, e * C, (e + 1) * C, a[:, v, :])
            if u == 0:
                late_sigmoids[e, s] = work.tile([P, 2, C // 2, 2, 2], F32, name="late_sigmoid", bufs=LATE_HALVES)
            nc.scalar.activation(
                out=late_sigmoids[e, s][:, u], in_=a[:].rearrange("p v (d n) -> p d v n", n=2), func=SIGMOID
            )

        def value_product(j, s):
            e = j // PER_EXPERT
            values[j, s] = bank("b_%d_%d" % (j, s), [P, PASS], None)
            if e < EARLY_EXPERTS:
                early_product(j, s, 1, values[j, s][:])
            else:
                for t in range(VALUES):
                    late_product(e, 1, s, t, j * P, (j + 1) * P, values[j, s][:, P * t : P * (t + 1)])

        def slots_of(j, s):
            h, tiles = quantiser_input[j]
            place = tiles.index(j)
            return h[:].rearrange("p (s c t) -> p s c t", s=PASSES, t=VALUES)[:, s, place * P : (place + 1) * P, :]

        def multiply(j, s):
            e = j // PER_EXPERT
            if e < EARLY_EXPERTS:
                hidden[j, s] = work.tile([P, 2, P, 2], BF16, name="early_h", bufs=EARLY_HALVES)
                dst, b, sig = hidden[j, s][:], early_order(values[j, s]), early_sigmoids[j, s][:]
            else:
                first_pair = j % PER_EXPERT * P // 2
                dst = slots_of(j, s).rearrange("p (d n) (u v) -> p d u v n", n=2, u=2)
                b = values[j, s][:].rearrange("p (u v d n) -> p d u v n", u=2, v=2, n=2)
                sig = late_sigmoids[e, s][:, :, first_pair : first_pair + P // 2].rearrange("p u d v n -> p d u v n")
            nc.vector.tensor_tensor(out=dst, in0=b, in1=sig, op=MULT)

        def turn(j, copy, behind):
            xt = bank("xt_%d" % j, [P, PASSES, 2, P], behind)
            for s in range(PASSES):
                pairs = hidden[j, s][:].rearrange("c u p v -> c (u p v)").bitcast(F32)
                for u in range(2):
                    nc.tensor.transpose(xt[:, s, u, :], pairs[:, u * P : (u + 1) * P], ident[:])
            h, tiles = quantiser_input[j]
            place = tiles.index(j)
            words = h[:].bitcast(F32).rearrange("p (s c u) -> p s c u", s=PASSES, u=2)
            copy(out=words[:, :, place * P : (place + 1) * P, :], in_=xt[:].rearrange("p s u c -> p s c u"))

        def quantise(j, passes=range(PASSES)):
            h, tiles = quantiser_input[j]
            slots = len(tiles) * P
            if passes[0] == 0:
                codes = work.tile([P, PASSES * slots], U32, name="codes", align_bytes=ALIGN)
                scales = work.tile([P, PASSES * slots], U8, name="scales", align_bytes=ALIGN)
                quantised[j] = (codes, scales)
            codes, scales = quantised[j]
            lo, hi = passes[0] * slots, (passes[-1] + 1) * slots
            nc.vector.quantize_mx(
                out=codes[:, lo:hi].bitcast(FP8X4), scales=scales[:, lo:hi], in_=h[:, VALUES * lo : VALUES * hi]
            )

        def second_layer(j, behind=None):
            slots = len(quantiser_input[j][1]) * P
            sums[j] = bank("y_%d" % j, [P, slots], behind)
            codes, scales = quantised[j]
            for s in range(PASSES):
                g = j // PER_EXPERT * PASSES + s
                nc.tensor.matmul_mx(
                    out=sums[j][:],
                    lhsT=w2w[:, g, :].bitcast(FP4X4),
                    lhsT_scale=w2s[:, g * N : (g + 1) * N],
                    rhs=codes[:, s * slots : (s + 1) * slots].bitcast(FP8X4),
                    rhs_scale=scales[:, s * slots : (s + 1) * slots],
                    start=(s == 0),
                    stop=(s == PASSES - 1),
                )

        def weigh(j):
            lo, hi = j * P, (j + len(quantiser_input[j][1])) * P
            nc.vector.tensor_tensor(out=results[:, lo:hi], in0=sums[j][:], in1=gates[:, lo:hi], op=MULT)

        def scatter_expert(e):
            lo, hi = e * C, (e + 1) * C
            nc.scalar.activation(out=window[:].indirect(listed(lo, hi)), in_=results[:, lo:hi], func=COPY)

        def scatter_tile(j):
            lo, hi = j * P, (j + 1) * P
            nc.vector.tensor_tensor(out=window[:].indirect(listed(lo, hi)), in0=results[:, lo:hi], in1=zeros[:], op=ADD)

        nc.vector.tensor_copy(out=early_scales[:], in_=xs[:].indirect(listed(0, EARLY_SLOTS)))
        for lo, hi in zip(WORD_CUTS, WORD_CUTS[1:]):
            nc.vector.tensor_copy(out=slot_words[:, lo:hi], in_=xw[:].bitcast(U32).indirect(listed(lo, hi)))
        nc.vector.tensor_copy(out=late_scales[:], in_=xs[:].indirect(listed(EARLY_SLOTS, E * C)))

        sorted_rows = keep.tile([P, H], U8, name="sorted_rows", align_bytes=ALIGN)
        nc.gpsimd.tensor_copy(
            out=sorted_rows[:].rearrange("row (s t p) -> row s t p", s=PASSES, t=VALUES),
            in_=late_rows[:].rearrange("row (s p t) -> row s t p", s=PASSES, t=VALUES),
        )
        for e in range(EARLY_EXPERTS, E):
            place_rows(e)
        nc.sync.dma_start(out=w2w[:].bitcast(I32), in_=w2_words.rearrange("e s p b -> p (e s) b").bitcast(I32))
        nc.sync.dma_start(out=gates[:, :C], in_=gate[:, :C])
        load_matrix(3, 1)
        nc.sync.dma_start(out=gates[:, C:], in_=gate[:, C:])

        for tiles in GROUPS:
            if tiles == GROUPS[0]:
                h = first_h_bytes.tile([P, len(tiles) * H], BF16, name="first_h", align_bytes=ALIGN, offset=0)
            else:
                h = work.tile([P, len(tiles) * H], BF16, name="h", align_bytes=ALIGN)
            for j in tiles:
                quantiser_input[j] = (h, tiles)

        for m in range(2):
            for s in range(PASSES):
                sort_words(2, m, s)
        sort_words(3, 0, 0)

        for s in range(PASSES):
            for j in GROUPS[0]:
                early_sigmoid(j, s)
        for s in range(PASSES):
            value_product(0, s)
            multiply(0, s)
        for s in range(PASSES):
            early_sigmoid(2, s)
            value_product(1, s)
            multiply(1, s)
        early_sigmoid(3, 0)
        value_product(2, 0)
        multiply(2, 0)
        early_sigmoid(3, 1)
        value_product(2, 1)
        turn(0, nc.scalar.copy, behind="a_2_1")
        turn(1, nc.scalar.copy, behind="a_3_0")
        multiply(2, 1)
        for s in range(PASSES):
            value_product(3, s)
            late_sigmoid(2, 0, s)
            multiply(3, s)
        late_sigmoid(2, 1, 0)
        quantise(0)
        sort_words(3, 0, 1, pool=first_h_bytes, offset=0)
        for s in range(PASSES):
            sort_words(3, 1, s)
        value_product(4, 0)
        late_sigmoid(2, 1, 1)
        multiply(4, 0)
        value_product(5, 0)
        late_sigmoid(3, 0, 0)
        multiply(5, 0)
        value_product(4, 1)
        late_sigmoid(3, 0, 1)
        multiply(4, 1)
        turn(2, nc.vector.tensor_copy, behind="b_5_0")
        turn(3, nc.scalar.copy, behind="a_2_1_1")
        second_layer(0, behind="a_3_0_0")
        weigh(0)
        scatter_expert(0)
        value_product(5, 1)
        for u in range(2):
            late_sigmoid(3, 1, u)
        multiply(5, 1)
        value_product(6, 0)
        quantise(2)
        value_product(7, 0)
        quantise(4)
        second_layer(2)
        multiply(6, 0)
        second_layer(4)
        weigh(2)
        value_product(6, 1)
        weigh(4)
        scatter_expert(1)
        multiply(7, 0)
        value_product(7, 1)
        scatter_expert(2)
        multiply(6, 1)
        quantise(7, range(1))
        quantise(6)
        multiply(7, 1)
        second_layer(6)
        weigh(6)
        quantise(7, range(1, PASSES))
        second_layer(7)
        scatter_tile(6)
        weigh(7)
        scatter_tile(7)
        nc.sync.dma_start(out=out, in_=window[:])
